import numpy as np
import ml_dtypes


def mxq(x, axis, fmt="e4m3"):
    dtype, down = {"e4m3": (ml_dtypes.float8_e4m3fn, 7), "e5m2": (ml_dtypes.float8_e5m2, 14)}[fmt]
    v = np.moveaxis(np.asarray(x, np.float32).astype(ml_dtypes.bfloat16).astype(np.float64), axis, -1)
    blocks = v.reshape(v.shape[:-1] + (-1, 32))
    amax = np.abs(blocks).max(-1, keepdims=True)
    byte = np.maximum(np.where(amax > 0, np.frexp(amax)[1] - 1 + 127, 0) - down, 1)
    scale = np.exp2(byte - 127.0)
    codes = (blocks / scale).astype(np.float32).astype(dtype).astype(np.float64)
    return np.moveaxis((codes * scale).reshape(v.shape), -1, axis)


WIDE = False


def mx_kscale(k):
    if not WIDE:
        return np.ones(k)
    levels = np.array([24, -24, 12, -12, 0])
    if k % 512:
        return np.exp2(np.random.permutation(np.resize(levels, k // 32))).repeat(32)
    a = np.empty((k // 512, 16))
    for p in range(k // 512):
        a[p, :8] = np.random.permutation(np.resize(levels, 8))
        for g in range(8):
            far = levels[np.abs(levels - a[p, g]) >= 10]
            a[p, g + 8] = far[np.random.randint(len(far))]
    return np.exp2(a.ravel()).repeat(32)


def f64(x):
    return np.asarray(x).astype(np.float64)


def striped(idx):
    return np.tile(idx.reshape(-1, 16).T, (8, 1)).astype(np.uint16)


def unstriped(offs):
    return offs[:16].T.reshape(-1).astype(np.int64)


E2M1 = np.array([0.0, 0.5, 1.0, 1.5, 2.0, 3.0, 4.0, 6.0, -0.0, -0.5, -1.0, -1.5, -2.0, -3.0, -4.0, -6.0])


def pack_weight(w, fmt):
    k, n = w.shape
    w = f64(np.asarray(w, np.float32).astype(ml_dtypes.bfloat16)).reshape(k // 32, 32, n)
    amax = np.abs(w).max(1)
    if fmt == "e4m3":
        byte = np.frexp(amax)[1] - 1 + 127 - 7
    else:
        mant, ex = np.frexp(amax / 6.0)
        byte = np.where(mant > 0.5, ex, ex - 1) + 127
    byte = np.clip(np.where(amax > 0, byte, 1), 1, 254)
    scaled = (w * np.exp2(127.0 - byte)[:, None, :]).reshape(k, n).astype(np.float32)
    by_word = np.ascontiguousarray(scaled.reshape(k // 512, 128, 4, n).transpose(0, 1, 3, 2))
    if fmt == "e4m3":
        words = by_word.astype(ml_dtypes.float8_e4m3fn).view(np.uint8)
    else:
        c = by_word.astype(ml_dtypes.float4_e2m1fn).view(np.uint8) & 0xF
        words = (c[..., 0::2] | (c[..., 1::2] << 4)).reshape(k // 512, 128, 2 * n)
    return np.ascontiguousarray(words), np.ascontiguousarray(byte.astype(np.uint8).reshape(k // 512, 16, n))


def unpack_weight(words, scales, fmt):
    g, _, n = scales.shape
    words = np.ascontiguousarray(words).reshape(g, 128, n, -1)
    if fmt == "e4m3":
        vals = words.view(ml_dtypes.float8_e4m3fn).astype(np.float64)
    else:
        nib = np.empty((g, 128, n, 4), np.uint8)
        nib[..., 0::2] = words & 0xF
        nib[..., 1::2] = words >> 4
        vals = E2M1[nib]
    vals = vals * np.repeat(np.exp2(scales.astype(np.float64) - 127.0), 8, axis=1)[..., None]
    return vals.transpose(0, 1, 3, 2).reshape(g * 512, n)


K, R, M, N, T, J = 1024, 1024, 256, 256, 4096, 1024


def setup_inputs():
    n = np.random.standard_normal
    s = mx_kscale(K)[:, None]
    s2 = mx_kscale(K)[:, None]
    u = mx_kscale(R)[:, None]
    wv = n((K, N)) / np.sqrt(K) / s2
    p_tab = pack_weight(n((K, T)) * s2, "e4m3")
    p_wq = pack_weight(n((K, R)) / np.sqrt(K) / s / u.T, "e4m3")
    p_wk = pack_weight(n((K, R)) / np.sqrt(K) / s2 * u.T, "e2m1")
    p_wv4 = pack_weight(wv[512:], "e2m1")
    return {
        "tab_words": p_tab[0],
        "tab_scales": p_tab[1],
        "x": (n((K, M)) * s).astype(np.float32),
        "wq_words": p_wq[0],
        "wq_scales": p_wq[1],
        "wk_words": p_wk[0],
        "wk_scales": p_wk[1],
        "wv8": (wv[:512]).astype(np.float32),
        "wv4_words": p_wv4[0],
        "wv4_scales": p_wv4[1],
        "offs": striped(np.random.permutation(T)[:J]),
    }


def reference(tab_words, tab_scales, x, wq_words, wq_scales, wk_words, wk_scales, wv8, wv4_words, wv4_scales, offs):
    idx = unstriped(offs)
    tab_ = unpack_weight(tab_words, tab_scales, "e4m3")[:, idx]
    x_ = mxq(f64(x), 0, "e4m3")
    wq_ = unpack_weight(wq_words, wq_scales, "e4m3")
    wk_ = unpack_weight(wk_words, wk_scales, "e2m1")
    qr = wq_.T @ x_
    kr = wk_.T @ tab_
    qa = np.maximum(qr, 0.0)
    ka = np.maximum(kr, 0.0)
    qa_ = mxq(qa, 0, "e4m3")
    ka_ = mxq(ka, 0, "e4m3")
    sc = qa_.T @ ka_
    wv8_ = mxq(f64(wv8), 0, "e4m3")
    wv4_ = unpack_weight(wv4_words, wv4_scales, "e2m1")
    vv = wv8_.T @ tab_[:512] + wv4_.T @ tab_[512:]
    return sc * 0.03125, vv

@@ -1,0 +1,314 @@
+from contextlib import ExitStack
+
+import concourse.mybir as mybir
+
+K, R, M, N, T, J = 1024, 1024, 256, 256, 4096, 1024
+FLOPS = 2 * (K * R * M + K * R * J + R * M * J + K * N * J)
+BYTES = (K * J + K * J // 32) + 4 * K * M + (K * R + K * R // 32) + (K * R // 2 + K * R // 32) + 4 * 512 * N + (512 * N // 2 + 512 * N // 32) + 2 * J + 4 * (M + N) * J
+
+F32 = mybir.dt.float32
+BF16 = mybir.dt.bfloat16
+I32 = mybir.dt.int32
+U32 = mybir.dt.uint32
+U16 = mybir.dt.uint16
+U8 = mybir.dt.uint8
+FP8X4 = mybir.dt.float8_e4m3fn_x4
+FP4X4 = mybir.dt.float4_e2m1fn_x4
+RELU = mybir.ActivationFunctionType.Relu
+COPY = mybir.ActivationFunctionType.Copy
+MULT = mybir.AluOpType.mult
+
+P = 128
+PASSES = 2
+HALF = 512
+CHUNK = 128
+SCORE_SCALE = 0.03125
+
+
+def tile_list_kvt_qf_act_kernel(
+    tc, tab_words, tab_scales, x, wq_words, wq_scales, wk_words, wk_scales, wv8, wv4_words, wv4_scales, offs, out_0, out_1
+):
+    nc = tc.nc
+    with ExitStack() as ctx:
+        keep = ctx.enter_context(tc.tile_pool(name="keep", bufs=1))
+        stage = ctx.enter_context(tc.tile_pool(name="stage", bufs=4))
+        psum = ctx.enter_context(tc.psum_pool(name="psum", bufs=8))
+
+        def held(name, shape, dtype, slot=None):
+            return keep.tile(shape, dtype, name=name, tag=slot or name, align_bytes=64)
+
+        offsets = keep.tile([P, J // 16], U16, name="offsets")
+        tab_scale_rows = held("tab_scale_rows", [P, T // 4], I32)
+        tab_win = [held("tab_win%d" % a, [P, T], I32) for a in range(PASSES)]
+        wk_raw = held("wk_raw", [P, PASSES * R // 2], I32)
+        wk_scale_raw = held("wk_scale_raw", [P, PASSES * R // 4], I32)
+        wv4_codes = held("wv4_codes", [P, N // 2], I32)
+        wv4_plane = held("wv4_plane", [P, N // 4], I32)
+        v_plane = held("v_plane", [P, PASSES, J // 4], I32)
+
+        nc.sync.dma_start(offsets[:], offs)
+        nc.sync.dma_start(out=tab_scale_rows[0:32, :], in_=tab_scales.rearrange("a q t -> (a q) t").bitcast(I32))
+        nc.vector.memset(wk_scale_raw[:], 0)
+        nc.vector.memset(tab_scale_rows[32:64, :], 0)
+        nc.vector.memset(tab_scale_rows[64:128, :], 0)
+        nc.vector.memset(v_plane[:], 0)
+        nc.vector.memset(wv4_plane[:], 0)
+        for quad in range(4):
+            nc.gpsimd.dma_start(
+                out=wk_scale_raw[32 * quad : 32 * quad + 4, :].rearrange("p (a w) -> p a w", a=PASSES),
+                in_=wk_scales[:, 4 * quad : 4 * quad + 4, :].rearrange("a r n -> r a n").bitcast(I32),
+            )
+        nc.sync.dma_start(out=tab_win[0][:], in_=tab_words[0].rearrange("p t i -> p (t i)").bitcast(I32))
+        nc.sync.dma_start(
+            out=wk_raw[:].rearrange("p (a w) -> p a w", a=PASSES), in_=wk_words.rearrange("a p n -> p a n").bitcast(I32)
+        )
+        nc.sync.dma_start(out=wv4_codes[:], in_=wv4_words[0].bitcast(I32))
+        nc.sync.dma_start(out=tab_win[1][:], in_=tab_words[1].rearrange("p t i -> p (t i)").bitcast(I32))
+
+        v_scale_rows = held("v_scale_rows", [P, J], U8)
+        nc.vector.tensor_copy(out=v_scale_rows[:], in_=tab_scale_rows[:].bitcast(U8).indirect(offsets[:]))
+        for a in range(PASSES):
+            for quad in range(4):
+                row = 16 * a + 4 * quad
+                queue = nc.scalar if a == 0 else nc.gpsimd
+                queue.dma_start(
+                    out=v_plane[32 * quad : 32 * quad + 4, a, :], in_=v_scale_rows[row : row + 4, :].bitcast(I32)
+                )
+        for quad in range(4):
+            nc.gpsimd.dma_start(
+                out=wv4_plane[32 * quad : 32 * quad + 4, :], in_=wv4_scales[0, 4 * quad : 4 * quad + 4, :].bitcast(I32)
+            )
+
+        def reorder(dst, src, run):
+            nc.vector.tensor_copy(
+                out=dst.rearrange("p (g t q u) -> p g t q u", t=4, q=16, u=run),
+                in_=src.rearrange("p (g q t u) -> p g t q u", t=4, q=16, u=run),
+            )
+
+        v_codes = [[held("v_codes%d%d" % (a, h), [P, HALF], U32) for h in range(2)] for a in range(PASSES)]
+
+        def gather_words(a, h):
+            nc.vector.tensor_copy(
+                out=v_codes[a][h][:], in_=tab_win[a][:].bitcast(U32).indirect(offsets[:, 32 * h : 32 * h + 32])
+            )
+
+        wk_plane = held("wk_plane", [P, PASSES * R // 4], I32)
+        wk_codes = held("wk_codes", [P, PASSES * R // 2], I32)
+        reorder(wk_plane[:], wk_scale_raw[:], 2)
+        wq_scale_raw = held("wq_scale_raw", [P, R // 4], I32, slot="wk_scale_raw")
+        nc.vector.memset(wq_scale_raw[:], 0)
+        for quad in range(4):
+            nc.scalar.dma_start(
+                out=wq_scale_raw[32 * quad + 4 : 32 * quad + 12, :],
+                in_=wq_scales[:, 4 * quad : 4 * quad + 4, :].bitcast(I32),
+            )
+        gather_words(0, 0)
+        reorder(wk_codes[:], wk_raw[:], 4)
+        gather_words(0, 1)
+        wv8_raw = held("wv8_raw", [P, 4, N], F32, slot="tab_win0")
+        nc.sync.dma_start(out=wv8_raw[:], in_=wv8.rearrange("(p i) n -> p i n", i=4))
+        x_raw = held("x_raw", [P, PASSES, 4, M], F32, slot="tab_scale_rows")
+        nc.sync.dma_start(out=x_raw[:], in_=x.rearrange("(a p i) m -> p a i m", a=PASSES, i=4))
+        wq_raw = held("wq_raw", [P, PASSES * R], I32, slot="wk_raw")
+        nc.sync.dma_start(
+            out=wq_raw[:].rearrange("p (a w) -> p a w", a=PASSES),
+            in_=wq_words.rearrange("a p r i -> p a (r i)").bitcast(I32),
+        )
+        gather_words(1, 0)
+        gather_words(1, 1)
+
+        v_plane_bytes = v_plane[:].rearrange("p a w -> p (a w)").bitcast(U8)
+        wk_plane_bytes = wk_plane[:].bitcast(U8)
+        wk_code_bytes = wk_codes[:].bitcast(U8)
+
+        ka_bf = held("ka_bf", [P, 2, J * 4], BF16)
+        ka_codes = held("ka_codes", [P, 2, J], U32)
+        ka_plane = held("ka_plane", [P, 2, J], U8)
+
+        def keys(jc, b):
+            h, j0 = divmod(jc * CHUNK, HALF)
+            bank = psum.tile([P, 4, CHUNK], F32, name="bank", tag="bank")
+            for t in range(4):
+                for a in range(PASSES):
+                    col = a * R + b * 512 + t * 128
+                    nc.tensor.matmul_mx(
+                        out=bank[:, t, :],
+                        lhsT=wk_code_bytes[:, 2 * col : 2 * col + 256].bitcast(FP4X4),
+                        lhsT_scale=wk_plane_bytes[:, col : col + 128],
+                        rhs=v_codes[a][h][:, j0 : j0 + CHUNK].bitcast(FP8X4),
+                        rhs_scale=v_plane_bytes[:, a * J + jc * CHUNK : a * J + (jc + 1) * CHUNK],
+                        start=(a == 0),
+                        stop=(a == PASSES - 1),
+                    )
+            nc.scalar.activation(
+                out=ka_bf[:, b, 4 * jc * CHUNK : 4 * (jc + 1) * CHUNK].rearrange("p (n t) -> p n t", t=4),
+                in_=bank[:].rearrange("p t n -> p n t"),
+                func=RELU,
+            )
+
+        wide_banks = {}
+        ka_planar = held("ka_planar", [P, 2, 4, HALF], BF16)
+
+        def wide_pass(b, a):
+            for t in range(4):
+                if a == 0:
+                    wide_banks[b, t] = psum.tile([P, HALF], F32, name="bank", tag="bank")
+                col = a * R + b * 512 + t * 128
+                nc.tensor.matmul_mx(
+                    out=wide_banks[b, t][:],
+                    lhsT=wk_code_bytes[:, 2 * col : 2 * col + 256].bitcast(FP4X4),
+                    lhsT_scale=wk_plane_bytes[:, col : col + 128],
+                    rhs=v_codes[a][0][:].bitcast(FP8X4),
+                    rhs_scale=v_plane_bytes[:, a * J : a * J + HALF],
+                    start=(a == 0),
+                    stop=(a == PASSES - 1),
+                )
+                if a == PASSES - 1:
+                    nc.scalar.activation(out=ka_planar[:, b, t, :], in_=wide_banks[b, t][:], func=RELU)
+
+        def wide_finish(b):
+            nc.vector.tensor_copy(
+                out=ka_bf[:, b, 0 : 4 * HALF].rearrange("p (c u t) -> p c t u", u=4, t=4),
+                in_=ka_planar[:, b].rearrange("p t (c u) -> p c t u", u=4),
+            )
+
+        def quantise_keys(j0, width, b):
+            nc.vector.quantize_mx(
+                out=ka_codes[:, b, j0 : j0 + width].bitcast(FP8X4),
+                scales=ka_plane[:, b, j0 : j0 + width],
+                in_=ka_bf[:, b, 4 * j0 : 4 * (j0 + width)],
+            )
+
+        def key_pair(jc):
+            for c in (jc, jc + 1):
+                for b in range(2):
+                    keys(c, b)
+            for b in range(2):
+                quantise_keys(jc * CHUNK, 2 * CHUNK, b)
+
+        x_bf = held("x_bf", [P, PASSES, M, 4], BF16)
+        x_codes = held("x_codes", [P, PASSES * M], U32)
+        x_plane = held("x_plane", [P, PASSES * M], U8)
+        wq_codes = held("wq_codes", [P, PASSES * R], I32)
+        wq_plane = held("wq_plane", [P, R // 4], I32)
+        wv8_bf = held("wv8_bf", [P, N, 4], BF16)
+        wv8_codes = held("wv8_codes", [P, N], U32)
+        wv8_plane = held("wv8_plane", [P, N], U8)
+        qa_bf = held("qa_bf", [P, 2, M * 4], BF16)
+        qa_codes = held("qa_codes", [P, 2, M], U32)
+        qa_plane = held("qa_plane", [P, 2, M], U8)
+
+        def prepare_queries():
+            nc.vector.tensor_copy(
+                out=x_bf[:].rearrange("p a (c u) i -> p a c i u", u=4),
+                in_=x_raw[:].rearrange("p a i (c u) -> p a c i u", u=4),
+            )
+            reorder(wq_plane[:], wq_scale_raw[:], 2)
+            nc.vector.quantize_mx(
+                out=x_codes[:].bitcast(FP8X4), scales=x_plane[:], in_=x_bf[:].rearrange("p a m i -> p (a m i)")
+            )
+            reorder(wq_codes[:], wq_raw[:], 8)
+
+        def prepare_values():
+            nc.vector.tensor_copy(
+                out=wv8_bf[:].rearrange("p (c u) i -> p c i u", u=4),
+                in_=wv8_raw[:].rearrange("p i (c u) -> p c i u", u=4),
+            )
+            nc.vector.quantize_mx(
+                out=wv8_codes[:].bitcast(FP8X4), scales=wv8_plane[:], in_=wv8_bf[:].rearrange("p n i -> p (n i)")
+            )
+
+        wq_plane_bytes = wq_plane[:].bitcast(U8)
+
+        def queries(b):
+            for mc in range(M // CHUNK):
+                bank = psum.tile([P, 4, CHUNK], F32, name="bank", tag="bank")
+                for t in range(4):
+                    for a in range(PASSES):
+                        col = b * 512 + t * 128
+                        m0 = a * M + mc * CHUNK
+                        nc.tensor.matmul_mx(
+                            out=bank[:, t, :],
+                            lhsT=wq_codes[:, a * R + col : a * R + col + 128].bitcast(FP8X4),
+                            lhsT_scale=wq_plane_bytes[4 + 4 * a : P, col : col + 128],
+                            rhs=x_codes[:, m0 : m0 + CHUNK].bitcast(FP8X4),
+                            rhs_scale=x_plane[:, m0 : m0 + CHUNK],
+                            start=(a == 0),
+                            stop=(a == PASSES - 1),
+                        )
+                nc.scalar.activation(
+                    out=qa_bf[:, b, 4 * mc * CHUNK : 4 * (mc + 1) * CHUNK].rearrange("p (n t) -> p n t", t=4),
+                    in_=bank[:].rearrange("p t n -> p n t"),
+                    func=RELU,
+                )
+            nc.vector.quantize_mx(out=qa_codes[:, b, :].bitcast(FP8X4), scales=qa_plane[:, b, :], in_=qa_bf[:, b, :])
+
+        wv4_code_bytes = wv4_codes[:].bitcast(U8)
+        wv4_plane_bytes = wv4_plane[:].bitcast(U8)
+
+        def values(h):
+            for nt in range(N // P):
+                bank = psum.tile([P, HALF], F32, name="bank", tag="bank")
+                cols = slice(nt * P, (nt + 1) * P)
+                nc.tensor.matmul_mx(
+                    out=bank[:],
+                    lhsT=wv8_codes[:, cols].bitcast(FP8X4),
+                    lhsT_scale=wv8_plane[:, cols],
+                    rhs=v_codes[0][h][:].bitcast(FP8X4),
+                    rhs_scale=v_plane_bytes[:, h * HALF : (h + 1) * HALF],
+                    start=True,
+                    stop=False,
+                )
+                nc.tensor.matmul_mx(
+                    out=bank[:],
+                    lhsT=wv4_code_bytes[:, 2 * nt * P : 2 * (nt + 1) * P].bitcast(FP4X4),
+                    lhsT_scale=wv4_plane_bytes[:, cols],
+                    rhs=v_codes[1][h][:].bitcast(FP8X4),
+                    rhs_scale=v_plane_bytes[:, J + h * HALF : J + (h + 1) * HALF],
+                    start=False,
+                    stop=True,
+                )
+                result = stage.tile([P, HALF], F32, name="result", tag="result")
+                nc.vector.tensor_copy(out=result[:], in_=bank[:])
+                nc.sync.dma_start(out=out_1[cols, h * HALF : (h + 1) * HALF], in_=result[:])
+
+        def scores(j0, width, split):
+            for mt in range(M // P):
+                bank = psum.tile([P, width], F32, name="bank", tag="bank")
+                cols = slice(mt * P, (mt + 1) * P)
+                for b in range(2):
+                    nc.tensor.matmul_mx(
+                        out=bank[:],
+                        lhsT=qa_codes[:, b, cols].bitcast(FP8X4),
+                        lhsT_scale=qa_plane[:, b, cols],
+                        rhs=ka_codes[:, b, j0 : j0 + width].bitcast(FP8X4),
+                        rhs_scale=ka_plane[:, b, j0 : j0 + width],
+                        start=(b == 0),
+                        stop=(b == 1),
+                    )
+                result = stage.tile([P, width], F32, name="result", tag="result")
+                if split and mt == 0:
+                    nc.scalar.activation(out=result[:], in_=bank[:], func=COPY, scale=SCORE_SCALE)
+                else:
+                    nc.vector.tensor_scalar(out=result[:], in0=bank[:], scalar1=SCORE_SCALE, scalar2=None, op0=MULT)
+                nc.sync.dma_start(out=out_0[cols, j0 : j0 + width], in_=result[:])
+
+        wide_pass(0, 0)
+        wide_pass(1, 0)
+        wide_pass(0, 1)
+        wide_pass(1, 1)
+        prepare_values()
+        wide_finish(0)
+        key_pair(4)
+        wide_finish(1)
+        quantise_keys(0, HALF, 0)
+        quantise_keys(0, HALF, 1)
+        values(0)
+        prepare_queries()
+        queries(0)
+        queries(1)
+        values(1)
+        key_pair(6)
+        scores(0, HALF, False)
+        scores(HALF, 256, True)
+        scores(HALF + 256, 256, True)

@@ -23,6 +23,7 @@ PASSES = 2
 HALF = 512
 CHUNK = 128
 SCORE_SCALE = 0.03125
+QUADS = (0, 2, 1, 3)
 
 
 def tile_list_kvt_qf_act_kernel(
@@ -31,7 +32,7 @@ def tile_list_kvt_qf_act_kernel(
     nc = tc.nc
     with ExitStack() as ctx:
         keep = ctx.enter_context(tc.tile_pool(name="keep", bufs=1))
-        stage = ctx.enter_context(tc.tile_pool(name="stage", bufs=4))
+        stage = ctx.enter_context(tc.tile_pool(name="stage", bufs=10))
         psum = ctx.enter_context(tc.psum_pool(name="psum", bufs=8))
 
         def held(name, shape, dtype, slot=None):
@@ -39,45 +40,42 @@ def tile_list_kvt_qf_act_kernel(
 
         offsets = keep.tile([P, J // 16], U16, name="offsets")
         tab_scale_rows = held("tab_scale_rows", [P, T // 4], I32)
-        tab_win = [held("tab_win%d" % a, [P, T], I32) for a in range(PASSES)]
         wk_raw = held("wk_raw", [P, PASSES * R // 2], I32)
         wk_scale_raw = held("wk_scale_raw", [P, PASSES * R // 4], I32)
-        wv4_codes = held("wv4_codes", [P, N // 2], I32)
-        wv4_plane = held("wv4_plane", [P, N // 4], I32)
         v_plane = held("v_plane", [P, PASSES, J // 4], I32)
+        v_scale_rows = held("v_scale_rows", [P, J], U8)
+        tab_win = [held("tab_win0", [P, T], I32)]
 
-        nc.sync.dma_start(offsets[:], offs)
-        nc.sync.dma_start(out=tab_scale_rows[0:32, :], in_=tab_scales.rearrange("a q t -> (a q) t").bitcast(I32))
+        def load_table(a):
+            nc.sync.dma_start(out=tab_win[a][:], in_=tab_words[a].rearrange("p t i -> p (t i)").bitcast(I32))
+
+        def move_table_scales(a):
+            for quad in QUADS:
+                row = 16 * a + 4 * quad
+                nc.sync.dma_start(
+                    out=v_plane[32 * quad : 32 * quad + 4, a, :], in_=v_scale_rows[row : row + 4, :].bitcast(I32)
+                )
+
         nc.vector.memset(wk_scale_raw[:], 0)
         nc.vector.memset(tab_scale_rows[32:64, :], 0)
         nc.vector.memset(tab_scale_rows[64:128, :], 0)
         nc.vector.memset(v_plane[:], 0)
-        nc.vector.memset(wv4_plane[:], 0)
-        for quad in range(4):
-            nc.gpsimd.dma_start(
-                out=wk_scale_raw[32 * quad : 32 * quad + 4, :].rearrange("p (a w) -> p a w", a=PASSES),
-                in_=wk_scales[:, 4 * quad : 4 * quad + 4, :].rearrange("a r n -> r a n").bitcast(I32),
-            )
-        nc.sync.dma_start(out=tab_win[0][:], in_=tab_words[0].rearrange("p t i -> p (t i)").bitcast(I32))
+        nc.sync.dma_start(offsets[:], offs)
+        nc.sync.dma_start(out=tab_scale_rows[0:32, :], in_=tab_scales.rearrange("a q t -> (a q) t").bitcast(I32))
         nc.sync.dma_start(
             out=wk_raw[:].rearrange("p (a w) -> p a w", a=PASSES), in_=wk_words.rearrange("a p n -> p a n").bitcast(I32)
         )
-        nc.sync.dma_start(out=wv4_codes[:], in_=wv4_words[0].bitcast(I32))
-        nc.sync.dma_start(out=tab_win[1][:], in_=tab_words[1].rearrange("p t i -> p (t i)").bitcast(I32))
-
-        v_scale_rows = held("v_scale_rows", [P, J], U8)
-        nc.vector.tensor_copy(out=v_scale_rows[:], in_=tab_scale_rows[:].bitcast(U8).indirect(offsets[:]))
-        for a in range(PASSES):
-            for quad in range(4):
-                row = 16 * a + 4 * quad
-                queue = nc.scalar if a == 0 else nc.gpsimd
-                queue.dma_start(
-                    out=v_plane[32 * quad : 32 * quad + 4, a, :], in_=v_scale_rows[row : row + 4, :].bitcast(I32)
-                )
-        for quad in range(4):
-            nc.gpsimd.dma_start(
-                out=wv4_plane[32 * quad : 32 * quad + 4, :], in_=wv4_scales[0, 4 * quad : 4 * quad + 4, :].bitcast(I32)
+        for quad in QUADS:
+            nc.sync.dma_start(
+                out=wk_scale_raw[32 * quad : 32 * quad + 4, :].rearrange("p (a w) -> p a w", a=PASSES),
+                in_=wk_scales[:, 4 * quad : 4 * quad + 4, :].rearrange("a r n -> r a n").bitcast(I32),
             )
+        load_table(0)
+        nc.vector.tensor_copy(out=v_scale_rows[:], in_=tab_scale_rows[:].bitcast(U8).indirect(offsets[:]))
+        move_table_scales(0)
+        tab_win.append(held("tab_win1", [P, T], I32))
+        load_table(1)
+        move_table_scales(1)
 
         def reorder(dst, src, run):
             nc.vector.tensor_copy(
@@ -95,25 +93,52 @@ def tile_list_kvt_qf_act_kernel(
         wk_plane = held("wk_plane", [P, PASSES * R // 4], I32)
         wk_codes = held("wk_codes", [P, PASSES * R // 2], I32)
         reorder(wk_plane[:], wk_scale_raw[:], 2)
-        wq_scale_raw = held("wq_scale_raw", [P, R // 4], I32, slot="wk_scale_raw")
-        nc.vector.memset(wq_scale_raw[:], 0)
-        for quad in range(4):
-            nc.scalar.dma_start(
-                out=wq_scale_raw[32 * quad + 4 : 32 * quad + 12, :],
-                in_=wq_scales[:, 4 * quad : 4 * quad + 4, :].bitcast(I32),
-            )
-        gather_words(0, 0)
         reorder(wk_codes[:], wk_raw[:], 4)
+        gather_words(0, 0)
         gather_words(0, 1)
-        wv8_raw = held("wv8_raw", [P, 4, N], F32, slot="tab_win0")
-        nc.sync.dma_start(out=wv8_raw[:], in_=wv8.rearrange("(p i) n -> p i n", i=4))
-        x_raw = held("x_raw", [P, PASSES, 4, M], F32, slot="tab_scale_rows")
-        nc.sync.dma_start(out=x_raw[:], in_=x.rearrange("(a p i) m -> p a i m", a=PASSES, i=4))
-        wq_raw = held("wq_raw", [P, PASSES * R], I32, slot="wk_raw")
-        nc.sync.dma_start(
-            out=wq_raw[:].rearrange("p (a w) -> p a w", a=PASSES),
-            in_=wq_words.rearrange("a p r i -> p a (r i)").bitcast(I32),
-        )
+
+        wq_scale_raw = wk_scale_raw[:, 0 : R // 4]
+        wv4_plane = wk_scale_raw[:, R // 4 : R // 4 + N // 4]
+        x_raw = held("x_raw", [P, PASSES, 4, M], F32)[:]
+        wq_raw = held("wq_raw", [P, PASSES * R], I32)[:]
+        wv8_raw = held("wv8_raw", [P, 4, N], F32)[:]
+        wv4_codes = held("wv4_codes", [P, N // 2], I32)[:]
+
+        def load_wq_scales():
+            for quad in QUADS:
+                nc.sync.dma_start(
+                    out=wq_scale_raw[32 * quad + 4 : 32 * quad + 12, :],
+                    in_=wq_scales[:, 4 * quad : 4 * quad + 4, :].bitcast(I32),
+                )
+
+        def load_wv4_scales():
+            for quad in QUADS:
+                nc.sync.dma_start(
+                    out=wv4_plane[32 * quad : 32 * quad + 4, :],
+                    in_=wv4_scales[0, 4 * quad : 4 * quad + 4, :].bitcast(I32),
+                )
+
+        def load_x():
+            nc.sync.dma_start(out=x_raw, in_=x.rearrange("(a p i) m -> p a i m", a=PASSES, i=4))
+
+        def load_wq():
+            nc.sync.dma_start(
+                out=wq_raw.rearrange("p (a w) -> p a w", a=PASSES),
+                in_=wq_words.rearrange("a p r i -> p a (r i)").bitcast(I32),
+            )
+
+        def load_wv8():
+            nc.sync.dma_start(out=wv8_raw, in_=wv8.rearrange("(p i) n -> p i n", i=4))
+
+        def load_wv4():
+            nc.sync.dma_start(out=wv4_codes, in_=wv4_words[0].bitcast(I32))
+
+        load_x()
+        load_wq()
+        load_wq_scales()
+        load_wv8()
+        load_wv4()
+        load_wv4_scales()
         gather_words(1, 0)
         gather_words(1, 1)
 
@@ -125,7 +150,13 @@ def tile_list_kvt_qf_act_kernel(
         ka_codes = held("ka_codes", [P, 2, J], U32)
         ka_plane = held("ka_plane", [P, 2, J], U8)
 
-        def keys(jc, b):
+        def relu_out(engine, out, in_):
+            if engine == "S":
+                nc.scalar.activation(out=out, in_=in_, func=RELU)
+            else:
+                nc.vector.tensor_scalar_max(out=out, in0=in_, scalar1=0.0)
+
+        def keys(jc, b, engine="S"):
             h, j0 = divmod(jc * CHUNK, HALF)
             bank = psum.tile([P, 4, CHUNK], F32, name="bank", tag="bank")
             for t in range(4):
@@ -140,16 +171,16 @@ def tile_list_kvt_qf_act_kernel(
                         start=(a == 0),
                         stop=(a == PASSES - 1),
                     )
-            nc.scalar.activation(
-                out=ka_bf[:, b, 4 * jc * CHUNK : 4 * (jc + 1) * CHUNK].rearrange("p (n t) -> p n t", t=4),
-                in_=bank[:].rearrange("p t n -> p n t"),
-                func=RELU,
+            relu_out(
+                engine,
+                ka_bf[:, b, 4 * jc * CHUNK : 4 * (jc + 1) * CHUNK].rearrange("p (n t) -> p n t", t=4),
+                bank[:].rearrange("p t n -> p n t"),
             )
 
         wide_banks = {}
         ka_planar = held("ka_planar", [P, 2, 4, HALF], BF16)
 
-        def wide_pass(b, a):
+        def wide_pass(b, a, engines="SSSS"):
             for t in range(4):
                 if a == 0:
                     wide_banks[b, t] = psum.tile([P, HALF], F32, name="bank", tag="bank")
@@ -164,7 +195,7 @@ def tile_list_kvt_qf_act_kernel(
                     stop=(a == PASSES - 1),
                 )
                 if a == PASSES - 1:
-                    nc.scalar.activation(out=ka_planar[:, b, t, :], in_=wide_banks[b, t][:], func=RELU)
+                    relu_out(engines[t], ka_planar[:, b, t, :], wide_banks[b, t][:])
 
         def wide_finish(b):
             nc.vector.tensor_copy(
@@ -198,15 +229,19 @@ def tile_list_kvt_qf_act_kernel(
         qa_codes = held("qa_codes", [P, 2, M], U32)
         qa_plane = held("qa_plane", [P, 2, M], U8)
 
-        def prepare_queries():
+        def round_x():
             nc.vector.tensor_copy(
                 out=x_bf[:].rearrange("p a (c u) i -> p a c i u", u=4),
                 in_=x_raw[:].rearrange("p a i (c u) -> p a c i u", u=4),
             )
-            reorder(wq_plane[:], wq_scale_raw[:], 2)
+
+        def quantise_x():
             nc.vector.quantize_mx(
                 out=x_codes[:].bitcast(FP8X4), scales=x_plane[:], in_=x_bf[:].rearrange("p a m i -> p (a m i)")
             )
+
+        def reorder_wq():
+            reorder(wq_plane[:], wq_scale_raw[:], 2)
             reorder(wq_codes[:], wq_raw[:], 8)
 
         def prepare_values():
@@ -220,7 +255,7 @@ def tile_list_kvt_qf_act_kernel(
 
         wq_plane_bytes = wq_plane[:].bitcast(U8)
 
-        def queries(b):
+        def queries(b, engines="SS"):
             for mc in range(M // CHUNK):
                 bank = psum.tile([P, 4, CHUNK], F32, name="bank", tag="bank")
                 for t in range(4):
@@ -236,17 +271,17 @@ def tile_list_kvt_qf_act_kernel(
                             start=(a == 0),
                             stop=(a == PASSES - 1),
                         )
-                nc.scalar.activation(
-                    out=qa_bf[:, b, 4 * mc * CHUNK : 4 * (mc + 1) * CHUNK].rearrange("p (n t) -> p n t", t=4),
-                    in_=bank[:].rearrange("p t n -> p n t"),
-                    func=RELU,
+                relu_out(
+                    engines[mc],
+                    qa_bf[:, b, 4 * mc * CHUNK : 4 * (mc + 1) * CHUNK].rearrange("p (n t) -> p n t", t=4),
+                    bank[:].rearrange("p t n -> p n t"),
                 )
             nc.vector.quantize_mx(out=qa_codes[:, b, :].bitcast(FP8X4), scales=qa_plane[:, b, :], in_=qa_bf[:, b, :])
 
         wv4_code_bytes = wv4_codes[:].bitcast(U8)
         wv4_plane_bytes = wv4_plane[:].bitcast(U8)
 
-        def values(h):
+        def values(h, engines="VV"):
             for nt in range(N // P):
                 bank = psum.tile([P, HALF], F32, name="bank", tag="bank")
                 cols = slice(nt * P, (nt + 1) * P)
@@ -269,10 +304,13 @@ def tile_list_kvt_qf_act_kernel(
                     stop=True,
                 )
                 result = stage.tile([P, HALF], F32, name="result", tag="result")
-                nc.vector.tensor_copy(out=result[:], in_=bank[:])
+                if engines[nt] == "S":
+                    nc.scalar.activation(out=result[:], in_=bank[:], func=COPY)
+                else:
+                    nc.vector.tensor_copy(out=result[:], in_=bank[:])
                 nc.sync.dma_start(out=out_1[cols, h * HALF : (h + 1) * HALF], in_=result[:])
 
-        def scores(j0, width, split):
+        def scores(j0, width, engines):
             for mt in range(M // P):
                 bank = psum.tile([P, width], F32, name="bank", tag="bank")
                 cols = slice(mt * P, (mt + 1) * P)
@@ -287,7 +325,7 @@ def tile_list_kvt_qf_act_kernel(
                         stop=(b == 1),
                     )
                 result = stage.tile([P, width], F32, name="result", tag="result")
-                if split and mt == 0:
+                if engines[mt] == "S":
                     nc.scalar.activation(out=result[:], in_=bank[:], func=COPY, scale=SCORE_SCALE)
                 else:
                     nc.vector.tensor_scalar(out=result[:], in0=bank[:], scalar1=SCORE_SCALE, scalar2=None, op0=MULT)
@@ -295,20 +333,32 @@ def tile_list_kvt_qf_act_kernel(
 
         wide_pass(0, 0)
         wide_pass(1, 0)
-        wide_pass(0, 1)
-        wide_pass(1, 1)
-        prepare_values()
+        wide_pass(1, 1, "VSSS")
+        wide_pass(0, 1, "SSSS")
+        round_x()
+        reorder_wq()
         wide_finish(0)
-        key_pair(4)
+        keys(4,0,"S")
+        keys(7,0,"S")
+        quantise_x()
+        keys(5,0,"S")
+        keys(7,1,"S")
+        keys(5,1,"S")
+        keys(6,0,"S")
+        keys(4,1,"S")
         wide_finish(1)
+        prepare_values()
+        quantise_keys(512,256,0)
         quantise_keys(0, HALF, 0)
         quantise_keys(0, HALF, 1)
-        values(0)
-        prepare_queries()
-        queries(0)
-        queries(1)
-        values(1)
-        key_pair(6)
-        scores(0, HALF, False)
-        scores(HALF, 256, True)
-        scores(HALF + 256, 256, True)
+        quantise_keys(768,256,0)
+        queries(1,"SS")
+        queries(0,"SV")
+        keys(6,1,"S")
+        values(1,"SV")
+        quantise_keys(768,256,1)
+        scores(0, HALF, "VS")
+        scores(HALF + 256, 256, "SV")
+        quantise_keys(512,256,1)
+        values(0,"VS")
+        scores(HALF, 256, "SV")

@@ -106,14 +106,14 @@ def tile_list_kvt_qf_act_kernel(
 
         def load_wq_scales():
             for quad in QUADS:
-                nc.sync.dma_start(
+                nc.gpsimd.dma_start(
                     out=wq_scale_raw[32 * quad + 4 : 32 * quad + 12, :],
                     in_=wq_scales[:, 4 * quad : 4 * quad + 4, :].bitcast(I32),
                 )
 
         def load_wv4_scales():
             for quad in QUADS:
-                nc.sync.dma_start(
+                nc.gpsimd.dma_start(
                     out=wv4_plane[32 * quad : 32 * quad + 4, :],
                     in_=wv4_scales[0, 4 * quad : 4 * quad + 4, :].bitcast(I32),
                 )
@@ -121,10 +121,10 @@ def tile_list_kvt_qf_act_kernel(
         def load_x():
             nc.sync.dma_start(out=x_raw, in_=x.rearrange("(a p i) m -> p a i m", a=PASSES, i=4))
 
-        def load_wq():
+        def load_wq(b):
             nc.sync.dma_start(
-                out=wq_raw.rearrange("p (a w) -> p a w", a=PASSES),
-                in_=wq_words.rearrange("a p r i -> p a (r i)").bitcast(I32),
+                out=wq_raw[:, b * R : (b + 1) * R].rearrange("p (a w) -> p a w", a=PASSES),
+                in_=wq_words[:, :, b * 512 : (b + 1) * 512, :].rearrange("a p r i -> p a (r i)").bitcast(I32),
             )
 
         def load_wv8():
@@ -133,12 +133,13 @@ def tile_list_kvt_qf_act_kernel(
         def load_wv4():
             nc.sync.dma_start(out=wv4_codes, in_=wv4_words[0].bitcast(I32))
 
-        load_x()
-        load_wq()
         load_wq_scales()
+        load_wv4_scales()
+        load_x()
         load_wv8()
         load_wv4()
-        load_wv4_scales()
+        load_wq(0)
+        load_wq(1)
         gather_words(1, 0)
         gather_words(1, 1)
 
@@ -221,7 +222,7 @@ def tile_list_kvt_qf_act_kernel(
         x_codes = held("x_codes", [P, PASSES * M], U32)
         x_plane = held("x_plane", [P, PASSES * M], U8)
         wq_codes = held("wq_codes", [P, PASSES * R], I32)
-        wq_plane = held("wq_plane", [P, R // 4], I32)
+        wq_plane = held("wq_plane", [P, R // 4], I32, slot="tab_win1")
         wv8_bf = held("wv8_bf", [P, N, 4], BF16)
         wv8_codes = held("wv8_codes", [P, N], U32)
         wv8_plane = held("wv8_plane", [P, N], U8)
@@ -229,26 +230,32 @@ def tile_list_kvt_qf_act_kernel(
         qa_codes = held("qa_codes", [P, 2, M], U32)
         qa_plane = held("qa_plane", [P, 2, M], U8)
 
-        def round_x():
-            nc.vector.tensor_copy(
-                out=x_bf[:].rearrange("p a (c u) i -> p a c i u", u=4),
-                in_=x_raw[:].rearrange("p a i (c u) -> p a c i u", u=4),
-            )
+        def round_rows(engine, dst, src):
+            dst = dst.rearrange("p (c u) i -> p c i u", u=4)
+            src = src.rearrange("p i (c u) -> p c i u", u=4)
+            if engine == "S":
+                nc.scalar.copy(out=dst, in_=src)
+            else:
+                nc.vector.tensor_copy(out=dst, in_=src)
+
+        def round_x(a, engine):
+            round_rows(engine, x_bf[:, a], x_raw[:, a])
 
         def quantise_x():
             nc.vector.quantize_mx(
                 out=x_codes[:].bitcast(FP8X4), scales=x_plane[:], in_=x_bf[:].rearrange("p a m i -> p (a m i)")
             )
 
-        def reorder_wq():
+        def reorder_wq_scales():
             reorder(wq_plane[:], wq_scale_raw[:], 2)
-            reorder(wq_codes[:], wq_raw[:], 8)
 
-        def prepare_values():
-            nc.vector.tensor_copy(
-                out=wv8_bf[:].rearrange("p (c u) i -> p c i u", u=4),
-                in_=wv8_raw[:].rearrange("p i (c u) -> p c i u", u=4),
-            )
+        def reorder_wq(b):
+            reorder(wq_codes[:, b * R : (b + 1) * R], wq_raw[:, b * R : (b + 1) * R], 8)
+
+        def round_wv8(engine):
+            round_rows(engine, wv8_bf[:], wv8_raw)
+
+        def quantise_wv8():
             nc.vector.quantize_mx(
                 out=wv8_codes[:].bitcast(FP8X4), scales=wv8_plane[:], in_=wv8_bf[:].rearrange("p n i -> p (n i)")
             )
@@ -261,10 +268,11 @@ def tile_list_kvt_qf_act_kernel(
                 for t in range(4):
                     for a in range(PASSES):
                         col = b * 512 + t * 128
+                        word = b * R + a * 512 + t * 128
                         m0 = a * M + mc * CHUNK
                         nc.tensor.matmul_mx(
                             out=bank[:, t, :],
-                            lhsT=wq_codes[:, a * R + col : a * R + col + 128].bitcast(FP8X4),
+                            lhsT=wq_codes[:, word : word + 128].bitcast(FP8X4),
                             lhsT_scale=wq_plane_bytes[4 + 4 * a : P, col : col + 128],
                             rhs=x_codes[:, m0 : m0 + CHUNK].bitcast(FP8X4),
                             rhs_scale=x_plane[:, m0 : m0 + CHUNK],
@@ -281,8 +289,8 @@ def tile_list_kvt_qf_act_kernel(
         wv4_code_bytes = wv4_codes[:].bitcast(U8)
         wv4_plane_bytes = wv4_plane[:].bitcast(U8)
 
-        def values(h, engines="VV"):
-            for nt in range(N // P):
+        def values(h, nt, engine):
+            if True:
                 bank = psum.tile([P, HALF], F32, name="bank", tag="bank")
                 cols = slice(nt * P, (nt + 1) * P)
                 nc.tensor.matmul_mx(
@@ -304,7 +312,7 @@ def tile_list_kvt_qf_act_kernel(
                     stop=True,
                 )
                 result = stage.tile([P, HALF], F32, name="result", tag="result")
-                if engines[nt] == "S":
+                if engine == "S":
                     nc.scalar.activation(out=result[:], in_=bank[:], func=COPY)
                 else:
                     nc.vector.tensor_copy(out=result[:], in_=bank[:])
@@ -333,32 +341,36 @@ def tile_list_kvt_qf_act_kernel(
 
         wide_pass(0, 0)
         wide_pass(1, 0)
-        wide_pass(1, 1, "VSSS")
         wide_pass(0, 1, "SSSS")
-        round_x()
-        reorder_wq()
-        wide_finish(0)
-        keys(4,0,"S")
-        keys(7,0,"S")
+        wide_pass(1, 1, "SSSS")
+        reorder_wq_scales()
+        reorder_wq(0)
+        reorder_wq(1)
+        round_x(0,"V")
+        round_x(1,"V")
+        round_wv8("V")
         quantise_x()
-        keys(5,0,"S")
-        keys(7,1,"S")
-        keys(5,1,"S")
-        keys(6,0,"S")
-        keys(4,1,"S")
+        quantise_wv8()
+        wide_finish(0)
         wide_finish(1)
-        prepare_values()
-        quantise_keys(512,256,0)
+        keys(4,0,"S")
+        keys(5,0,"S")
+        keys(6,0,"S")
+        keys(7,0,"S")
+        keys(4,1,"S")
+        keys(5,1,"S")
+        keys(6,1,"S")
+        keys(7,1,"S")
+        queries(0,"SS")
+        queries(1,"SV")
         quantise_keys(0, HALF, 0)
         quantise_keys(0, HALF, 1)
-        quantise_keys(768,256,0)
-        queries(1,"SS")
-        queries(0,"SV")
-        keys(6,1,"S")
-        values(1,"SV")
-        quantise_keys(768,256,1)
-        scores(0, HALF, "VS")
-        scores(HALF + 256, 256, "SV")
-        quantise_keys(512,256,1)
-        values(0,"VS")
-        scores(HALF, 256, "SV")
+        quantise_keys(HALF, HALF, 0)
+        values(0,0,"V")
+        values(0,1,"S")
+        values(1,0,"S")
+        values(1,1,"S")
+        quantise_keys(HALF, HALF, 1)
+        scores(0, HALF, "VV")
+        scores(HALF, 256, "SS")
+        scores(HALF + 256, 256, "VV")

@@ -4,7 +4,16 @@ import concourse.mybir as mybir
 
 K, R, M, N, T, J = 1024, 1024, 256, 256, 4096, 1024
 FLOPS = 2 * (K * R * M + K * R * J + R * M * J + K * N * J)
-BYTES = (K * J + K * J // 32) + 4 * K * M + (K * R + K * R // 32) + (K * R // 2 + K * R // 32) + 4 * 512 * N + (512 * N // 2 + 512 * N // 32) + 2 * J + 4 * (M + N) * J
+BYTES = (
+    (K * J + K * J // 32)
+    + 4 * K * M
+    + (K * R + K * R // 32)
+    + (K * R // 2 + K * R // 32)
+    + 4 * (K // 2) * N
+    + ((K // 2) * N // 2 + (K // 2) * N // 32)
+    + 2 * J
+    + 4 * (M + N) * J
+)
 
 F32 = mybir.dt.float32
 BF16 = mybir.dt.bfloat16
@@ -19,11 +28,20 @@ COPY = mybir.ActivationFunctionType.Copy
 MULT = mybir.AluOpType.mult
 
 P = 128
-PASSES = 2
-HALF = 512
-CHUNK = 128
+PACK = 4
+PASS = P * PACK
+PASSES = K // PASS
+BLOCKS = PASS // 32
+HALF = J // 2
+QUARTER = J // 4
+CHUNK = HALF // PACK
+LIST_GROUP = 16
+QUADRANTS = (0, 2, 1, 3)
 SCORE_SCALE = 0.03125
-QUADS = (0, 2, 1, 3)
+SCALAR, VECTOR = "scalar", "vector"
+VECTOR_TILES = 23
+SCALAR_RESULTS = 7
+PSUM_BANKS = 8
 
 
 def tile_list_kvt_qf_act_kernel(
@@ -32,113 +50,110 @@ def tile_list_kvt_qf_act_kernel(
     nc = tc.nc
     with ExitStack() as ctx:
         keep = ctx.enter_context(tc.tile_pool(name="keep", bufs=1))
-        stage = ctx.enter_context(tc.tile_pool(name="stage", bufs=10))
-        psum = ctx.enter_context(tc.psum_pool(name="psum", bufs=8))
+        stage = ctx.enter_context(tc.tile_pool(name="stage", bufs=SCALAR_RESULTS))
+        ring = ctx.enter_context(tc.tile_pool(name="ring", bufs=VECTOR_TILES))
+        psum = ctx.enter_context(tc.psum_pool(name="psum", bufs=PSUM_BANKS))
 
-        def held(name, shape, dtype, slot=None):
-            return keep.tile(shape, dtype, name=name, tag=slot or name, align_bytes=64)
+        def held(name, shape, dtype):
+            return keep.tile(shape, dtype, name=name, tag=name, align_bytes=64)
 
-        offsets = keep.tile([P, J // 16], U16, name="offsets")
+        def in_turn(name, shape, dtype):
+            return ring.tile(shape, dtype, name=name, tag="in_turn", align_bytes=64)
+
+        def new_bank(shape):
+            return psum.tile(shape, F32, name="bank", tag="bank")
+
+        def quadrant_rows(quad, first=0, count=4):
+            return slice(32 * quad + first, 32 * quad + first + count)
+
+        offsets = keep.tile([P, J // LIST_GROUP], U16, name="offsets")
         tab_scale_rows = held("tab_scale_rows", [P, T // 4], I32)
         wk_raw = held("wk_raw", [P, PASSES * R // 2], I32)
-        wk_scale_raw = held("wk_scale_raw", [P, PASSES * R // 4], I32)
+        weight_scale_rows = held("weight_scale_rows", [P, PASSES * R // 4], I32)
         v_plane = held("v_plane", [P, PASSES, J // 4], I32)
         v_scale_rows = held("v_scale_rows", [P, J], U8)
-        tab_win = [held("tab_win0", [P, T], I32)]
+        tab_win = [held("tab_win%d" % a, [P, T], I32) for a in range(PASSES)]
 
         def load_table(a):
             nc.sync.dma_start(out=tab_win[a][:], in_=tab_words[a].rearrange("p t i -> p (t i)").bitcast(I32))
 
         def move_table_scales(a):
-            for quad in QUADS:
-                row = 16 * a + 4 * quad
+            for quad in QUADRANTS:
+                row = BLOCKS * a + 4 * quad
                 nc.sync.dma_start(
-                    out=v_plane[32 * quad : 32 * quad + 4, a, :], in_=v_scale_rows[row : row + 4, :].bitcast(I32)
+                    out=v_plane[quadrant_rows(quad), a, :], in_=v_scale_rows[row : row + 4, :].bitcast(I32)
                 )
 
-        nc.vector.memset(wk_scale_raw[:], 0)
+        nc.vector.memset(weight_scale_rows[:], 0)
         nc.vector.memset(tab_scale_rows[32:64, :], 0)
         nc.vector.memset(tab_scale_rows[64:128, :], 0)
         nc.vector.memset(v_plane[:], 0)
+
         nc.sync.dma_start(offsets[:], offs)
         nc.sync.dma_start(out=tab_scale_rows[0:32, :], in_=tab_scales.rearrange("a q t -> (a q) t").bitcast(I32))
         nc.sync.dma_start(
             out=wk_raw[:].rearrange("p (a w) -> p a w", a=PASSES), in_=wk_words.rearrange("a p n -> p a n").bitcast(I32)
         )
-        for quad in QUADS:
+        for quad in QUADRANTS:
             nc.sync.dma_start(
-                out=wk_scale_raw[32 * quad : 32 * quad + 4, :].rearrange("p (a w) -> p a w", a=PASSES),
+                out=weight_scale_rows[quadrant_rows(quad), :].rearrange("p (a w) -> p a w", a=PASSES),
                 in_=wk_scales[:, 4 * quad : 4 * quad + 4, :].rearrange("a r n -> r a n").bitcast(I32),
             )
         load_table(0)
         nc.vector.tensor_copy(out=v_scale_rows[:], in_=tab_scale_rows[:].bitcast(U8).indirect(offsets[:]))
         move_table_scales(0)
-        tab_win.append(held("tab_win1", [P, T], I32))
         load_table(1)
         move_table_scales(1)
 
         def reorder(dst, src, run):
             nc.vector.tensor_copy(
-                out=dst.rearrange("p (g t q u) -> p g t q u", t=4, q=16, u=run),
-                in_=src.rearrange("p (g q t u) -> p g t q u", t=4, q=16, u=run),
+                out=dst.rearrange("p (g t q u) -> p g t q u", t=PACK, q=BLOCKS, u=run),
+                in_=src.rearrange("p (g q t u) -> p g t q u", t=PACK, q=BLOCKS, u=run),
             )
 
-        v_codes = [[held("v_codes%d%d" % (a, h), [P, HALF], U32) for h in range(2)] for a in range(PASSES)]
+        v_codes = {}
 
         def gather_words(a, h):
+            columns = HALF // LIST_GROUP
+            v_codes[a, h] = in_turn("v_codes", [P, HALF], U32)
             nc.vector.tensor_copy(
-                out=v_codes[a][h][:], in_=tab_win[a][:].bitcast(U32).indirect(offsets[:, 32 * h : 32 * h + 32])
+                out=v_codes[a, h][:],
+                in_=tab_win[a][:].bitcast(U32).indirect(offsets[:, columns * h : columns * (h + 1)]),
             )
 
         wk_plane = held("wk_plane", [P, PASSES * R // 4], I32)
         wk_codes = held("wk_codes", [P, PASSES * R // 2], I32)
-        reorder(wk_plane[:], wk_scale_raw[:], 2)
+        reorder(wk_plane[:], weight_scale_rows[:], 2)
         reorder(wk_codes[:], wk_raw[:], 4)
         gather_words(0, 0)
         gather_words(0, 1)
 
-        wq_scale_raw = wk_scale_raw[:, 0 : R // 4]
-        wv4_plane = wk_scale_raw[:, R // 4 : R // 4 + N // 4]
-        x_raw = held("x_raw", [P, PASSES, 4, M], F32)[:]
-        wq_raw = held("wq_raw", [P, PASSES * R], I32)[:]
-        wv8_raw = held("wv8_raw", [P, 4, N], F32)[:]
-        wv4_codes = held("wv4_codes", [P, N // 2], I32)[:]
-
-        def load_wq_scales():
-            for quad in QUADS:
-                nc.gpsimd.dma_start(
-                    out=wq_scale_raw[32 * quad + 4 : 32 * quad + 12, :],
-                    in_=wq_scales[:, 4 * quad : 4 * quad + 4, :].bitcast(I32),
-                )
-
-        def load_wv4_scales():
-            for quad in QUADS:
-                nc.gpsimd.dma_start(
-                    out=wv4_plane[32 * quad : 32 * quad + 4, :],
-                    in_=wv4_scales[0, 4 * quad : 4 * quad + 4, :].bitcast(I32),
-                )
-
-        def load_x():
-            nc.sync.dma_start(out=x_raw, in_=x.rearrange("(a p i) m -> p a i m", a=PASSES, i=4))
+        wq_scale_rows = weight_scale_rows[:, 0 : R // 4]
+        wv4_plane = weight_scale_rows[:, R // 4 : R // 4 + N // 4]
+        x_raw = held("x_raw", [P, PASSES, PACK, M], F32)
+        wq_raw = held("wq_raw", [P, PASSES, R], I32)
+        wv8_raw = held("wv8_raw", [P, PACK, N], F32)
+        wv4_codes = held("wv4_codes", [P, N // 2], I32)
 
         def load_wq(b):
             nc.sync.dma_start(
-                out=wq_raw[:, b * R : (b + 1) * R].rearrange("p (a w) -> p a w", a=PASSES),
-                in_=wq_words[:, :, b * 512 : (b + 1) * 512, :].rearrange("a p r i -> p a (r i)").bitcast(I32),
+                out=wq_raw[:, b, :].rearrange("p (a w) -> p a w", a=PASSES),
+                in_=wq_words[:, :, b * PASS : (b + 1) * PASS, :].rearrange("a p r i -> p a (r i)").bitcast(I32),
             )
 
-        def load_wv8():
-            nc.sync.dma_start(out=wv8_raw, in_=wv8.rearrange("(p i) n -> p i n", i=4))
-
-        def load_wv4():
-            nc.sync.dma_start(out=wv4_codes, in_=wv4_words[0].bitcast(I32))
-
-        load_wq_scales()
-        load_wv4_scales()
-        load_x()
-        load_wv8()
-        load_wv4()
+        nc.sync.dma_start(out=wv8_raw[:], in_=wv8.rearrange("(p i) n -> p i n", i=PACK))
+        nc.sync.dma_start(out=wv4_codes[:], in_=wv4_words[0].bitcast(I32))
+        nc.sync.dma_start(out=x_raw[:], in_=x.rearrange("(a p i) m -> p a i m", a=PASSES, i=PACK))
+        for quad in QUADRANTS:
+            nc.sync.dma_start(
+                out=wv4_plane[quadrant_rows(quad), :], in_=wv4_scales[0, 4 * quad : 4 * quad + 4, :].bitcast(I32)
+            )
         load_wq(0)
+        for quad in QUADRANTS:
+            nc.sync.dma_start(
+                out=wq_scale_rows[quadrant_rows(quad, first=4, count=8), :],
+                in_=wq_scales[:, 4 * quad : 4 * quad + 4, :].bitcast(I32),
+            )
         load_wq(1)
         gather_words(1, 0)
         gather_words(1, 1)
@@ -146,231 +161,206 @@ def tile_list_kvt_qf_act_kernel(
         v_plane_bytes = v_plane[:].rearrange("p a w -> p (a w)").bitcast(U8)
         wk_plane_bytes = wk_plane[:].bitcast(U8)
         wk_code_bytes = wk_codes[:].bitcast(U8)
-
-        ka_bf = held("ka_bf", [P, 2, J * 4], BF16)
-        ka_codes = held("ka_codes", [P, 2, J], U32)
-        ka_plane = held("ka_plane", [P, 2, J], U8)
+        wv4_plane_bytes = wv4_plane.bitcast(U8)
+        wv4_code_bytes = wv4_codes[:].bitcast(U8)
 
         def relu_out(engine, out, in_):
-            if engine == "S":
+            if engine == SCALAR:
                 nc.scalar.activation(out=out, in_=in_, func=RELU)
             else:
                 nc.vector.tensor_scalar_max(out=out, in0=in_, scalar1=0.0)
 
-        def keys(jc, b, engine="S"):
-            h, j0 = divmod(jc * CHUNK, HALF)
-            bank = psum.tile([P, 4, CHUNK], F32, name="bank", tag="bank")
-            for t in range(4):
-                for a in range(PASSES):
-                    col = a * R + b * 512 + t * 128
-                    nc.tensor.matmul_mx(
-                        out=bank[:, t, :],
-                        lhsT=wk_code_bytes[:, 2 * col : 2 * col + 256].bitcast(FP4X4),
-                        lhsT_scale=wk_plane_bytes[:, col : col + 128],
-                        rhs=v_codes[a][h][:, j0 : j0 + CHUNK].bitcast(FP8X4),
-                        rhs_scale=v_plane_bytes[:, a * J + jc * CHUNK : a * J + (jc + 1) * CHUNK],
-                        start=(a == 0),
-                        stop=(a == PASSES - 1),
-                    )
-            relu_out(
-                engine,
-                ka_bf[:, b, 4 * jc * CHUNK : 4 * (jc + 1) * CHUNK].rearrange("p (n t) -> p n t", t=4),
-                bank[:].rearrange("p t n -> p n t"),
+        def quantise(name, values, width):
+            codes = in_turn(name + "_codes", [P, width], U32)
+            plane = held(name + "_plane", [P, width], U8)
+            nc.vector.quantize_mx(out=codes[:].bitcast(FP8X4), scales=plane[:], in_=values)
+            return codes, plane
+
+        def key_matmul(out, a, b, t, j0, width):
+            h, first = divmod(j0, HALF)
+            col = a * R + b * PASS + t * P
+            nc.tensor.matmul_mx(
+                out=out,
+                lhsT=wk_code_bytes[:, 2 * col : 2 * (col + P)].bitcast(FP4X4),
+                lhsT_scale=wk_plane_bytes[:, col : col + P],
+                rhs=v_codes[a, h][:, first : first + width].bitcast(FP8X4),
+                rhs_scale=v_plane_bytes[:, a * J + j0 : a * J + j0 + width],
+                start=(a == 0),
+                stop=(a == PASSES - 1),
             )
 
         wide_banks = {}
-        ka_planar = held("ka_planar", [P, 2, 4, HALF], BF16)
+        ka_planar = held("ka_planar", [P, PASSES, PACK, HALF], BF16)
+        ka_wide = {}
 
-        def wide_pass(b, a, engines="SSSS"):
-            for t in range(4):
-                if a == 0:
-                    wide_banks[b, t] = psum.tile([P, HALF], F32, name="bank", tag="bank")
-                col = a * R + b * 512 + t * 128
-                nc.tensor.matmul_mx(
-                    out=wide_banks[b, t][:],
-                    lhsT=wk_code_bytes[:, 2 * col : 2 * col + 256].bitcast(FP4X4),
-                    lhsT_scale=wk_plane_bytes[:, col : col + 128],
-                    rhs=v_codes[a][0][:].bitcast(FP8X4),
-                    rhs_scale=v_plane_bytes[:, a * J : a * J + HALF],
-                    start=(a == 0),
-                    stop=(a == PASSES - 1),
-                )
-                if a == PASSES - 1:
-                    relu_out(engines[t], ka_planar[:, b, t, :], wide_banks[b, t][:])
+        def wide_keys_open(b):
+            for t in range(PACK):
+                wide_banks[b, t] = new_bank([P, HALF])
+                key_matmul(wide_banks[b, t][:], 0, b, t, 0, HALF)
 
-        def wide_finish(b):
+        def wide_keys_close(b, engines):
+            for t in range(PACK):
+                key_matmul(wide_banks[b, t][:], 1, b, t, 0, HALF)
+                relu_out(engines[t], ka_planar[:, b, t, :], wide_banks[b, t][:])
+
+        def wide_keys_interleave(b):
+            ka_wide[b] = in_turn("ka_wide", [P, HALF * PACK], BF16)
             nc.vector.tensor_copy(
-                out=ka_bf[:, b, 0 : 4 * HALF].rearrange("p (c u t) -> p c t u", u=4, t=4),
+                out=ka_wide[b][:].rearrange("p (c u t) -> p c t u", u=4, t=PACK),
                 in_=ka_planar[:, b].rearrange("p t (c u) -> p c t u", u=4),
             )
 
-        def quantise_keys(j0, width, b):
-            nc.vector.quantize_mx(
-                out=ka_codes[:, b, j0 : j0 + width].bitcast(FP8X4),
-                scales=ka_plane[:, b, j0 : j0 + width],
-                in_=ka_bf[:, b, 4 * j0 : 4 * (j0 + width)],
+        ka_narrow = held("ka_narrow", [P, PASSES, HALF * PACK], BF16)
+
+        def narrow_keys(c, b):
+            bank = new_bank([P, PACK, CHUNK])
+            for t in range(PACK):
+                for a in range(PASSES):
+                    key_matmul(bank[:, t, :], a, b, t, HALF + c * CHUNK, CHUNK)
+            relu_out(
+                SCALAR,
+                ka_narrow[:, b, PACK * c * CHUNK : PACK * (c + 1) * CHUNK].rearrange("p (n t) -> p n t", t=PACK),
+                bank[:].rearrange("p t n -> p n t"),
             )
 
-        def key_pair(jc):
-            for c in (jc, jc + 1):
-                for b in range(2):
-                    keys(c, b)
-            for b in range(2):
-                quantise_keys(jc * CHUNK, 2 * CHUNK, b)
+        ka_mx = {}
 
-        x_bf = held("x_bf", [P, PASSES, M, 4], BF16)
-        x_codes = held("x_codes", [P, PASSES * M], U32)
-        x_plane = held("x_plane", [P, PASSES * M], U8)
-        wq_codes = held("wq_codes", [P, PASSES * R], I32)
-        wq_plane = held("wq_plane", [P, R // 4], I32, slot="tab_win1")
-        wv8_bf = held("wv8_bf", [P, N, 4], BF16)
-        wv8_codes = held("wv8_codes", [P, N], U32)
-        wv8_plane = held("wv8_plane", [P, N], U8)
-        qa_bf = held("qa_bf", [P, 2, M * 4], BF16)
-        qa_codes = held("qa_codes", [P, 2, M], U32)
-        qa_plane = held("qa_plane", [P, 2, M], U8)
-
-        def round_rows(engine, dst, src):
-            dst = dst.rearrange("p (c u) i -> p c i u", u=4)
-            src = src.rearrange("p i (c u) -> p c i u", u=4)
-            if engine == "S":
-                nc.scalar.copy(out=dst, in_=src)
+        def quantise_keys(b, j0, width):
+            if j0 < HALF:
+                values = ka_wide[b][:]
             else:
-                nc.vector.tensor_copy(out=dst, in_=src)
+                values = ka_narrow[:, b, PACK * (j0 - HALF) : PACK * (j0 - HALF + width)]
+            codes, plane = quantise("ka%d_%d" % (b, j0), values, width)
+            for first in range(0, width, QUARTER):
+                ka_mx[b, j0 + first] = (codes, plane, first)
 
-        def round_x(a, engine):
-            round_rows(engine, x_bf[:, a], x_raw[:, a])
+        qa_bf = held("qa_bf", [P, PASSES, M * PACK], BF16)
 
-        def quantise_x():
-            nc.vector.quantize_mx(
-                out=x_codes[:].bitcast(FP8X4), scales=x_plane[:], in_=x_bf[:].rearrange("p a m i -> p (a m i)")
-            )
-
-        def reorder_wq_scales():
-            reorder(wq_plane[:], wq_scale_raw[:], 2)
-
-        def reorder_wq(b):
-            reorder(wq_codes[:, b * R : (b + 1) * R], wq_raw[:, b * R : (b + 1) * R], 8)
-
-        def round_wv8(engine):
-            round_rows(engine, wv8_bf[:], wv8_raw)
-
-        def quantise_wv8():
-            nc.vector.quantize_mx(
-                out=wv8_codes[:].bitcast(FP8X4), scales=wv8_plane[:], in_=wv8_bf[:].rearrange("p n i -> p (n i)")
-            )
-
-        wq_plane_bytes = wq_plane[:].bitcast(U8)
-
-        def queries(b, engines="SS"):
-            for mc in range(M // CHUNK):
-                bank = psum.tile([P, 4, CHUNK], F32, name="bank", tag="bank")
-                for t in range(4):
+        def queries(b, wq_codes, wq_plane, x_mx):
+            x_codes, x_plane = x_mx
+            wq_plane_bytes = wq_plane[:].bitcast(U8)
+            for c in range(M // CHUNK):
+                bank = new_bank([P, PACK, CHUNK])
+                for t in range(PACK):
                     for a in range(PASSES):
-                        col = b * 512 + t * 128
-                        word = b * R + a * 512 + t * 128
-                        m0 = a * M + mc * CHUNK
+                        word = a * PASS + t * P
+                        col = b * PASS + t * P
+                        m0 = a * M + c * CHUNK
                         nc.tensor.matmul_mx(
                             out=bank[:, t, :],
-                            lhsT=wq_codes[:, word : word + 128].bitcast(FP8X4),
-                            lhsT_scale=wq_plane_bytes[4 + 4 * a : P, col : col + 128],
+                            lhsT=wq_codes[:, word : word + P].bitcast(FP8X4),
+                            lhsT_scale=wq_plane_bytes[4 + 4 * a : P, col : col + P],
                             rhs=x_codes[:, m0 : m0 + CHUNK].bitcast(FP8X4),
                             rhs_scale=x_plane[:, m0 : m0 + CHUNK],
                             start=(a == 0),
                             stop=(a == PASSES - 1),
                         )
                 relu_out(
-                    engines[mc],
-                    qa_bf[:, b, 4 * mc * CHUNK : 4 * (mc + 1) * CHUNK].rearrange("p (n t) -> p n t", t=4),
+                    SCALAR,
+                    qa_bf[:, b, PACK * c * CHUNK : PACK * (c + 1) * CHUNK].rearrange("p (n t) -> p n t", t=PACK),
                     bank[:].rearrange("p t n -> p n t"),
                 )
-            nc.vector.quantize_mx(out=qa_codes[:, b, :].bitcast(FP8X4), scales=qa_plane[:, b, :], in_=qa_bf[:, b, :])
 
-        wv4_code_bytes = wv4_codes[:].bitcast(U8)
-        wv4_plane_bytes = wv4_plane[:].bitcast(U8)
+        def result_tile(engine, width):
+            if engine == VECTOR:
+                return in_turn("result", [P, width], F32)
+            return stage.tile([P, width], F32, name="result", tag="result")
 
-        def values(h, nt, engine):
-            if True:
-                bank = psum.tile([P, HALF], F32, name="bank", tag="bank")
-                cols = slice(nt * P, (nt + 1) * P)
-                nc.tensor.matmul_mx(
-                    out=bank[:],
-                    lhsT=wv8_codes[:, cols].bitcast(FP8X4),
-                    lhsT_scale=wv8_plane[:, cols],
-                    rhs=v_codes[0][h][:].bitcast(FP8X4),
-                    rhs_scale=v_plane_bytes[:, h * HALF : (h + 1) * HALF],
-                    start=True,
-                    stop=False,
-                )
-                nc.tensor.matmul_mx(
-                    out=bank[:],
-                    lhsT=wv4_code_bytes[:, 2 * nt * P : 2 * (nt + 1) * P].bitcast(FP4X4),
-                    lhsT_scale=wv4_plane_bytes[:, cols],
-                    rhs=v_codes[1][h][:].bitcast(FP8X4),
-                    rhs_scale=v_plane_bytes[:, J + h * HALF : J + (h + 1) * HALF],
-                    start=False,
-                    stop=True,
-                )
-                result = stage.tile([P, HALF], F32, name="result", tag="result")
-                if engine == "S":
-                    nc.scalar.activation(out=result[:], in_=bank[:], func=COPY)
-                else:
-                    nc.vector.tensor_copy(out=result[:], in_=bank[:])
-                nc.sync.dma_start(out=out_1[cols, h * HALF : (h + 1) * HALF], in_=result[:])
+        def values(h, tile, wv8_mx, engine):
+            wv8_codes, wv8_plane = wv8_mx
+            rows = slice(tile * P, (tile + 1) * P)
+            bank = new_bank([P, HALF])
+            nc.tensor.matmul_mx(
+                out=bank[:],
+                lhsT=wv8_codes[:, rows].bitcast(FP8X4),
+                lhsT_scale=wv8_plane[:, rows],
+                rhs=v_codes[0, h][:].bitcast(FP8X4),
+                rhs_scale=v_plane_bytes[:, h * HALF : (h + 1) * HALF],
+                start=True,
+                stop=False,
+            )
+            nc.tensor.matmul_mx(
+                out=bank[:],
+                lhsT=wv4_code_bytes[:, 2 * tile * P : 2 * (tile + 1) * P].bitcast(FP4X4),
+                lhsT_scale=wv4_plane_bytes[:, rows],
+                rhs=v_codes[1, h][:].bitcast(FP8X4),
+                rhs_scale=v_plane_bytes[:, J + h * HALF : J + (h + 1) * HALF],
+                start=False,
+                stop=True,
+            )
+            result = result_tile(engine, HALF)
+            if engine == SCALAR:
+                nc.scalar.activation(out=result[:], in_=bank[:], func=COPY)
+            else:
+                nc.vector.tensor_copy(out=result[:], in_=bank[:])
+            nc.sync.dma_start(out=out_1[rows, h * HALF : (h + 1) * HALF], in_=result[:])
 
-        def scores(j0, width, engines):
-            for mt in range(M // P):
-                bank = psum.tile([P, width], F32, name="bank", tag="bank")
-                cols = slice(mt * P, (mt + 1) * P)
-                for b in range(2):
+        def scores(j0, width, qa_mx, engines):
+            for tile in range(M // P):
+                rows = slice(tile * P, (tile + 1) * P)
+                bank = new_bank([P, width])
+                for b in range(PASSES):
+                    qa_codes, qa_plane = qa_mx[b]
+                    ka_codes, ka_plane, first = ka_mx[b, j0]
                     nc.tensor.matmul_mx(
                         out=bank[:],
-                        lhsT=qa_codes[:, b, cols].bitcast(FP8X4),
-                        lhsT_scale=qa_plane[:, b, cols],
-                        rhs=ka_codes[:, b, j0 : j0 + width].bitcast(FP8X4),
-                        rhs_scale=ka_plane[:, b, j0 : j0 + width],
+                        lhsT=qa_codes[:, rows].bitcast(FP8X4),
+                        lhsT_scale=qa_plane[:, rows],
+                        rhs=ka_codes[:, first : first + width].bitcast(FP8X4),
+                        rhs_scale=ka_plane[:, first : first + width],
                         start=(b == 0),
-                        stop=(b == 1),
+                        stop=(b == PASSES - 1),
                     )
-                result = stage.tile([P, width], F32, name="result", tag="result")
-                if engines[mt] == "S":
+                result = result_tile(engines[tile], width)
+                if engines[tile] == SCALAR:
                     nc.scalar.activation(out=result[:], in_=bank[:], func=COPY, scale=SCORE_SCALE)
                 else:
                     nc.vector.tensor_scalar(out=result[:], in0=bank[:], scalar1=SCORE_SCALE, scalar2=None, op0=MULT)
-                nc.sync.dma_start(out=out_0[cols, j0 : j0 + width], in_=result[:])
+                nc.sync.dma_start(out=out_0[rows, j0 : j0 + width], in_=result[:])
 
-        wide_pass(0, 0)
-        wide_pass(1, 0)
-        wide_pass(0, 1, "SSSS")
-        wide_pass(1, 1, "SSSS")
-        reorder_wq_scales()
-        reorder_wq(0)
-        reorder_wq(1)
-        round_x(0,"V")
-        round_x(1,"V")
-        round_wv8("V")
-        quantise_x()
-        quantise_wv8()
-        wide_finish(0)
-        wide_finish(1)
-        keys(4,0,"S")
-        keys(5,0,"S")
-        keys(6,0,"S")
-        keys(7,0,"S")
-        keys(4,1,"S")
-        keys(5,1,"S")
-        keys(6,1,"S")
-        keys(7,1,"S")
-        queries(0,"SS")
-        queries(1,"SV")
-        quantise_keys(0, HALF, 0)
-        quantise_keys(0, HALF, 1)
-        quantise_keys(HALF, HALF, 0)
-        values(0,0,"V")
-        values(0,1,"S")
-        values(1,0,"S")
-        values(1,1,"S")
-        quantise_keys(HALF, HALF, 1)
-        scores(0, HALF, "VV")
-        scores(HALF, 256, "SS")
-        scores(HALF + 256, 256, "VV")
+        wide_keys_open(0)
+        wide_keys_open(1)
+        wide_keys_close(0, (SCALAR, SCALAR, VECTOR, VECTOR))
+        wide_keys_close(1, (SCALAR, VECTOR, SCALAR, SCALAR))
+
+        wv8_bf = in_turn("wv8_bf", [P, N, PACK], BF16)
+        nc.vector.tensor_copy(
+            out=wv8_bf[:].rearrange("p (c u) i -> p c i u", u=4), in_=wv8_raw[:].rearrange("p i (c u) -> p c i u", u=4)
+        )
+        x_bf = in_turn("x_bf", [P, PASSES, M, PACK], BF16)
+        nc.vector.tensor_copy(
+            out=x_bf[:].rearrange("p a (c u) i -> p a c i u", u=4),
+            in_=x_raw[:].rearrange("p a i (c u) -> p a c i u", u=4),
+        )
+        wv8_mx = quantise("wv8", wv8_bf[:].rearrange("p n i -> p (n i)"), N)
+        wq_plane = in_turn("wq_plane", [P, R // 4], I32)
+        reorder(wq_plane[:], wq_scale_rows, 2)
+        wq_codes_0 = in_turn("wq_codes", [P, R], I32)
+        reorder(wq_codes_0[:], wq_raw[:, 0, :], 8)
+        x_mx = quantise("x", x_bf[:].rearrange("p a m i -> p (a m i)"), PASSES * M)
+        wq_codes_1 = in_turn("wq_codes", [P, R], I32)
+        reorder(wq_codes_1[:], wq_raw[:, 1, :], 8)
+        wide_keys_interleave(0)
+        wide_keys_interleave(1)
+
+        for c in range(3):
+            for b in range(PASSES):
+                narrow_keys(c, b)
+        values(0, 0, wv8_mx, SCALAR)
+        values(0, 1, wv8_mx, SCALAR)
+        queries(0, wq_codes_0, wq_plane, x_mx)
+        queries(1, wq_codes_1, wq_plane, x_mx)
+        quantise_keys(0, 0, HALF)
+        qa_mx = [quantise("qa%d" % b, qa_bf[:, b, :], M) for b in range(PASSES)]
+        values(1, 0, wv8_mx, SCALAR)
+        narrow_keys(3, 0)
+        quantise_keys(1, 0, HALF)
+        values(1, 1, wv8_mx, VECTOR)
+        quantise_keys(0, HALF, HALF)
+        quantise_keys(1, HALF, QUARTER)
+        narrow_keys(3, 1)
+        quantise_keys(1, HALF + QUARTER, QUARTER)
+
+        scores(0, HALF, qa_mx, (SCALAR, SCALAR))
+        scores(HALF, QUARTER, qa_mx, (VECTOR, SCALAR))
+        scores(HALF + QUARTER, QUARTER, qa_mx, (VECTOR, SCALAR))

@@ -33,14 +33,16 @@ PASS = P * PACK
 PASSES = K // PASS
 BLOCKS = PASS // 32
 HALF = J // 2
-QUARTER = J // 4
 CHUNK = HALF // PACK
 LIST_GROUP = 16
 QUADRANTS = (0, 2, 1, 3)
+SCALE_ROWS = PASSES * BLOCKS
+FIRST_ROW = P - SCALE_ROWS
+EARLY_COLUMNS = T // 4
 SCORE_SCALE = 0.03125
 SCALAR, VECTOR = "scalar", "vector"
-VECTOR_TILES = 23
-SCALAR_RESULTS = 7
+VECTOR_TILES = 28
+SCALAR_RESULTS = 4
 PSUM_BANKS = 8
 
 
@@ -66,49 +68,76 @@ def tile_list_kvt_qf_act_kernel(
         def quadrant_rows(quad, first=0, count=4):
             return slice(32 * quad + first, 32 * quad + first + count)
 
-        offsets = keep.tile([P, J // LIST_GROUP], U16, name="offsets")
-        tab_scale_rows = held("tab_scale_rows", [P, T // 4], I32)
-        wk_raw = held("wk_raw", [P, PASSES * R // 2], I32)
-        weight_scale_rows = held("weight_scale_rows", [P, PASSES * R // 4], I32)
-        v_plane = held("v_plane", [P, PASSES, J // 4], I32)
-        v_scale_rows = held("v_scale_rows", [P, J], U8)
-        tab_win = [held("tab_win%d" % a, [P, T], I32) for a in range(PASSES)]
-
-        def load_table(a):
-            nc.sync.dma_start(out=tab_win[a][:], in_=tab_words[a].rearrange("p t i -> p (t i)").bitcast(I32))
-
-        def move_table_scales(a):
-            for quad in QUADRANTS:
-                row = BLOCKS * a + 4 * quad
-                nc.sync.dma_start(
-                    out=v_plane[quadrant_rows(quad), a, :], in_=v_scale_rows[row : row + 4, :].bitcast(I32)
-                )
-
-        nc.vector.memset(weight_scale_rows[:], 0)
-        nc.vector.memset(tab_scale_rows[32:64, :], 0)
-        nc.vector.memset(tab_scale_rows[64:128, :], 0)
-        nc.vector.memset(v_plane[:], 0)
-
-        nc.sync.dma_start(offsets[:], offs)
-        nc.sync.dma_start(out=tab_scale_rows[0:32, :], in_=tab_scales.rearrange("a q t -> (a q) t").bitcast(I32))
-        nc.sync.dma_start(
-            out=wk_raw[:].rearrange("p (a w) -> p a w", a=PASSES), in_=wk_words.rearrange("a p n -> p a n").bitcast(I32)
-        )
-        for quad in QUADRANTS:
-            nc.sync.dma_start(
-                out=weight_scale_rows[quadrant_rows(quad), :].rearrange("p (a w) -> p a w", a=PASSES),
-                in_=wk_scales[:, 4 * quad : 4 * quad + 4, :].rearrange("a r n -> r a n").bitcast(I32),
-            )
-        load_table(0)
-        nc.vector.tensor_copy(out=v_scale_rows[:], in_=tab_scale_rows[:].bitcast(U8).indirect(offsets[:]))
-        move_table_scales(0)
-        load_table(1)
-        move_table_scales(1)
-
         def reorder(dst, src, run):
             nc.vector.tensor_copy(
                 out=dst.rearrange("p (g t q u) -> p g t q u", t=PACK, q=BLOCKS, u=run),
                 in_=src.rearrange("p (g q t u) -> p g t q u", t=PACK, q=BLOCKS, u=run),
+            )
+
+        v_cols = slice(0, J // 4)
+        wk_cols = slice(v_cols.stop, v_cols.stop + R // 4)
+        wv4_cols = slice(wk_cols.stop, wk_cols.stop + N // 4)
+        plane_width = (wk_cols.stop, wv4_cols.stop)
+
+        offsets = keep.tile([P, J // LIST_GROUP], U16, name="offsets")
+        tab_scale_rows = held("tab_scale_rows", [P, T // 4], I32)
+        wk_scale_rows = held("wk_scale_rows", [P, R // 4], I32)
+        v_scale_rows = held("v_scale_rows", [P, J], U8)
+        staged_rows = held("staged_rows", [P, wv4_cols.stop], I32)
+        planes = [held("planes%d" % a, [P, plane_width[a]], I32) for a in range(PASSES)]
+        wq_scale_rows = held("wq_scale_rows", [P, R // 4], I32)
+        wk_raw = [held("wk_raw%d" % a, [P, R // 2], I32) for a in range(PASSES)]
+        staged = slice(FIRST_ROW, P)
+        tab_win = [held("tab_win%d" % a, [P, T], I32) for a in range(PASSES)]
+
+        def load_table(a, columns):
+            words = tab_words[a].rearrange("p t i -> p (t i)").bitcast(I32)
+            nc.sync.dma_start(out=tab_win[a][:, columns], in_=words[:, columns])
+
+        def move_to_planes(a):
+            for quad in QUADRANTS:
+                row = FIRST_ROW + BLOCKS * a + 4 * quad
+                nc.sync.dma_start(
+                    out=planes[a][quadrant_rows(quad), :], in_=staged_rows[row : row + 4, 0 : plane_width[a]]
+                )
+
+        nc.vector.memset(tab_scale_rows[0:FIRST_ROW, :], 0)
+        for a in range(PASSES):
+            nc.gpsimd.memset(planes[a][:], 0)
+        nc.gpsimd.memset(wq_scale_rows[:], 0)
+
+        nc.sync.dma_start(out=wk_scale_rows[staged, :], in_=wk_scales.rearrange("a q r -> (a q) r").bitcast(I32))
+        nc.sync.dma_start(offsets[:], offs)
+        nc.sync.dma_start(out=tab_scale_rows[staged, :], in_=tab_scales.rearrange("a q t -> (a q) t").bitcast(I32))
+        load_table(0, slice(0, T))
+        nc.sync.dma_start(out=wk_raw[0][:], in_=wk_words[0].bitcast(I32))
+        nc.sync.dma_start(out=staged_rows[FIRST_ROW + BLOCKS : P, wv4_cols], in_=wv4_scales[0].bitcast(I32))
+        load_table(1, slice(0, EARLY_COLUMNS))
+        reorder(staged_rows[staged, wk_cols], wk_scale_rows[staged, :], 2)
+        nc.vector.tensor_copy(out=v_scale_rows[:], in_=tab_scale_rows[:].bitcast(U8).indirect(offsets[:]))
+        nc.vector.tensor_copy(out=staged_rows[staged, v_cols], in_=v_scale_rows[staged, :].bitcast(I32))
+        move_to_planes(0)
+        load_table(1, slice(EARLY_COLUMNS, T))
+        nc.sync.dma_start(out=wk_raw[1][:], in_=wk_words[1].bitcast(I32))
+        move_to_planes(1)
+
+        x_raw = held("x_raw", [P, PASSES, PACK, M], F32)
+        wq_raw = [held("wq_raw%d" % b, [P, PASSES, PASS], I32) for b in range(PASSES)]
+        wv8_raw = held("wv8_raw", [P, PACK, N], F32)
+        wv4_codes = held("wv4_codes", [P, N // 2], I32)
+
+        nc.sync.dma_start(out=wv8_raw[:], in_=wv8.rearrange("(p i) n -> p i n", i=PACK))
+        nc.sync.dma_start(out=x_raw[:], in_=x.rearrange("(a p i) m -> p a i m", a=PASSES, i=PACK))
+        nc.sync.dma_start(out=wv4_codes[:], in_=wv4_words[0].bitcast(I32))
+        for quad in QUADRANTS:
+            nc.sync.dma_start(
+                out=wq_scale_rows[quadrant_rows(quad, count=8), :],
+                in_=wq_scales[:, 4 * quad : 4 * quad + 4, :].bitcast(I32),
+            )
+        for b in range(PASSES):
+            nc.sync.dma_start(
+                out=wq_raw[b][:],
+                in_=wq_words[:, :, b * PASS : (b + 1) * PASS, :].rearrange("a p r i -> p a (r i)").bitcast(I32),
             )
 
         v_codes = {}
@@ -121,50 +150,18 @@ def tile_list_kvt_qf_act_kernel(
                 in_=tab_win[a][:].bitcast(U32).indirect(offsets[:, columns * h : columns * (h + 1)]),
             )
 
-        wk_plane = held("wk_plane", [P, PASSES * R // 4], I32)
-        wk_codes = held("wk_codes", [P, PASSES * R // 2], I32)
-        reorder(wk_plane[:], weight_scale_rows[:], 2)
-        reorder(wk_codes[:], wk_raw[:], 4)
-        gather_words(0, 0)
-        gather_words(0, 1)
+        wk_codes = {}
 
-        wq_scale_rows = weight_scale_rows[:, 0 : R // 4]
-        wv4_plane = weight_scale_rows[:, R // 4 : R // 4 + N // 4]
-        x_raw = held("x_raw", [P, PASSES, PACK, M], F32)
-        wq_raw = held("wq_raw", [P, PASSES, R], I32)
-        wv8_raw = held("wv8_raw", [P, PACK, N], F32)
-        wv4_codes = held("wv4_codes", [P, N // 2], I32)
+        def reorder_wk(a):
+            wk_codes[a] = in_turn("wk_codes", [P, R // 2], I32)
+            reorder(wk_codes[a][:], wk_raw[a][:], 4)
 
-        def load_wq(b):
-            nc.sync.dma_start(
-                out=wq_raw[:, b, :].rearrange("p (a w) -> p a w", a=PASSES),
-                in_=wq_words[:, :, b * PASS : (b + 1) * PASS, :].rearrange("a p r i -> p a (r i)").bitcast(I32),
-            )
+        def plane_bytes(a, cols, first, width):
+            return planes[a][:].bitcast(U8)[:, 4 * cols.start + first : 4 * cols.start + first + width]
 
-        nc.sync.dma_start(out=wv8_raw[:], in_=wv8.rearrange("(p i) n -> p i n", i=PACK))
-        nc.sync.dma_start(out=wv4_codes[:], in_=wv4_words[0].bitcast(I32))
-        nc.sync.dma_start(out=x_raw[:], in_=x.rearrange("(a p i) m -> p a i m", a=PASSES, i=PACK))
-        for quad in QUADRANTS:
-            nc.sync.dma_start(
-                out=wv4_plane[quadrant_rows(quad), :], in_=wv4_scales[0, 4 * quad : 4 * quad + 4, :].bitcast(I32)
-            )
-        load_wq(0)
-        for quad in QUADRANTS:
-            nc.sync.dma_start(
-                out=wq_scale_rows[quadrant_rows(quad, first=4, count=8), :],
-                in_=wq_scales[:, 4 * quad : 4 * quad + 4, :].bitcast(I32),
-            )
-        load_wq(1)
-        gather_words(1, 0)
-        gather_words(1, 1)
-
-        v_plane_bytes = v_plane[:].rearrange("p a w -> p (a w)").bitcast(U8)
-        wk_plane_bytes = wk_plane[:].bitcast(U8)
-        wk_code_bytes = wk_codes[:].bitcast(U8)
-        wv4_plane_bytes = wv4_plane.bitcast(U8)
-        wv4_code_bytes = wv4_codes[:].bitcast(U8)
-
-        def relu_out(engine, out, in_):
+        def relu_out(engine, out, bank):
+            out = out.rearrange("p (n t) -> p n t", t=PACK)
+            in_ = bank[:].rearrange("p t n -> p n t")
             if engine == SCALAR:
                 nc.scalar.activation(out=out, in_=in_, func=RELU)
             else:
@@ -176,65 +173,38 @@ def tile_list_kvt_qf_act_kernel(
             nc.vector.quantize_mx(out=codes[:].bitcast(FP8X4), scales=plane[:], in_=values)
             return codes, plane
 
-        def key_matmul(out, a, b, t, j0, width):
-            h, first = divmod(j0, HALF)
-            col = a * R + b * PASS + t * P
-            nc.tensor.matmul_mx(
-                out=out,
-                lhsT=wk_code_bytes[:, 2 * col : 2 * (col + P)].bitcast(FP4X4),
-                lhsT_scale=wk_plane_bytes[:, col : col + P],
-                rhs=v_codes[a, h][:, first : first + width].bitcast(FP8X4),
-                rhs_scale=v_plane_bytes[:, a * J + j0 : a * J + j0 + width],
-                start=(a == 0),
-                stop=(a == PASSES - 1),
-            )
-
-        wide_banks = {}
-        ka_planar = held("ka_planar", [P, PASSES, PACK, HALF], BF16)
-        ka_wide = {}
-
-        def wide_keys_open(b):
+        def key_pass(bank, a, c, b):
+            h, first = divmod(c * CHUNK, HALF)
             for t in range(PACK):
-                wide_banks[b, t] = new_bank([P, HALF])
-                key_matmul(wide_banks[b, t][:], 0, b, t, 0, HALF)
+                col = b * PASS + t * P
+                nc.tensor.matmul_mx(
+                    out=bank[:, t, :],
+                    lhsT=wk_codes[a][:].bitcast(U8)[:, 2 * col : 2 * (col + P)].bitcast(FP4X4),
+                    lhsT_scale=plane_bytes(a, wk_cols, col, P),
+                    rhs=v_codes[a, h][:, first : first + CHUNK].bitcast(FP8X4),
+                    rhs_scale=plane_bytes(a, v_cols, c * CHUNK, CHUNK),
+                    start=(a == 0 and t == 0),
+                    stop=(a == PASSES - 1 and t == PACK - 1),
+                )
 
-        def wide_keys_close(b, engines):
-            for t in range(PACK):
-                key_matmul(wide_banks[b, t][:], 1, b, t, 0, HALF)
-                relu_out(engines[t], ka_planar[:, b, t, :], wide_banks[b, t][:])
+        ka_bf = [held("ka_bf%d" % b, [P, J * PACK], BF16) for b in range(PASSES)]
 
-        def wide_keys_interleave(b):
-            ka_wide[b] = in_turn("ka_wide", [P, HALF * PACK], BF16)
-            nc.vector.tensor_copy(
-                out=ka_wide[b][:].rearrange("p (c u t) -> p c t u", u=4, t=PACK),
-                in_=ka_planar[:, b].rearrange("p t (c u) -> p c t u", u=4),
-            )
+        def keys_out(bank, c, b, engine):
+            relu_out(engine, ka_bf[b][:, PACK * c * CHUNK : PACK * (c + 1) * CHUNK], bank)
 
-        ka_narrow = held("ka_narrow", [P, PASSES, HALF * PACK], BF16)
-
-        def narrow_keys(c, b):
-            bank = new_bank([P, PACK, CHUNK])
-            for t in range(PACK):
+        def keys(c):
+            for b in range(PASSES):
+                bank = new_bank([P, PACK, CHUNK])
                 for a in range(PASSES):
-                    key_matmul(bank[:, t, :], a, b, t, HALF + c * CHUNK, CHUNK)
-            relu_out(
-                SCALAR,
-                ka_narrow[:, b, PACK * c * CHUNK : PACK * (c + 1) * CHUNK].rearrange("p (n t) -> p n t", t=PACK),
-                bank[:].rearrange("p t n -> p n t"),
-            )
+                    key_pass(bank, a, c, b)
+                keys_out(bank, c, b, SCALAR)
 
         ka_mx = {}
 
         def quantise_keys(b, j0, width):
-            if j0 < HALF:
-                values = ka_wide[b][:]
-            else:
-                values = ka_narrow[:, b, PACK * (j0 - HALF) : PACK * (j0 - HALF + width)]
-            codes, plane = quantise("ka%d_%d" % (b, j0), values, width)
-            for first in range(0, width, QUARTER):
-                ka_mx[b, j0 + first] = (codes, plane, first)
+            ka_mx[b, j0] = quantise("ka%d_%d" % (b, j0), ka_bf[b][:, PACK * j0 : PACK * (j0 + width)], width)
 
-        qa_bf = held("qa_bf", [P, PASSES, M * PACK], BF16)
+        qa_bf = [held("qa_bf%d" % b, [P, M * PACK], BF16) for b in range(PASSES)]
 
         def queries(b, wq_codes, wq_plane, x_mx):
             x_codes, x_plane = x_mx
@@ -249,22 +219,18 @@ def tile_list_kvt_qf_act_kernel(
                         nc.tensor.matmul_mx(
                             out=bank[:, t, :],
                             lhsT=wq_codes[:, word : word + P].bitcast(FP8X4),
-                            lhsT_scale=wq_plane_bytes[4 + 4 * a : P, col : col + P],
+                            lhsT_scale=wq_plane_bytes[4 * a : P, col : col + P],
                             rhs=x_codes[:, m0 : m0 + CHUNK].bitcast(FP8X4),
                             rhs_scale=x_plane[:, m0 : m0 + CHUNK],
                             start=(a == 0),
                             stop=(a == PASSES - 1),
                         )
-                relu_out(
-                    SCALAR,
-                    qa_bf[:, b, PACK * c * CHUNK : PACK * (c + 1) * CHUNK].rearrange("p (n t) -> p n t", t=PACK),
-                    bank[:].rearrange("p t n -> p n t"),
-                )
+                relu_out(SCALAR, qa_bf[b][:, PACK * c * CHUNK : PACK * (c + 1) * CHUNK], bank)
 
-        def result_tile(engine, width):
+        def result_tile(engine, shape):
             if engine == VECTOR:
-                return in_turn("result", [P, width], F32)
-            return stage.tile([P, width], F32, name="result", tag="result")
+                return in_turn("result", shape, F32)
+            return stage.tile(shape, F32, name="result", tag="result")
 
         def values(h, tile, wv8_mx, engine):
             wv8_codes, wv8_plane = wv8_mx
@@ -275,92 +241,105 @@ def tile_list_kvt_qf_act_kernel(
                 lhsT=wv8_codes[:, rows].bitcast(FP8X4),
                 lhsT_scale=wv8_plane[:, rows],
                 rhs=v_codes[0, h][:].bitcast(FP8X4),
-                rhs_scale=v_plane_bytes[:, h * HALF : (h + 1) * HALF],
+                rhs_scale=plane_bytes(0, v_cols, h * HALF, HALF),
                 start=True,
                 stop=False,
             )
             nc.tensor.matmul_mx(
                 out=bank[:],
-                lhsT=wv4_code_bytes[:, 2 * tile * P : 2 * (tile + 1) * P].bitcast(FP4X4),
-                lhsT_scale=wv4_plane_bytes[:, rows],
+                lhsT=wv4_codes[:].bitcast(U8)[:, 2 * tile * P : 2 * (tile + 1) * P].bitcast(FP4X4),
+                lhsT_scale=plane_bytes(1, wv4_cols, tile * P, P),
                 rhs=v_codes[1, h][:].bitcast(FP8X4),
-                rhs_scale=v_plane_bytes[:, J + h * HALF : J + (h + 1) * HALF],
+                rhs_scale=plane_bytes(1, v_cols, h * HALF, HALF),
                 start=False,
                 stop=True,
             )
-            result = result_tile(engine, HALF)
+            result = result_tile(engine, [P, HALF])
             if engine == SCALAR:
                 nc.scalar.activation(out=result[:], in_=bank[:], func=COPY)
             else:
                 nc.vector.tensor_copy(out=result[:], in_=bank[:])
             nc.sync.dma_start(out=out_1[rows, h * HALF : (h + 1) * HALF], in_=result[:])
 
-        def scores(j0, width, qa_mx, engines):
-            for tile in range(M // P):
+        def scores(j0, width, tiles, qa_mx, engine):
+            bank = new_bank([P, len(tiles), width])
+            for place, tile in enumerate(tiles):
                 rows = slice(tile * P, (tile + 1) * P)
-                bank = new_bank([P, width])
                 for b in range(PASSES):
                     qa_codes, qa_plane = qa_mx[b]
-                    ka_codes, ka_plane, first = ka_mx[b, j0]
+                    ka_codes, ka_plane = ka_mx[b, j0]
                     nc.tensor.matmul_mx(
-                        out=bank[:],
+                        out=bank[:, place, :],
                         lhsT=qa_codes[:, rows].bitcast(FP8X4),
                         lhsT_scale=qa_plane[:, rows],
-                        rhs=ka_codes[:, first : first + width].bitcast(FP8X4),
-                        rhs_scale=ka_plane[:, first : first + width],
+                        rhs=ka_codes[:].bitcast(FP8X4),
+                        rhs_scale=ka_plane[:],
                         start=(b == 0),
                         stop=(b == PASSES - 1),
                     )
-                result = result_tile(engines[tile], width)
-                if engines[tile] == SCALAR:
-                    nc.scalar.activation(out=result[:], in_=bank[:], func=COPY, scale=SCORE_SCALE)
-                else:
-                    nc.vector.tensor_scalar(out=result[:], in0=bank[:], scalar1=SCORE_SCALE, scalar2=None, op0=MULT)
-                nc.sync.dma_start(out=out_0[rows, j0 : j0 + width], in_=result[:])
+            result = result_tile(engine, [P, len(tiles), width])
+            if engine == SCALAR:
+                nc.scalar.activation(out=result[:], in_=bank[:], func=COPY, scale=SCORE_SCALE)
+            else:
+                nc.vector.tensor_scalar(out=result[:], in0=bank[:], scalar1=SCORE_SCALE, scalar2=None, op0=MULT)
+            nc.sync.dma_start(
+                out=out_0.rearrange("(i p) j -> p i j", p=P)[:, tiles[0] : tiles[-1] + 1, j0 : j0 + width],
+                in_=result[:],
+            )
 
-        wide_keys_open(0)
-        wide_keys_open(1)
-        wide_keys_close(0, (SCALAR, SCALAR, VECTOR, VECTOR))
-        wide_keys_close(1, (SCALAR, VECTOR, SCALAR, SCALAR))
+        first_groups = [(c, b) for b in range(PASSES) for c in range(PACK)]
+        gather_words(0, 0)
+        reorder_wk(0)
+        open_banks = {}
+        for c, b in first_groups:
+            open_banks[c, b] = new_bank([P, PACK, CHUNK])
+            key_pass(open_banks[c, b], 0, c, b)
+        gather_words(0, 1)
+        gather_words(1, 0)
+        reorder_wk(1)
+        gather_words(1, 1)
+        for c, b in first_groups:
+            key_pass(open_banks[c, b], 1, c, b)
+            keys_out(open_banks[c, b], c, b, VECTOR if (c, b) in ((3, 0), (1, 1)) else SCALAR)
 
         wv8_bf = in_turn("wv8_bf", [P, N, PACK], BF16)
         nc.vector.tensor_copy(
             out=wv8_bf[:].rearrange("p (c u) i -> p c i u", u=4), in_=wv8_raw[:].rearrange("p i (c u) -> p c i u", u=4)
         )
+        keys(4)
+        wv8_mx = quantise("wv8", wv8_bf[:].rearrange("p n i -> p (n i)"), N)
         x_bf = in_turn("x_bf", [P, PASSES, M, PACK], BF16)
         nc.vector.tensor_copy(
             out=x_bf[:].rearrange("p a (c u) i -> p a c i u", u=4),
             in_=x_raw[:].rearrange("p a i (c u) -> p a c i u", u=4),
         )
-        wv8_mx = quantise("wv8", wv8_bf[:].rearrange("p n i -> p (n i)"), N)
+        keys(5)
         wq_plane = in_turn("wq_plane", [P, R // 4], I32)
-        reorder(wq_plane[:], wq_scale_rows, 2)
-        wq_codes_0 = in_turn("wq_codes", [P, R], I32)
-        reorder(wq_codes_0[:], wq_raw[:, 0, :], 8)
+        reorder(wq_plane[:], wq_scale_rows[:], 2)
         x_mx = quantise("x", x_bf[:].rearrange("p a m i -> p (a m i)"), PASSES * M)
-        wq_codes_1 = in_turn("wq_codes", [P, R], I32)
-        reorder(wq_codes_1[:], wq_raw[:, 1, :], 8)
-        wide_keys_interleave(0)
-        wide_keys_interleave(1)
-
-        for c in range(3):
-            for b in range(PASSES):
-                narrow_keys(c, b)
+        wq_codes = []
+        for b in range(PASSES):
+            wq_codes.append(in_turn("wq_codes", [P, R], I32))
+            reorder(wq_codes[b][:], wq_raw[b][:].rearrange("p a w -> p (a w)"), 8)
         values(0, 0, wv8_mx, SCALAR)
         values(0, 1, wv8_mx, SCALAR)
-        queries(0, wq_codes_0, wq_plane, x_mx)
-        queries(1, wq_codes_1, wq_plane, x_mx)
-        quantise_keys(0, 0, HALF)
-        qa_mx = [quantise("qa%d" % b, qa_bf[:, b, :], M) for b in range(PASSES)]
-        values(1, 0, wv8_mx, SCALAR)
-        narrow_keys(3, 0)
-        quantise_keys(1, 0, HALF)
-        values(1, 1, wv8_mx, VECTOR)
-        quantise_keys(0, HALF, HALF)
-        quantise_keys(1, HALF, QUARTER)
-        narrow_keys(3, 1)
-        quantise_keys(1, HALF + QUARTER, QUARTER)
-
-        scores(0, HALF, qa_mx, (SCALAR, SCALAR))
-        scores(HALF, QUARTER, qa_mx, (VECTOR, SCALAR))
-        scores(HALF + QUARTER, QUARTER, qa_mx, (VECTOR, SCALAR))
+        for b in range(PASSES):
+            quantise_keys(b, 0, HALF)
+        for b in range(PASSES):
+            queries(b, wq_codes[b], wq_plane, x_mx)
+        for b in range(PASSES):
+            quantise_keys(b, HALF, 2 * CHUNK)
+        qa_mx = [quantise("qa%d" % b, qa_bf[b][:], M) for b in range(PASSES)]
+        values(1, 0, wv8_mx, VECTOR)
+        keys(6)
+        scores(0, HALF, (0,), qa_mx, VECTOR)
+        scores(0, HALF, (1,), qa_mx, VECTOR)
+        keys(7)
+        for b in range(PASSES):
+            quantise_keys(b, 6 * CHUNK, CHUNK)
+        scores(HALF, 2 * CHUNK, (0, 1), qa_mx, SCALAR)
+        for b in range(PASSES):
+            quantise_keys(b, 7 * CHUNK, CHUNK)
+        scores(6 * CHUNK, CHUNK, (0, 1), qa_mx, VECTOR)
+        values(1, 1, wv8_mx, SCALAR)
+        scores(7 * CHUNK, CHUNK, (0, 1), qa_mx, VECTOR)

@@ -26,6 +26,7 @@ FP4X4 = mybir.dt.float4_e2m1fn_x4
 RELU = mybir.ActivationFunctionType.Relu
 COPY = mybir.ActivationFunctionType.Copy
 MULT = mybir.AluOpType.mult
+ADD = mybir.AluOpType.add
 
 P = 128
 PACK = 4
@@ -38,11 +39,10 @@ LIST_GROUP = 16
 QUADRANTS = (0, 2, 1, 3)
 SCALE_ROWS = PASSES * BLOCKS
 FIRST_ROW = P - SCALE_ROWS
-EARLY_COLUMNS = T // 4
 SCORE_SCALE = 0.03125
 SCALAR, VECTOR = "scalar", "vector"
-VECTOR_TILES = 28
-SCALAR_RESULTS = 4
+VECTOR_TILES = 24
+SCALAR_RESULTS = 7
 PSUM_BANKS = 8
 
 
@@ -68,8 +68,8 @@ def tile_list_kvt_qf_act_kernel(
         def quadrant_rows(quad, first=0, count=4):
             return slice(32 * quad + first, 32 * quad + first + count)
 
-        def reorder(dst, src, run):
-            nc.vector.tensor_copy(
+        def reorder(dst, src, run, engine=nc.vector):
+            engine.tensor_copy(
                 out=dst.rearrange("p (g t q u) -> p g t q u", t=PACK, q=BLOCKS, u=run),
                 in_=src.rearrange("p (g q t u) -> p g t q u", t=PACK, q=BLOCKS, u=run),
             )
@@ -86,13 +86,14 @@ def tile_list_kvt_qf_act_kernel(
         staged_rows = held("staged_rows", [P, wv4_cols.stop], I32)
         planes = [held("planes%d" % a, [P, plane_width[a]], I32) for a in range(PASSES)]
         wq_scale_rows = held("wq_scale_rows", [P, R // 4], I32)
-        wk_raw = [held("wk_raw%d" % a, [P, R // 2], I32) for a in range(PASSES)]
+        wk_group0 = [held("wk_group0_%d" % a, [P, PASS // 2], I32) for a in range(PASSES)]
+        wk_group1 = held("wk_group1", [P, PASSES, PASS // 2], I32)
+        wk_dram = wk_words.rearrange("a p (b n) -> b p a n", b=PASSES).bitcast(I32)
         staged = slice(FIRST_ROW, P)
         tab_win = [held("tab_win%d" % a, [P, T], I32) for a in range(PASSES)]
 
-        def load_table(a, columns):
-            words = tab_words[a].rearrange("p t i -> p (t i)").bitcast(I32)
-            nc.sync.dma_start(out=tab_win[a][:, columns], in_=words[:, columns])
+        def load_table(a):
+            nc.sync.dma_start(out=tab_win[a][:], in_=tab_words[a].rearrange("p t i -> p (t i)").bitcast(I32))
 
         def move_to_planes(a):
             for quad in QUADRANTS:
@@ -106,19 +107,19 @@ def tile_list_kvt_qf_act_kernel(
             nc.gpsimd.memset(planes[a][:], 0)
         nc.gpsimd.memset(wq_scale_rows[:], 0)
 
-        nc.sync.dma_start(out=wk_scale_rows[staged, :], in_=wk_scales.rearrange("a q r -> (a q) r").bitcast(I32))
         nc.sync.dma_start(offsets[:], offs)
         nc.sync.dma_start(out=tab_scale_rows[staged, :], in_=tab_scales.rearrange("a q t -> (a q) t").bitcast(I32))
-        load_table(0, slice(0, T))
-        nc.sync.dma_start(out=wk_raw[0][:], in_=wk_words[0].bitcast(I32))
+        nc.sync.dma_start(out=wk_scale_rows[staged, :], in_=wk_scales.rearrange("a q r -> (a q) r").bitcast(I32))
+        nc.sync.dma_start(out=wk_group0[0][:], in_=wk_dram[0][:, 0, :])
+        load_table(0)
+        nc.sync.dma_start(out=wk_group1[:], in_=wk_dram[1])
         nc.sync.dma_start(out=staged_rows[FIRST_ROW + BLOCKS : P, wv4_cols], in_=wv4_scales[0].bitcast(I32))
-        load_table(1, slice(0, EARLY_COLUMNS))
-        reorder(staged_rows[staged, wk_cols], wk_scale_rows[staged, :], 2)
+        reorder(staged_rows[staged, wk_cols], wk_scale_rows[staged, :], 2, nc.gpsimd)
         nc.vector.tensor_copy(out=v_scale_rows[:], in_=tab_scale_rows[:].bitcast(U8).indirect(offsets[:]))
         nc.vector.tensor_copy(out=staged_rows[staged, v_cols], in_=v_scale_rows[staged, :].bitcast(I32))
         move_to_planes(0)
-        load_table(1, slice(EARLY_COLUMNS, T))
-        nc.sync.dma_start(out=wk_raw[1][:], in_=wk_words[1].bitcast(I32))
+        load_table(1)
+        nc.sync.dma_start(out=wk_group0[1][:], in_=wk_dram[0][:, 1, :])
         move_to_planes(1)
 
         x_raw = held("x_raw", [P, PASSES, PACK, M], F32)
@@ -152,9 +153,16 @@ def tile_list_kvt_qf_act_kernel(
 
         wk_codes = {}
 
-        def reorder_wk(a):
-            wk_codes[a] = in_turn("wk_codes", [P, R // 2], I32)
-            reorder(wk_codes[a][:], wk_raw[a][:], 4)
+        def reorder_wk_group0(a):
+            codes = in_turn("wk_codes", [P, PASS // 2], I32)
+            reorder(codes[:], wk_group0[a][:], 4)
+            wk_codes[a, 0] = codes[:]
+
+        def reorder_wk_group1():
+            codes = in_turn("wk_codes", [P, PASSES, PASS // 2], I32)
+            reorder(codes[:].rearrange("p a w -> p (a w)"), wk_group1[:].rearrange("p a w -> p (a w)"), 4)
+            for a in range(PASSES):
+                wk_codes[a, 1] = codes[:, a, :]
 
         def plane_bytes(a, cols, first, width):
             return planes[a][:].bitcast(U8)[:, 4 * cols.start + first : 4 * cols.start + first + width]
@@ -173,36 +181,47 @@ def tile_list_kvt_qf_act_kernel(
             nc.vector.quantize_mx(out=codes[:].bitcast(FP8X4), scales=plane[:], in_=values)
             return codes, plane
 
-        def key_pass(bank, a, c, b):
+        def key_pass(bank, a, c, b, opens, closes):
             h, first = divmod(c * CHUNK, HALF)
             for t in range(PACK):
                 col = b * PASS + t * P
                 nc.tensor.matmul_mx(
                     out=bank[:, t, :],
-                    lhsT=wk_codes[a][:].bitcast(U8)[:, 2 * col : 2 * (col + P)].bitcast(FP4X4),
+                    lhsT=wk_codes[a, b].bitcast(U8)[:, 2 * t * P : 2 * (t + 1) * P].bitcast(FP4X4),
                     lhsT_scale=plane_bytes(a, wk_cols, col, P),
                     rhs=v_codes[a, h][:, first : first + CHUNK].bitcast(FP8X4),
                     rhs_scale=plane_bytes(a, v_cols, c * CHUNK, CHUNK),
-                    start=(a == 0 and t == 0),
-                    stop=(a == PASSES - 1 and t == PACK - 1),
+                    start=(opens and t == 0),
+                    stop=(closes and t == PACK - 1),
                 )
 
-        ka_bf = [held("ka_bf%d" % b, [P, J * PACK], BF16) for b in range(PASSES)]
+        ka_bf = {}
+
+        def chunk_columns(c):
+            return slice(PACK * CHUNK * (c % PACK), PACK * CHUNK * (c % PACK + 1))
 
         def keys_out(bank, c, b, engine):
-            relu_out(engine, ka_bf[b][:, PACK * c * CHUNK : PACK * (c + 1) * CHUNK], bank)
+            if (c // PACK, b) not in ka_bf:
+                ka_bf[c // PACK, b] = held("ka_bf%d%d" % (c // PACK, b), [P, HALF * PACK], BF16)
+            relu_out(engine, ka_bf[c // PACK, b][:, chunk_columns(c)], bank)
 
-        def keys(c):
-            for b in range(PASSES):
-                bank = new_bank([P, PACK, CHUNK])
-                for a in range(PASSES):
-                    key_pass(bank, a, c, b)
-                keys_out(bank, c, b, SCALAR)
+        def keys(c, b):
+            bank = new_bank([P, PACK, CHUNK])
+            key_pass(bank, 0, c, b, True, False)
+            key_pass(bank, 1, c, b, False, True)
+            keys_out(bank, c, b, SCALAR)
 
         ka_mx = {}
 
-        def quantise_keys(b, j0, width):
-            ka_mx[b, j0] = quantise("ka%d_%d" % (b, j0), ka_bf[b][:, PACK * j0 : PACK * (j0 + width)], width)
+        def quantise_keys(h, b, first, width):
+            if (h, b) not in ka_mx:
+                ka_mx[h, b] = (in_turn("ka_codes", [P, HALF], U32), held("ka_plane%d%d" % (h, b), [P, HALF], U8))
+            codes, plane = ka_mx[h, b]
+            nc.vector.quantize_mx(
+                out=codes[:, first : first + width].bitcast(FP8X4),
+                scales=plane[:, first : first + width],
+                in_=ka_bf[h, b][:, PACK * first : PACK * (first + width)],
+            )
 
         qa_bf = [held("qa_bf%d" % b, [P, M * PACK], BF16) for b in range(PASSES)]
 
@@ -261,85 +280,105 @@ def tile_list_kvt_qf_act_kernel(
                 nc.vector.tensor_copy(out=result[:], in_=bank[:])
             nc.sync.dma_start(out=out_1[rows, h * HALF : (h + 1) * HALF], in_=result[:])
 
-        def scores(j0, width, tiles, qa_mx, engine):
-            bank = new_bank([P, len(tiles), width])
-            for place, tile in enumerate(tiles):
-                rows = slice(tile * P, (tile + 1) * P)
-                for b in range(PASSES):
-                    qa_codes, qa_plane = qa_mx[b]
-                    ka_codes, ka_plane = ka_mx[b, j0]
-                    nc.tensor.matmul_mx(
-                        out=bank[:, place, :],
-                        lhsT=qa_codes[:, rows].bitcast(FP8X4),
-                        lhsT_scale=qa_plane[:, rows],
-                        rhs=ka_codes[:].bitcast(FP8X4),
-                        rhs_scale=ka_plane[:],
-                        start=(b == 0),
-                        stop=(b == PASSES - 1),
-                    )
-            result = result_tile(engine, [P, len(tiles), width])
+        def scores(h, tile, first, width, qa_mx, engine):
+            rows = slice(tile * P, (tile + 1) * P)
+            columns = slice(first, first + width)
+            bank = new_bank([P, width])
+            for b in range(PASSES):
+                qa_codes, qa_plane = qa_mx[b]
+                ka_codes, ka_plane = ka_mx[h, b]
+                nc.tensor.matmul_mx(
+                    out=bank[:],
+                    lhsT=qa_codes[:, rows].bitcast(FP8X4),
+                    lhsT_scale=qa_plane[:, rows],
+                    rhs=ka_codes[:, columns].bitcast(FP8X4),
+                    rhs_scale=ka_plane[:, columns],
+                    start=(b == 0),
+                    stop=(b == PASSES - 1),
+                )
+            result = result_tile(engine, [P, width])
             if engine == SCALAR:
                 nc.scalar.activation(out=result[:], in_=bank[:], func=COPY, scale=SCORE_SCALE)
             else:
                 nc.vector.tensor_scalar(out=result[:], in0=bank[:], scalar1=SCORE_SCALE, scalar2=None, op0=MULT)
-            nc.sync.dma_start(
-                out=out_0.rearrange("(i p) j -> p i j", p=P)[:, tiles[0] : tiles[-1] + 1, j0 : j0 + width],
-                in_=result[:],
-            )
+            nc.sync.dma_start(out=out_0[rows, h * HALF + first : h * HALF + first + width], in_=result[:])
 
-        first_groups = [(c, b) for b in range(PASSES) for c in range(PACK)]
+        first_half, second_half = range(PACK), range(PACK, 2 * PACK)
+        open_groups = [(c, 1) for c in first_half] + [(c, 0) for c in second_half]
+        reorder_wk_group0(0)
         gather_words(0, 0)
-        reorder_wk(0)
-        open_banks = {}
-        for c, b in first_groups:
-            open_banks[c, b] = new_bank([P, PACK, CHUNK])
-            key_pass(open_banks[c, b], 0, c, b)
+        reorder_wk_group1()
+        pass0_sums = held("pass0_sums", [P, HALF * PACK], F32)
+        for c in first_half:
+            bank = new_bank([P, PACK, CHUNK])
+            key_pass(bank, 0, c, 0, True, True)
+            nc.scalar.activation(
+                out=pass0_sums[:, chunk_columns(c)].rearrange("p (n t) -> p n t", t=PACK),
+                in_=bank[:].rearrange("p t n -> p n t"),
+                func=COPY,
+            )
         gather_words(0, 1)
+        open_banks = {}
+        for c, b in open_groups:
+            open_banks[c, b] = new_bank([P, PACK, CHUNK])
+            key_pass(open_banks[c, b], 0, c, b, True, False)
         gather_words(1, 0)
-        reorder_wk(1)
+        reorder_wk_group0(1)
         gather_words(1, 1)
-        for c, b in first_groups:
-            key_pass(open_banks[c, b], 1, c, b)
-            keys_out(open_banks[c, b], c, b, VECTOR if (c, b) in ((3, 0), (1, 1)) else SCALAR)
+        for c, b in open_groups:
+            key_pass(open_banks[c, b], 1, c, b, False, True)
+            keys_out(open_banks[c, b], c, b, VECTOR if c == first_half[-1] else SCALAR)
 
         wv8_bf = in_turn("wv8_bf", [P, N, PACK], BF16)
         nc.vector.tensor_copy(
             out=wv8_bf[:].rearrange("p (c u) i -> p c i u", u=4), in_=wv8_raw[:].rearrange("p i (c u) -> p c i u", u=4)
         )
-        keys(4)
         wv8_mx = quantise("wv8", wv8_bf[:].rearrange("p n i -> p (n i)"), N)
         x_bf = in_turn("x_bf", [P, PASSES, M, PACK], BF16)
         nc.vector.tensor_copy(
             out=x_bf[:].rearrange("p a (c u) i -> p a c i u", u=4),
             in_=x_raw[:].rearrange("p a i (c u) -> p a c i u", u=4),
         )
-        keys(5)
+
+        kr_bf = in_turn("kr_bf", [P, HALF * PACK], BF16)
+        for c in first_half:
+            bank = new_bank([P, PACK, CHUNK])
+            key_pass(bank, 1, c, 0, True, True)
+            nc.vector.tensor_tensor(
+                out=kr_bf[:, chunk_columns(c)].rearrange("p (n t) -> p n t", t=PACK),
+                in0=bank[:].rearrange("p t n -> p n t"),
+                in1=pass0_sums[:, chunk_columns(c)].rearrange("p (n t) -> p n t", t=PACK),
+                op=ADD,
+            )
+        x_mx = quantise("x", x_bf[:].rearrange("p a m i -> p (a m i)"), PASSES * M)
         wq_plane = in_turn("wq_plane", [P, R // 4], I32)
         reorder(wq_plane[:], wq_scale_rows[:], 2)
-        x_mx = quantise("x", x_bf[:].rearrange("p a m i -> p (a m i)"), PASSES * M)
         wq_codes = []
         for b in range(PASSES):
             wq_codes.append(in_turn("wq_codes", [P, R], I32))
             reorder(wq_codes[b][:], wq_raw[b][:].rearrange("p a w -> p (a w)"), 8)
-        values(0, 0, wv8_mx, SCALAR)
-        values(0, 1, wv8_mx, SCALAR)
-        for b in range(PASSES):
-            quantise_keys(b, 0, HALF)
+        ka_bf[0, 0] = in_turn("ka_bf", [P, HALF * PACK], BF16)
+        nc.vector.tensor_scalar_max(out=ka_bf[0, 0][:], in0=kr_bf[:], scalar1=0.0)
+
+        for h in range(J // HALF):
+            for tile in range(N // P):
+                values(h, tile, wv8_mx, SCALAR)
+        keys(4, 1)
+        keys(5, 1)
         for b in range(PASSES):
             queries(b, wq_codes[b], wq_plane, x_mx)
-        for b in range(PASSES):
-            quantise_keys(b, HALF, 2 * CHUNK)
-        qa_mx = [quantise("qa%d" % b, qa_bf[b][:], M) for b in range(PASSES)]
-        values(1, 0, wv8_mx, VECTOR)
-        keys(6)
-        scores(0, HALF, (0,), qa_mx, VECTOR)
-        scores(0, HALF, (1,), qa_mx, VECTOR)
-        keys(7)
-        for b in range(PASSES):
-            quantise_keys(b, 6 * CHUNK, CHUNK)
-        scores(HALF, 2 * CHUNK, (0, 1), qa_mx, SCALAR)
-        for b in range(PASSES):
-            quantise_keys(b, 7 * CHUNK, CHUNK)
-        scores(6 * CHUNK, CHUNK, (0, 1), qa_mx, VECTOR)
-        values(1, 1, wv8_mx, SCALAR)
-        scores(7 * CHUNK, CHUNK, (0, 1), qa_mx, VECTOR)
+        keys(6, 1)
+        keys(7, 1)
+        quantise_keys(0, 1, 0, HALF)
+        quantise_keys(0, 0, 0, HALF)
+        quantise_keys(1, 0, 0, HALF)
+        qa_mx = [quantise("qa0", qa_bf[0][:], M)]
+        qa_mx.append(quantise("qa1", qa_bf[1][:], M))
+        quantise_keys(1, 1, 0, 2 * CHUNK)
+        quantise_keys(1, 1, 2 * CHUNK, CHUNK)
+        quantise_keys(1, 1, 3 * CHUNK, CHUNK)
+        scores(0, 0, 0, HALF, qa_mx, SCALAR)
+        scores(0, 1, 0, HALF, qa_mx, VECTOR)
+        scores(1, 0, 0, HALF, qa_mx, SCALAR)
+        scores(1, 1, 0, HALF // 2, qa_mx, VECTOR)
+        scores(1, 1, HALF // 2, HALF // 2, qa_mx, SCALAR)

@@ -280,36 +280,42 @@ def tile_list_kvt_qf_act_kernel(
                 nc.vector.tensor_copy(out=result[:], in_=bank[:])
             nc.sync.dma_start(out=out_1[rows, h * HALF : (h + 1) * HALF], in_=result[:])
 
-        def scores(h, tile, first, width, qa_mx, engine):
-            rows = slice(tile * P, (tile + 1) * P)
+        def scores(h, tiles, first, width, qa_mx, engine):
             columns = slice(first, first + width)
-            bank = new_bank([P, width])
-            for b in range(PASSES):
-                qa_codes, qa_plane = qa_mx[b]
-                ka_codes, ka_plane = ka_mx[h, b]
-                nc.tensor.matmul_mx(
-                    out=bank[:],
-                    lhsT=qa_codes[:, rows].bitcast(FP8X4),
-                    lhsT_scale=qa_plane[:, rows],
-                    rhs=ka_codes[:, columns].bitcast(FP8X4),
-                    rhs_scale=ka_plane[:, columns],
-                    start=(b == 0),
-                    stop=(b == PASSES - 1),
-                )
-            result = result_tile(engine, [P, width])
+            bank = new_bank([P, len(tiles), width])
+            for place, tile in enumerate(tiles):
+                rows = slice(tile * P, (tile + 1) * P)
+                for b in range(PASSES):
+                    qa_codes, qa_plane = qa_mx[b]
+                    ka_codes, ka_plane = ka_mx[h, b]
+                    nc.tensor.matmul_mx(
+                        out=bank[:, place, :],
+                        lhsT=qa_codes[:, rows].bitcast(FP8X4),
+                        lhsT_scale=qa_plane[:, rows],
+                        rhs=ka_codes[:, columns].bitcast(FP8X4),
+                        rhs_scale=ka_plane[:, columns],
+                        start=(b == 0),
+                        stop=(b == PASSES - 1),
+                    )
+            result = result_tile(engine, [P, len(tiles), width])
             if engine == SCALAR:
                 nc.scalar.activation(out=result[:], in_=bank[:], func=COPY, scale=SCORE_SCALE)
             else:
                 nc.vector.tensor_scalar(out=result[:], in0=bank[:], scalar1=SCORE_SCALE, scalar2=None, op0=MULT)
-            nc.sync.dma_start(out=out_0[rows, h * HALF + first : h * HALF + first + width], in_=result[:])
+            nc.sync.dma_start(
+                out=out_0.rearrange("(i p) j -> p i j", p=P)[
+                    :, tiles[0] : tiles[-1] + 1, h * HALF + first : h * HALF + first + width
+                ],
+                in_=result[:],
+            )
 
         first_half, second_half = range(PACK), range(PACK, 2 * PACK)
-        open_groups = [(c, 1) for c in first_half] + [(c, 0) for c in second_half]
+        open_groups = [(c, b) for b in (1, 0) for c in first_half]
         reorder_wk_group0(0)
-        gather_words(0, 0)
+        gather_words(0, 1)
         reorder_wk_group1()
         pass0_sums = held("pass0_sums", [P, HALF * PACK], F32)
-        for c in first_half:
+        for c in second_half:
             bank = new_bank([P, PACK, CHUNK])
             key_pass(bank, 0, c, 0, True, True)
             nc.scalar.activation(
@@ -317,7 +323,7 @@ def tile_list_kvt_qf_act_kernel(
                 in_=bank[:].rearrange("p t n -> p n t"),
                 func=COPY,
             )
-        gather_words(0, 1)
+        gather_words(0, 0)
         open_banks = {}
         for c, b in open_groups:
             open_banks[c, b] = new_bank([P, PACK, CHUNK])
@@ -327,7 +333,7 @@ def tile_list_kvt_qf_act_kernel(
         gather_words(1, 1)
         for c, b in open_groups:
             key_pass(open_banks[c, b], 1, c, b, False, True)
-            keys_out(open_banks[c, b], c, b, VECTOR if c == first_half[-1] else SCALAR)
+            keys_out(open_banks[c, b], c, b, VECTOR if (c, b) == open_groups[PACK - 1] else SCALAR)
 
         wv8_bf = in_turn("wv8_bf", [P, N, PACK], BF16)
         nc.vector.tensor_copy(
@@ -340,8 +346,16 @@ def tile_list_kvt_qf_act_kernel(
             in_=x_raw[:].rearrange("p a i (c u) -> p a c i u", u=4),
         )
 
+        wq_plane = in_turn("wq_plane", [P, R // 4], I32)
+        reorder(wq_plane[:], wq_scale_rows[:], 2)
+        x_mx = quantise("x", x_bf[:].rearrange("p a m i -> p (a m i)"), PASSES * M)
+        wq_codes = []
+        for b in range(PASSES):
+            wq_codes.append(in_turn("wq_codes", [P, R], I32))
+            reorder(wq_codes[b][:], wq_raw[b][:].rearrange("p a w -> p (a w)"), 8)
+
         kr_bf = in_turn("kr_bf", [P, HALF * PACK], BF16)
-        for c in first_half:
+        for c in second_half:
             bank = new_bank([P, PACK, CHUNK])
             key_pass(bank, 1, c, 0, True, True)
             nc.vector.tensor_tensor(
@@ -350,35 +364,24 @@ def tile_list_kvt_qf_act_kernel(
                 in1=pass0_sums[:, chunk_columns(c)].rearrange("p (n t) -> p n t", t=PACK),
                 op=ADD,
             )
-        x_mx = quantise("x", x_bf[:].rearrange("p a m i -> p (a m i)"), PASSES * M)
-        wq_plane = in_turn("wq_plane", [P, R // 4], I32)
-        reorder(wq_plane[:], wq_scale_rows[:], 2)
-        wq_codes = []
-        for b in range(PASSES):
-            wq_codes.append(in_turn("wq_codes", [P, R], I32))
-            reorder(wq_codes[b][:], wq_raw[b][:].rearrange("p a w -> p (a w)"), 8)
-        ka_bf[0, 0] = in_turn("ka_bf", [P, HALF * PACK], BF16)
-        nc.vector.tensor_scalar_max(out=ka_bf[0, 0][:], in0=kr_bf[:], scalar1=0.0)
-
         for h in range(J // HALF):
             for tile in range(N // P):
                 values(h, tile, wv8_mx, SCALAR)
-        keys(4, 1)
-        keys(5, 1)
         for b in range(PASSES):
             queries(b, wq_codes[b], wq_plane, x_mx)
-        keys(6, 1)
-        keys(7, 1)
+        for c in second_half:
+            keys(c, 1)
         quantise_keys(0, 1, 0, HALF)
         quantise_keys(0, 0, 0, HALF)
-        quantise_keys(1, 0, 0, HALF)
-        qa_mx = [quantise("qa0", qa_bf[0][:], M)]
-        qa_mx.append(quantise("qa1", qa_bf[1][:], M))
+        qa_mx = [quantise("qa%d" % b, qa_bf[b][:], M) for b in range(PASSES)]
+        ka_bf[1, 0] = in_turn("ka_bf", [P, HALF * PACK], BF16)
+        nc.vector.tensor_scalar_max(out=ka_bf[1, 0][:], in0=kr_bf[:], scalar1=0.0)
         quantise_keys(1, 1, 0, 2 * CHUNK)
+        quantise_keys(1, 0, 0, HALF)
         quantise_keys(1, 1, 2 * CHUNK, CHUNK)
         quantise_keys(1, 1, 3 * CHUNK, CHUNK)
-        scores(0, 0, 0, HALF, qa_mx, SCALAR)
-        scores(0, 1, 0, HALF, qa_mx, VECTOR)
-        scores(1, 0, 0, HALF, qa_mx, SCALAR)
-        scores(1, 1, 0, HALF // 2, qa_mx, VECTOR)
-        scores(1, 1, HALF // 2, HALF // 2, qa_mx, SCALAR)
+        scores(0, (0,), 0, HALF, qa_mx, SCALAR)
+        scores(0, (1,), 0, HALF, qa_mx, VECTOR)
+        scores(1, (0,), 0, HALF, qa_mx, SCALAR)
+        scores(1, (1,), 0, HALF // 2, qa_mx, VECTOR)
+        scores(1, (1,), HALF // 2, HALF // 2, qa_mx, SCALAR)

@@ -41,9 +41,10 @@ SCALE_ROWS = PASSES * BLOCKS
 FIRST_ROW = P - SCALE_ROWS
 SCORE_SCALE = 0.03125
 SCALAR, VECTOR = "scalar", "vector"
-VECTOR_TILES = 24
+VECTOR_TILES = 25
 SCALAR_RESULTS = 7
 PSUM_BANKS = 8
+TABLE_PIECE = 8192
 
 
 def tile_list_kvt_qf_act_kernel(
@@ -86,19 +87,27 @@ def tile_list_kvt_qf_act_kernel(
         staged_rows = held("staged_rows", [P, wv4_cols.stop], I32)
         planes = [held("planes%d" % a, [P, plane_width[a]], I32) for a in range(PASSES)]
         wq_scale_rows = held("wq_scale_rows", [P, R // 4], I32)
-        wk_group0 = [held("wk_group0_%d" % a, [P, PASS // 2], I32) for a in range(PASSES)]
-        wk_group1 = held("wk_group1", [P, PASSES, PASS // 2], I32)
-        wk_dram = wk_words.rearrange("a p (b n) -> b p a n", b=PASSES).bitcast(I32)
+        wk_raw = {
+            (a, b): held("wk_raw%d%d" % (a, b), [P, PASS // 2], I32) for a in range(PASSES) for b in range(PASSES)
+        }
+        wk_dram = wk_words.bitcast(I32)
         staged = slice(FIRST_ROW, P)
         tab_win = [held("tab_win%d" % a, [P, T], I32) for a in range(PASSES)]
 
         def load_table(a):
-            nc.sync.dma_start(out=tab_win[a][:], in_=tab_words[a].rearrange("p t i -> p (t i)").bitcast(I32))
+            nc.sync.dma_start(
+                out=tab_win[a][:],
+                in_=tab_words[a].rearrange("p t i -> p (t i)").bitcast(I32),
+                max_dma_last_dim=TABLE_PIECE,
+            )
 
-        def move_to_planes(a):
+        def load_wk(a, b):
+            nc.sync.dma_start(out=wk_raw[a, b][:], in_=wk_dram[a][:, b * PASS // 2 : (b + 1) * PASS // 2])
+
+        def move_to_planes(a, queue):
             for quad in QUADRANTS:
                 row = FIRST_ROW + BLOCKS * a + 4 * quad
-                nc.sync.dma_start(
+                queue.dma_start(
                     out=planes[a][quadrant_rows(quad), :], in_=staged_rows[row : row + 4, 0 : plane_width[a]]
                 )
 
@@ -110,17 +119,18 @@ def tile_list_kvt_qf_act_kernel(
         nc.sync.dma_start(offsets[:], offs)
         nc.sync.dma_start(out=tab_scale_rows[staged, :], in_=tab_scales.rearrange("a q t -> (a q) t").bitcast(I32))
         nc.sync.dma_start(out=wk_scale_rows[staged, :], in_=wk_scales.rearrange("a q r -> (a q) r").bitcast(I32))
-        nc.sync.dma_start(out=wk_group0[0][:], in_=wk_dram[0][:, 0, :])
+        load_wk(0, 0)
         load_table(0)
-        nc.sync.dma_start(out=wk_group1[:], in_=wk_dram[1])
+        load_wk(0, 1)
         nc.sync.dma_start(out=staged_rows[FIRST_ROW + BLOCKS : P, wv4_cols], in_=wv4_scales[0].bitcast(I32))
         reorder(staged_rows[staged, wk_cols], wk_scale_rows[staged, :], 2, nc.gpsimd)
         nc.vector.tensor_copy(out=v_scale_rows[:], in_=tab_scale_rows[:].bitcast(U8).indirect(offsets[:]))
         nc.vector.tensor_copy(out=staged_rows[staged, v_cols], in_=v_scale_rows[staged, :].bitcast(I32))
-        move_to_planes(0)
+        move_to_planes(0, nc.scalar)
         load_table(1)
-        nc.sync.dma_start(out=wk_group0[1][:], in_=wk_dram[0][:, 1, :])
-        move_to_planes(1)
+        load_wk(1, 1)
+        move_to_planes(1, nc.sync)
+        load_wk(1, 0)
 
         x_raw = held("x_raw", [P, PASSES, PACK, M], F32)
         wq_raw = [held("wq_raw%d" % b, [P, PASSES, PASS], I32) for b in range(PASSES)]
@@ -153,16 +163,10 @@ def tile_list_kvt_qf_act_kernel(
 
         wk_codes = {}
 
-        def reorder_wk_group0(a):
+        def reorder_wk(a, b):
             codes = in_turn("wk_codes", [P, PASS // 2], I32)
-            reorder(codes[:], wk_group0[a][:], 4)
-            wk_codes[a, 0] = codes[:]
-
-        def reorder_wk_group1():
-            codes = in_turn("wk_codes", [P, PASSES, PASS // 2], I32)
-            reorder(codes[:].rearrange("p a w -> p (a w)"), wk_group1[:].rearrange("p a w -> p (a w)"), 4)
-            for a in range(PASSES):
-                wk_codes[a, 1] = codes[:, a, :]
+            reorder(codes[:], wk_raw[a, b][:], 4)
+            wk_codes[a, b] = codes[:]
 
         def plane_bytes(a, cols, first, width):
             return planes[a][:].bitcast(U8)[:, 4 * cols.start + first : 4 * cols.start + first + width]
@@ -311,9 +315,8 @@ def tile_list_kvt_qf_act_kernel(
 
         first_half, second_half = range(PACK), range(PACK, 2 * PACK)
         open_groups = [(c, b) for b in (1, 0) for c in first_half]
-        reorder_wk_group0(0)
+        reorder_wk(0, 0)
         gather_words(0, 1)
-        reorder_wk_group1()
         pass0_sums = held("pass0_sums", [P, HALF * PACK], F32)
         for c in second_half:
             bank = new_bank([P, PACK, CHUNK])
@@ -324,13 +327,15 @@ def tile_list_kvt_qf_act_kernel(
                 func=COPY,
             )
         gather_words(0, 0)
+        reorder_wk(0, 1)
         open_banks = {}
         for c, b in open_groups:
             open_banks[c, b] = new_bank([P, PACK, CHUNK])
             key_pass(open_banks[c, b], 0, c, b, True, False)
         gather_words(1, 0)
-        reorder_wk_group0(1)
+        reorder_wk(1, 1)
         gather_words(1, 1)
+        reorder_wk(1, 0)
         for c, b in open_groups:
             key_pass(open_banks[c, b], 1, c, b, False, True)
             keys_out(open_banks[c, b], c, b, VECTOR if (c, b) == open_groups[PACK - 1] else SCALAR)

@@ -44,7 +44,7 @@ SCALAR, VECTOR = "scalar", "vector"
 VECTOR_TILES = 25
 SCALAR_RESULTS = 7
 PSUM_BANKS = 8
-TABLE_PIECE = 8192
+EARLY_COLUMNS = 5 * T // 8
 
 
 def tile_list_kvt_qf_act_kernel(
@@ -75,41 +75,44 @@ def tile_list_kvt_qf_act_kernel(
                 in_=src.rearrange("p (g q t u) -> p g t q u", t=PACK, q=BLOCKS, u=run),
             )
 
-        v_cols = slice(0, J // 4)
-        wk_cols = slice(v_cols.stop, v_cols.stop + R // 4)
-        wv4_cols = slice(wk_cols.stop, wk_cols.stop + N // 4)
-        plane_width = (wk_cols.stop, wv4_cols.stop)
+        wk_cols = slice(HALF // 4, HALF // 4 + R // 4)
+        v_cols = [slice(wk_cols.stop, wk_cols.stop + HALF // 4), slice(0, HALF // 4)]
+        wv4_cols = slice(v_cols[0].stop, v_cols[0].stop + N // 4)
+        plane_width = (v_cols[0].stop, wv4_cols.stop)
 
         offsets = keep.tile([P, J // LIST_GROUP], U16, name="offsets")
         tab_scale_rows = held("tab_scale_rows", [P, T // 4], I32)
         wk_scale_rows = held("wk_scale_rows", [P, R // 4], I32)
-        v_scale_rows = held("v_scale_rows", [P, J], U8)
+        v_scale_rows = held("v_scale_rows", [P, HALF], U8)
         staged_rows = held("staged_rows", [P, wv4_cols.stop], I32)
         planes = [held("planes%d" % a, [P, plane_width[a]], I32) for a in range(PASSES)]
         wq_scale_rows = held("wq_scale_rows", [P, R // 4], I32)
-        wk_raw = {
-            (a, b): held("wk_raw%d%d" % (a, b), [P, PASS // 2], I32) for a in range(PASSES) for b in range(PASSES)
-        }
+        wk_raw = {(a, 0): held("wk_raw%d0" % a, [P, PASS // 2], I32) for a in range(PASSES)}
+        wk_group1 = held("wk_group1", [P, PASSES, PASS // 2], I32)
         wk_dram = wk_words.bitcast(I32)
         staged = slice(FIRST_ROW, P)
         tab_win = [held("tab_win%d" % a, [P, T], I32) for a in range(PASSES)]
 
-        def load_table(a):
+        def load_table(a, cols):
             nc.sync.dma_start(
-                out=tab_win[a][:],
-                in_=tab_words[a].rearrange("p t i -> p (t i)").bitcast(I32),
-                max_dma_last_dim=TABLE_PIECE,
+                out=tab_win[a][:, cols], in_=tab_words[a].rearrange("p t i -> p (t i)").bitcast(I32)[:, cols]
             )
+
+        def half_of_list(h):
+            columns = HALF // LIST_GROUP
+            return offsets[:, columns * h : columns * (h + 1)]
+
+        def gather_scales(h):
+            nc.vector.tensor_copy(out=v_scale_rows[:], in_=tab_scale_rows[:].bitcast(U8).indirect(half_of_list(h)))
+            nc.vector.tensor_copy(out=staged_rows[staged, v_cols[h]], in_=v_scale_rows[staged, :].bitcast(I32))
 
         def load_wk(a, b):
             nc.sync.dma_start(out=wk_raw[a, b][:], in_=wk_dram[a][:, b * PASS // 2 : (b + 1) * PASS // 2])
 
-        def move_to_planes(a, queue):
+        def move_to_planes(a, cols):
             for quad in QUADRANTS:
                 row = FIRST_ROW + BLOCKS * a + 4 * quad
-                queue.dma_start(
-                    out=planes[a][quadrant_rows(quad), :], in_=staged_rows[row : row + 4, 0 : plane_width[a]]
-                )
+                nc.sync.dma_start(out=planes[a][quadrant_rows(quad), cols], in_=staged_rows[row : row + 4, cols])
 
         nc.vector.memset(tab_scale_rows[0:FIRST_ROW, :], 0)
         for a in range(PASSES):
@@ -120,46 +123,58 @@ def tile_list_kvt_qf_act_kernel(
         nc.sync.dma_start(out=tab_scale_rows[staged, :], in_=tab_scales.rearrange("a q t -> (a q) t").bitcast(I32))
         nc.sync.dma_start(out=wk_scale_rows[staged, :], in_=wk_scales.rearrange("a q r -> (a q) r").bitcast(I32))
         load_wk(0, 0)
-        load_table(0)
-        load_wk(0, 1)
+        load_table(0, slice(0, T))
+        nc.sync.dma_start(
+            out=wk_group1[:], in_=wk_words.rearrange("a p (b n) -> b p a n", b=PASSES).bitcast(I32)[1]
+        )
         nc.sync.dma_start(out=staged_rows[FIRST_ROW + BLOCKS : P, wv4_cols], in_=wv4_scales[0].bitcast(I32))
         reorder(staged_rows[staged, wk_cols], wk_scale_rows[staged, :], 2, nc.gpsimd)
-        nc.vector.tensor_copy(out=v_scale_rows[:], in_=tab_scale_rows[:].bitcast(U8).indirect(offsets[:]))
-        nc.vector.tensor_copy(out=staged_rows[staged, v_cols], in_=v_scale_rows[staged, :].bitcast(I32))
-        move_to_planes(0, nc.scalar)
-        load_table(1)
-        load_wk(1, 1)
-        move_to_planes(1, nc.sync)
+        gather_scales(1)
+        move_to_planes(0, slice(0, wk_cols.stop))
+        load_table(1, slice(0, EARLY_COLUMNS))
+        gather_scales(0)
+        move_to_planes(0, v_cols[0])
+        load_table(1, slice(EARLY_COLUMNS, T))
         load_wk(1, 0)
+        move_to_planes(1, slice(0, plane_width[1]))
 
         x_raw = held("x_raw", [P, PASSES, PACK, M], F32)
         wq_raw = [held("wq_raw%d" % b, [P, PASSES, PASS], I32) for b in range(PASSES)]
         wv8_raw = held("wv8_raw", [P, PACK, N], F32)
         wv4_codes = held("wv4_codes", [P, N // 2], I32)
 
-        nc.sync.dma_start(out=wv8_raw[:], in_=wv8.rearrange("(p i) n -> p i n", i=PACK))
-        nc.sync.dma_start(out=x_raw[:], in_=x.rearrange("(a p i) m -> p a i m", a=PASSES, i=PACK))
-        nc.sync.dma_start(out=wv4_codes[:], in_=wv4_words[0].bitcast(I32))
-        for quad in QUADRANTS:
-            nc.sync.dma_start(
-                out=wq_scale_rows[quadrant_rows(quad, count=8), :],
-                in_=wq_scales[:, 4 * quad : 4 * quad + 4, :].bitcast(I32),
-            )
-        for b in range(PASSES):
+        def load_value_weights():
+            nc.sync.dma_start(out=wv8_raw[:], in_=wv8.rearrange("(p i) n -> p i n", i=PACK))
+            nc.sync.dma_start(out=wv4_codes[:], in_=wv4_words[0].bitcast(I32))
+
+        def load_x():
+            nc.sync.dma_start(out=x_raw[:], in_=x.rearrange("(a p i) m -> p a i m", a=PASSES, i=PACK))
+
+        def load_wq_scales():
+            for quad in QUADRANTS:
+                nc.sync.dma_start(
+                    out=wq_scale_rows[quadrant_rows(quad, count=8), :],
+                    in_=wq_scales[:, 4 * quad : 4 * quad + 4, :].bitcast(I32),
+                )
+
+        def load_wq(b):
             nc.sync.dma_start(
                 out=wq_raw[b][:],
                 in_=wq_words[:, :, b * PASS : (b + 1) * PASS, :].rearrange("a p r i -> p a (r i)").bitcast(I32),
             )
 
+        nc.sync.dma_start(out=wv8_raw[:], in_=wv8.rearrange("(p i) n -> p i n", i=PACK))
+        load_x()
+        nc.sync.dma_start(out=wv4_codes[:], in_=wv4_words[0].bitcast(I32))
+        load_wq_scales()
+        load_wq(0)
+        load_wq(1)
+
         v_codes = {}
 
         def gather_words(a, h):
-            columns = HALF // LIST_GROUP
             v_codes[a, h] = in_turn("v_codes", [P, HALF], U32)
-            nc.vector.tensor_copy(
-                out=v_codes[a, h][:],
-                in_=tab_win[a][:].bitcast(U32).indirect(offsets[:, columns * h : columns * (h + 1)]),
-            )
+            nc.vector.tensor_copy(out=v_codes[a, h][:], in_=tab_win[a][:].bitcast(U32).indirect(half_of_list(h)))
 
         wk_codes = {}
 
@@ -167,6 +182,12 @@ def tile_list_kvt_qf_act_kernel(
             codes = in_turn("wk_codes", [P, PASS // 2], I32)
             reorder(codes[:], wk_raw[a, b][:], 4)
             wk_codes[a, b] = codes[:]
+
+        def reorder_wk_group1():
+            codes = in_turn("wk_codes", [P, PASSES, PASS // 2], I32)
+            reorder(codes[:].rearrange("p a w -> p (a w)"), wk_group1[:].rearrange("p a w -> p (a w)"), 4)
+            for a in range(PASSES):
+                wk_codes[a, 1] = codes[:, a, :]
 
         def plane_bytes(a, cols, first, width):
             return planes[a][:].bitcast(U8)[:, 4 * cols.start + first : 4 * cols.start + first + width]
@@ -194,7 +215,7 @@ def tile_list_kvt_qf_act_kernel(
                     lhsT=wk_codes[a, b].bitcast(U8)[:, 2 * t * P : 2 * (t + 1) * P].bitcast(FP4X4),
                     lhsT_scale=plane_bytes(a, wk_cols, col, P),
                     rhs=v_codes[a, h][:, first : first + CHUNK].bitcast(FP8X4),
-                    rhs_scale=plane_bytes(a, v_cols, c * CHUNK, CHUNK),
+                    rhs_scale=plane_bytes(a, v_cols[h], first, CHUNK),
                     start=(opens and t == 0),
                     stop=(closes and t == PACK - 1),
                 )
@@ -264,7 +285,7 @@ def tile_list_kvt_qf_act_kernel(
                 lhsT=wv8_codes[:, rows].bitcast(FP8X4),
                 lhsT_scale=wv8_plane[:, rows],
                 rhs=v_codes[0, h][:].bitcast(FP8X4),
-                rhs_scale=plane_bytes(0, v_cols, h * HALF, HALF),
+                rhs_scale=plane_bytes(0, v_cols[h], 0, HALF),
                 start=True,
                 stop=False,
             )
@@ -273,7 +294,7 @@ def tile_list_kvt_qf_act_kernel(
                 lhsT=wv4_codes[:].bitcast(U8)[:, 2 * tile * P : 2 * (tile + 1) * P].bitcast(FP4X4),
                 lhsT_scale=plane_bytes(1, wv4_cols, tile * P, P),
                 rhs=v_codes[1, h][:].bitcast(FP8X4),
-                rhs_scale=plane_bytes(1, v_cols, h * HALF, HALF),
+                rhs_scale=plane_bytes(1, v_cols[h], 0, HALF),
                 start=False,
                 stop=True,
             )
@@ -327,40 +348,43 @@ def tile_list_kvt_qf_act_kernel(
                 func=COPY,
             )
         gather_words(0, 0)
-        reorder_wk(0, 1)
+        reorder_wk_group1()
         open_banks = {}
         for c, b in open_groups:
             open_banks[c, b] = new_bank([P, PACK, CHUNK])
             key_pass(open_banks[c, b], 0, c, b, True, False)
         gather_words(1, 0)
-        reorder_wk(1, 1)
-        gather_words(1, 1)
         reorder_wk(1, 0)
-        for c, b in open_groups:
+        gather_words(1, 1)
+
+        def close_keys(c, b, engine):
             key_pass(open_banks[c, b], 1, c, b, False, True)
-            keys_out(open_banks[c, b], c, b, VECTOR if (c, b) == open_groups[PACK - 1] else SCALAR)
+            keys_out(open_banks[c, b], c, b, engine)
 
-        wv8_bf = in_turn("wv8_bf", [P, N, PACK], BF16)
-        nc.vector.tensor_copy(
-            out=wv8_bf[:].rearrange("p (c u) i -> p c i u", u=4), in_=wv8_raw[:].rearrange("p i (c u) -> p c i u", u=4)
-        )
-        wv8_mx = quantise("wv8", wv8_bf[:].rearrange("p n i -> p (n i)"), N)
-        x_bf = in_turn("x_bf", [P, PASSES, M, PACK], BF16)
-        nc.vector.tensor_copy(
-            out=x_bf[:].rearrange("p a (c u) i -> p a c i u", u=4),
-            in_=x_raw[:].rearrange("p a i (c u) -> p a c i u", u=4),
-        )
+        def rounded(name, raw, pattern_in, pattern_out, shape):
+            values_bf = in_turn(name, shape, BF16)
+            nc.vector.tensor_copy(out=values_bf[:].rearrange(pattern_out, u=4), in_=raw[:].rearrange(pattern_in, u=4))
+            return values_bf
 
-        wq_plane = in_turn("wq_plane", [P, R // 4], I32)
-        reorder(wq_plane[:], wq_scale_rows[:], 2)
-        x_mx = quantise("x", x_bf[:].rearrange("p a m i -> p (a m i)"), PASSES * M)
-        wq_codes = []
-        for b in range(PASSES):
-            wq_codes.append(in_turn("wq_codes", [P, R], I32))
-            reorder(wq_codes[b][:], wq_raw[b][:].rearrange("p a w -> p (a w)"), 8)
+        def round_wv8():
+            return rounded("wv8_bf", wv8_raw, "p i (c u) -> p c i u", "p (c u) i -> p c i u", [P, N, PACK])
 
-        kr_bf = in_turn("kr_bf", [P, HALF * PACK], BF16)
-        for c in second_half:
+        def round_x():
+            return rounded(
+                "x_bf", x_raw, "p a i (c u) -> p a c i u", "p a (c u) i -> p a c i u", [P, PASSES, M, PACK]
+            )
+
+        def reorder_wq_plane():
+            plane = in_turn("wq_plane", [P, R // 4], I32)
+            reorder(plane[:], wq_scale_rows[:], 2)
+            return plane
+
+        def reorder_wq(b):
+            codes = in_turn("wq_codes", [P, R], I32)
+            reorder(codes[:], wq_raw[b][:].rearrange("p a w -> p (a w)"), 8)
+            return codes
+
+        def finish_parked(c, kr_bf):
             bank = new_bank([P, PACK, CHUNK])
             key_pass(bank, 1, c, 0, True, True)
             nc.vector.tensor_tensor(
@@ -369,18 +393,36 @@ def tile_list_kvt_qf_act_kernel(
                 in1=pass0_sums[:, chunk_columns(c)].rearrange("p (n t) -> p n t", t=PACK),
                 op=ADD,
             )
+
+        def relu_parked(kr_bf):
+            ka_bf[1, 0] = in_turn("ka_bf", [P, HALF * PACK], BF16)
+            nc.vector.tensor_scalar_max(out=ka_bf[1, 0][:], in0=kr_bf[:], scalar1=0.0)
+
+        for place, (c, b) in enumerate(open_groups):
+            close_keys(c, b, VECTOR if place in (3,) else SCALAR)
+        wv8_bf = round_wv8()
+        wv8_mx = quantise("wv8", wv8_bf[:].rearrange("p n i -> p (n i)"), N)
+        x_bf = round_x()
+        wq_plane = reorder_wq_plane()
+        x_mx = quantise("x", x_bf[:].rearrange("p a m i -> p (a m i)"), PASSES * M)
+        wq_codes0 = reorder_wq(0)
+        wq_codes1 = reorder_wq(1)
+        kr_bf = in_turn("kr_bf", [P, HALF * PACK], BF16)
+        keys(4, 1)
         for h in range(J // HALF):
             for tile in range(N // P):
                 values(h, tile, wv8_mx, SCALAR)
-        for b in range(PASSES):
-            queries(b, wq_codes[b], wq_plane, x_mx)
         for c in second_half:
+            finish_parked(c, kr_bf)
+        queries(0, wq_codes0, wq_plane, x_mx)
+        queries(1, wq_codes1, wq_plane, x_mx)
+        for c in (5, 6, 7):
             keys(c, 1)
         quantise_keys(0, 1, 0, HALF)
         quantise_keys(0, 0, 0, HALF)
-        qa_mx = [quantise("qa%d" % b, qa_bf[b][:], M) for b in range(PASSES)]
-        ka_bf[1, 0] = in_turn("ka_bf", [P, HALF * PACK], BF16)
-        nc.vector.tensor_scalar_max(out=ka_bf[1, 0][:], in0=kr_bf[:], scalar1=0.0)
+        qa_mx = [quantise("qa0", qa_bf[0][:], M)]
+        qa_mx.append(quantise("qa1", qa_bf[1][:], M))
+        relu_parked(kr_bf)
         quantise_keys(1, 1, 0, 2 * CHUNK)
         quantise_keys(1, 0, 0, HALF)
         quantise_keys(1, 1, 2 * CHUNK, CHUNK)

@@ -44,7 +44,8 @@ SCALAR, VECTOR = "scalar", "vector"
 VECTOR_TILES = 25
 SCALAR_RESULTS = 7
 PSUM_BANKS = 8
-EARLY_COLUMNS = 5 * T // 8
+WARM_UPS = 5
+EARLY_COLUMNS = T // 2
 
 
 def tile_list_kvt_qf_act_kernel(
@@ -135,6 +136,17 @@ def tile_list_kvt_qf_act_kernel(
         gather_scales(0)
         move_to_planes(0, v_cols[0])
         load_table(1, slice(EARLY_COLUMNS, T))
+        unread = new_bank([P, HALF])
+        for warm in range(WARM_UPS):
+            nc.tensor.matmul_mx(
+                out=unread[:],
+                lhsT=planes[1][:, 0:P].bitcast(FP8X4),
+                lhsT_scale=v_scale_rows[:, 0:P],
+                rhs=planes[1][:, 0:HALF].bitcast(FP8X4),
+                rhs_scale=v_scale_rows[:],
+                start=True,
+                stop=True,
+            )
         load_wk(1, 0)
         move_to_planes(1, slice(0, plane_width[1]))
 

@@ -41,11 +41,13 @@ SCALE_ROWS = PASSES * BLOCKS
 FIRST_ROW = P - SCALE_ROWS
 SCORE_SCALE = 0.03125
 SCALAR, VECTOR = "scalar", "vector"
-VECTOR_TILES = 25
+VECTOR_TILES = 24
 SCALAR_RESULTS = 7
 PSUM_BANKS = 8
 WARM_UPS = 5
 EARLY_COLUMNS = T // 2
+VECTOR_BANK = 1
+NEIGHBOURS = 4
 
 
 def tile_list_kvt_qf_act_kernel(
@@ -80,6 +82,7 @@ def tile_list_kvt_qf_act_kernel(
         v_cols = [slice(wk_cols.stop, wk_cols.stop + HALF // 4), slice(0, HALF // 4)]
         wv4_cols = slice(v_cols[0].stop, v_cols[0].stop + N // 4)
         plane_width = (v_cols[0].stop, wv4_cols.stop)
+        first_cols = slice(0, wk_cols.start + PASS // 4)
 
         offsets = keep.tile([P, J // LIST_GROUP], U16, name="offsets")
         tab_scale_rows = held("tab_scale_rows", [P, T // 4], I32)
@@ -88,9 +91,9 @@ def tile_list_kvt_qf_act_kernel(
         staged_rows = held("staged_rows", [P, wv4_cols.stop], I32)
         planes = [held("planes%d" % a, [P, plane_width[a]], I32) for a in range(PASSES)]
         wq_scale_rows = held("wq_scale_rows", [P, R // 4], I32)
-        wk_raw = {(a, 0): held("wk_raw%d0" % a, [P, PASS // 2], I32) for a in range(PASSES)}
+        wk_group0 = [held("wk_group0_%d" % a, [P, PASS // 2], I32) for a in range(PASSES)]
         wk_group1 = held("wk_group1", [P, PASSES, PASS // 2], I32)
-        wk_dram = wk_words.bitcast(I32)
+        wk_dram = wk_words.rearrange("a p (b n) -> b p a n", b=PASSES).bitcast(I32)
         staged = slice(FIRST_ROW, P)
         tab_win = [held("tab_win%d" % a, [P, T], I32) for a in range(PASSES)]
 
@@ -107,9 +110,6 @@ def tile_list_kvt_qf_act_kernel(
             nc.vector.tensor_copy(out=v_scale_rows[:], in_=tab_scale_rows[:].bitcast(U8).indirect(half_of_list(h)))
             nc.vector.tensor_copy(out=staged_rows[staged, v_cols[h]], in_=v_scale_rows[staged, :].bitcast(I32))
 
-        def load_wk(a, b):
-            nc.sync.dma_start(out=wk_raw[a, b][:], in_=wk_dram[a][:, b * PASS // 2 : (b + 1) * PASS // 2])
-
         def move_to_planes(a, cols):
             for quad in QUADRANTS:
                 row = FIRST_ROW + BLOCKS * a + 4 * quad
@@ -123,18 +123,16 @@ def tile_list_kvt_qf_act_kernel(
         nc.sync.dma_start(offsets[:], offs)
         nc.sync.dma_start(out=tab_scale_rows[staged, :], in_=tab_scales.rearrange("a q t -> (a q) t").bitcast(I32))
         nc.sync.dma_start(out=wk_scale_rows[staged, :], in_=wk_scales.rearrange("a q r -> (a q) r").bitcast(I32))
-        load_wk(0, 0)
+        nc.sync.dma_start(out=wk_group0[0][:], in_=wk_dram[0][:, 0, :])
         load_table(0, slice(0, T))
-        nc.sync.dma_start(
-            out=wk_group1[:], in_=wk_words.rearrange("a p (b n) -> b p a n", b=PASSES).bitcast(I32)[1]
-        )
+        nc.sync.dma_start(out=wk_group1[:], in_=wk_dram[1])
         nc.sync.dma_start(out=staged_rows[FIRST_ROW + BLOCKS : P, wv4_cols], in_=wv4_scales[0].bitcast(I32))
         reorder(staged_rows[staged, wk_cols], wk_scale_rows[staged, :], 2, nc.gpsimd)
         gather_scales(1)
-        move_to_planes(0, slice(0, wk_cols.stop))
+        move_to_planes(0, first_cols)
         load_table(1, slice(0, EARLY_COLUMNS))
         gather_scales(0)
-        move_to_planes(0, v_cols[0])
+        move_to_planes(0, slice(first_cols.stop, plane_width[0]))
         load_table(1, slice(EARLY_COLUMNS, T))
         unread = new_bank([P, HALF])
         for warm in range(WARM_UPS):
@@ -147,7 +145,7 @@ def tile_list_kvt_qf_act_kernel(
                 start=True,
                 stop=True,
             )
-        load_wk(1, 0)
+        nc.sync.dma_start(out=wk_group0[1][:], in_=wk_dram[0][:, 1, :])
         move_to_planes(1, slice(0, plane_width[1]))
 
         x_raw = held("x_raw", [P, PASSES, PACK, M], F32)
@@ -155,32 +153,19 @@ def tile_list_kvt_qf_act_kernel(
         wv8_raw = held("wv8_raw", [P, PACK, N], F32)
         wv4_codes = held("wv4_codes", [P, N // 2], I32)
 
-        def load_value_weights():
-            nc.sync.dma_start(out=wv8_raw[:], in_=wv8.rearrange("(p i) n -> p i n", i=PACK))
-            nc.sync.dma_start(out=wv4_codes[:], in_=wv4_words[0].bitcast(I32))
-
-        def load_x():
-            nc.sync.dma_start(out=x_raw[:], in_=x.rearrange("(a p i) m -> p a i m", a=PASSES, i=PACK))
-
-        def load_wq_scales():
-            for quad in QUADRANTS:
-                nc.sync.dma_start(
-                    out=wq_scale_rows[quadrant_rows(quad, count=8), :],
-                    in_=wq_scales[:, 4 * quad : 4 * quad + 4, :].bitcast(I32),
-                )
-
-        def load_wq(b):
+        nc.sync.dma_start(out=wv8_raw[:], in_=wv8.rearrange("(p i) n -> p i n", i=PACK))
+        nc.sync.dma_start(out=x_raw[:], in_=x.rearrange("(a p i) m -> p a i m", a=PASSES, i=PACK))
+        nc.sync.dma_start(out=wv4_codes[:], in_=wv4_words[0].bitcast(I32))
+        for quad in QUADRANTS:
+            nc.sync.dma_start(
+                out=wq_scale_rows[quadrant_rows(quad, count=8), :],
+                in_=wq_scales[:, 4 * quad : 4 * quad + 4, :].bitcast(I32),
+            )
+        for b in range(PASSES):
             nc.sync.dma_start(
                 out=wq_raw[b][:],
                 in_=wq_words[:, :, b * PASS : (b + 1) * PASS, :].rearrange("a p r i -> p a (r i)").bitcast(I32),
             )
-
-        nc.sync.dma_start(out=wv8_raw[:], in_=wv8.rearrange("(p i) n -> p i n", i=PACK))
-        load_x()
-        nc.sync.dma_start(out=wv4_codes[:], in_=wv4_words[0].bitcast(I32))
-        load_wq_scales()
-        load_wq(0)
-        load_wq(1)
 
         v_codes = {}
 
@@ -190,10 +175,10 @@ def tile_list_kvt_qf_act_kernel(
 
         wk_codes = {}
 
-        def reorder_wk(a, b):
+        def reorder_wk_group0(a):
             codes = in_turn("wk_codes", [P, PASS // 2], I32)
-            reorder(codes[:], wk_raw[a, b][:], 4)
-            wk_codes[a, b] = codes[:]
+            reorder(codes[:], wk_group0[a][:], 4)
+            wk_codes[a, 0] = codes[:]
 
         def reorder_wk_group1():
             codes = in_turn("wk_codes", [P, PASSES, PASS // 2], I32)
@@ -288,7 +273,7 @@ def tile_list_kvt_qf_act_kernel(
                 return in_turn("result", shape, F32)
             return stage.tile(shape, F32, name="result", tag="result")
 
-        def values(h, tile, wv8_mx, engine):
+        def values(h, tile, wv8_mx):
             wv8_codes, wv8_plane = wv8_mx
             rows = slice(tile * P, (tile + 1) * P)
             bank = new_bank([P, HALF])
@@ -310,45 +295,41 @@ def tile_list_kvt_qf_act_kernel(
                 start=False,
                 stop=True,
             )
-            result = result_tile(engine, [P, HALF])
-            if engine == SCALAR:
-                nc.scalar.activation(out=result[:], in_=bank[:], func=COPY)
-            else:
-                nc.vector.tensor_copy(out=result[:], in_=bank[:])
+            result = result_tile(SCALAR, [P, HALF])
+            nc.scalar.activation(out=result[:], in_=bank[:], func=COPY)
             nc.sync.dma_start(out=out_1[rows, h * HALF : (h + 1) * HALF], in_=result[:])
 
-        def scores(h, tiles, first, width, qa_mx, engine):
+        def scores(h, tile, first, width, qa_mx, engine):
             columns = slice(first, first + width)
-            bank = new_bank([P, len(tiles), width])
-            for place, tile in enumerate(tiles):
-                rows = slice(tile * P, (tile + 1) * P)
-                for b in range(PASSES):
-                    qa_codes, qa_plane = qa_mx[b]
-                    ka_codes, ka_plane = ka_mx[h, b]
-                    nc.tensor.matmul_mx(
-                        out=bank[:, place, :],
-                        lhsT=qa_codes[:, rows].bitcast(FP8X4),
-                        lhsT_scale=qa_plane[:, rows],
-                        rhs=ka_codes[:, columns].bitcast(FP8X4),
-                        rhs_scale=ka_plane[:, columns],
-                        start=(b == 0),
-                        stop=(b == PASSES - 1),
-                    )
-            result = result_tile(engine, [P, len(tiles), width])
+            rows = slice(tile * P, (tile + 1) * P)
+            bank = new_bank([P, width])
+            for b in range(PASSES):
+                qa_codes, qa_plane = qa_mx[b]
+                ka_codes, ka_plane = ka_mx[h, b]
+                nc.tensor.matmul_mx(
+                    out=bank[:],
+                    lhsT=qa_codes[:, rows].bitcast(FP8X4),
+                    lhsT_scale=qa_plane[:, rows],
+                    rhs=ka_codes[:, columns].bitcast(FP8X4),
+                    rhs_scale=ka_plane[:, columns],
+                    start=(b == 0),
+                    stop=(b == PASSES - 1),
+                )
+            result = result_tile(engine, [P, width])
             if engine == SCALAR:
                 nc.scalar.activation(out=result[:], in_=bank[:], func=COPY, scale=SCORE_SCALE)
             else:
                 nc.vector.tensor_scalar(out=result[:], in0=bank[:], scalar1=SCORE_SCALE, scalar2=None, op0=MULT)
-            nc.sync.dma_start(
-                out=out_0.rearrange("(i p) j -> p i j", p=P)[
-                    :, tiles[0] : tiles[-1] + 1, h * HALF + first : h * HALF + first + width
-                ],
-                in_=result[:],
-            )
+            nc.sync.dma_start(out=out_0[rows, h * HALF + first : h * HALF + first + width], in_=result[:])
+
+        def reorder_wq(b):
+            codes = in_turn("wq_codes", [P, R], I32)
+            reorder(codes[:], wq_raw[b][:].rearrange("p a w -> p (a w)"), 8)
+            return codes
 
         first_half, second_half = range(PACK), range(PACK, 2 * PACK)
         open_groups = [(c, b) for b in (1, 0) for c in first_half]
-        reorder_wk(0, 0)
+        reorder_wk_group0(0)
         gather_words(0, 1)
         pass0_sums = held("pass0_sums", [P, HALF * PACK], F32)
         for c in second_half:
@@ -366,37 +347,37 @@ def tile_list_kvt_qf_act_kernel(
             open_banks[c, b] = new_bank([P, PACK, CHUNK])
             key_pass(open_banks[c, b], 0, c, b, True, False)
         gather_words(1, 0)
-        reorder_wk(1, 0)
+        reorder_wk_group0(1)
         gather_words(1, 1)
-
-        def close_keys(c, b, engine):
+        for place, (c, b) in enumerate(open_groups):
             key_pass(open_banks[c, b], 1, c, b, False, True)
-            keys_out(open_banks[c, b], c, b, engine)
+            keys_out(open_banks[c, b], c, b, VECTOR if place == VECTOR_BANK else SCALAR)
 
-        def rounded(name, raw, pattern_in, pattern_out, shape):
-            values_bf = in_turn(name, shape, BF16)
-            nc.vector.tensor_copy(out=values_bf[:].rearrange(pattern_out, u=4), in_=raw[:].rearrange(pattern_in, u=4))
-            return values_bf
+        wv8_bf = in_turn("wv8_bf", [P, N, PACK], BF16)
+        nc.vector.tensor_copy(
+            out=wv8_bf[:].rearrange("p (c u) i -> p c i u", u=NEIGHBOURS),
+            in_=wv8_raw[:].rearrange("p i (c u) -> p c i u", u=NEIGHBOURS),
+        )
+        wv8_mx = quantise("wv8", wv8_bf[:].rearrange("p n i -> p (n i)"), N)
+        quantise_keys(0, 1, 0, HALF)
+        x_bf = in_turn("x_bf", [P, PASSES, M, PACK], BF16)
+        nc.vector.tensor_copy(
+            out=x_bf[:].rearrange("p a (c u) i -> p a c i u", u=NEIGHBOURS),
+            in_=x_raw[:].rearrange("p a i (c u) -> p a c i u", u=NEIGHBOURS),
+        )
+        wq_plane = in_turn("wq_plane", [P, R // 4], I32)
+        reorder(wq_plane[:], wq_scale_rows[:], 2)
+        x_mx = quantise("x", x_bf[:].rearrange("p a m i -> p (a m i)"), PASSES * M)
+        wq_codes = [reorder_wq(0)]
+        quantise_keys(0, 0, 0, HALF)
+        wq_codes.append(reorder_wq(1))
 
-        def round_wv8():
-            return rounded("wv8_bf", wv8_raw, "p i (c u) -> p c i u", "p (c u) i -> p c i u", [P, N, PACK])
-
-        def round_x():
-            return rounded(
-                "x_bf", x_raw, "p a i (c u) -> p a c i u", "p a (c u) i -> p a c i u", [P, PASSES, M, PACK]
-            )
-
-        def reorder_wq_plane():
-            plane = in_turn("wq_plane", [P, R // 4], I32)
-            reorder(plane[:], wq_scale_rows[:], 2)
-            return plane
-
-        def reorder_wq(b):
-            codes = in_turn("wq_codes", [P, R], I32)
-            reorder(codes[:], wq_raw[b][:].rearrange("p a w -> p (a w)"), 8)
-            return codes
-
-        def finish_parked(c, kr_bf):
+        kr_bf = in_turn("kr_bf", [P, HALF * PACK], BF16)
+        keys(second_half[0], 1)
+        for h in range(J // HALF):
+            for tile in range(N // P):
+                values(h, tile, wv8_mx)
+        for c in second_half:
             bank = new_bank([P, PACK, CHUNK])
             key_pass(bank, 1, c, 0, True, True)
             nc.vector.tensor_tensor(
@@ -405,42 +386,20 @@ def tile_list_kvt_qf_act_kernel(
                 in1=pass0_sums[:, chunk_columns(c)].rearrange("p (n t) -> p n t", t=PACK),
                 op=ADD,
             )
-
-        def relu_parked(kr_bf):
-            ka_bf[1, 0] = in_turn("ka_bf", [P, HALF * PACK], BF16)
-            nc.vector.tensor_scalar_max(out=ka_bf[1, 0][:], in0=kr_bf[:], scalar1=0.0)
-
-        for place, (c, b) in enumerate(open_groups):
-            close_keys(c, b, VECTOR if place in (3,) else SCALAR)
-        wv8_bf = round_wv8()
-        wv8_mx = quantise("wv8", wv8_bf[:].rearrange("p n i -> p (n i)"), N)
-        x_bf = round_x()
-        wq_plane = reorder_wq_plane()
-        x_mx = quantise("x", x_bf[:].rearrange("p a m i -> p (a m i)"), PASSES * M)
-        wq_codes0 = reorder_wq(0)
-        wq_codes1 = reorder_wq(1)
-        kr_bf = in_turn("kr_bf", [P, HALF * PACK], BF16)
-        keys(4, 1)
-        for h in range(J // HALF):
-            for tile in range(N // P):
-                values(h, tile, wv8_mx, SCALAR)
-        for c in second_half:
-            finish_parked(c, kr_bf)
-        queries(0, wq_codes0, wq_plane, x_mx)
-        queries(1, wq_codes1, wq_plane, x_mx)
-        for c in (5, 6, 7):
+        for b in range(PASSES):
+            queries(b, wq_codes[b], wq_plane, x_mx)
+        for c in second_half[1:]:
             keys(c, 1)
-        quantise_keys(0, 1, 0, HALF)
-        quantise_keys(0, 0, 0, HALF)
         qa_mx = [quantise("qa0", qa_bf[0][:], M)]
+        ka_bf[1, 0] = in_turn("ka_bf", [P, HALF * PACK], BF16)
+        nc.vector.tensor_scalar_max(out=ka_bf[1, 0][:], in0=kr_bf[:], scalar1=0.0)
         qa_mx.append(quantise("qa1", qa_bf[1][:], M))
-        relu_parked(kr_bf)
         quantise_keys(1, 1, 0, 2 * CHUNK)
         quantise_keys(1, 0, 0, HALF)
         quantise_keys(1, 1, 2 * CHUNK, CHUNK)
         quantise_keys(1, 1, 3 * CHUNK, CHUNK)
-        scores(0, (0,), 0, HALF, qa_mx, SCALAR)
-        scores(0, (1,), 0, HALF, qa_mx, VECTOR)
-        scores(1, (0,), 0, HALF, qa_mx, SCALAR)
-        scores(1, (1,), 0, HALF // 2, qa_mx, VECTOR)
-        scores(1, (1,), HALF // 2, HALF // 2, qa_mx, SCALAR)
+        scores(0, 0, 0, HALF, qa_mx, SCALAR)
+        scores(0, 1, 0, HALF, qa_mx, VECTOR)
+        scores(1, 0, 0, HALF, qa_mx, SCALAR)
+        scores(1, 1, 0, HALF // 2, qa_mx, VECTOR)
+        scores(1, 1, HALF // 2, HALF // 2, qa_mx, SCALAR)

@@ -323,8 +323,11 @@ def tile_list_kvt_qf_act_kernel(
             nc.sync.dma_start(out=out_0[rows, h * HALF + first : h * HALF + first + width], in_=result[:])
 
         def reorder_wq(b):
-            codes = in_turn("wq_codes", [P, R], I32)
-            reorder(codes[:], wq_raw[b][:].rearrange("p a w -> p (a w)"), 8)
+            if b == 0:
+                codes = in_turn("wq_codes", [P, R], I32)
+            else:
+                codes = keep.tile([P, R], I32, name="wq_codes1", tag="x_bf", align_bytes=64)
+            reorder(codes[:], wq_raw[b][:].rearrange("p a w -> p (a w)"), 8, nc.gpsimd if b else nc.vector)
             return codes
 
         first_half, second_half = range(PACK), range(PACK, 2 * PACK)
@@ -360,7 +363,7 @@ def tile_list_kvt_qf_act_kernel(
         )
         wv8_mx = quantise("wv8", wv8_bf[:].rearrange("p n i -> p (n i)"), N)
         quantise_keys(0, 1, 0, HALF)
-        x_bf = in_turn("x_bf", [P, PASSES, M, PACK], BF16)
+        x_bf = held("x_bf", [P, PASSES, M, PACK], BF16)
         nc.vector.tensor_copy(
             out=x_bf[:].rearrange("p a (c u) i -> p a c i u", u=NEIGHBOURS),
             in_=x_raw[:].rearrange("p a i (c u) -> p a c i u", u=NEIGHBOURS),
@@ -369,7 +372,6 @@ def tile_list_kvt_qf_act_kernel(
         reorder(wq_plane[:], wq_scale_rows[:], 2)
         x_mx = quantise("x", x_bf[:].rearrange("p a m i -> p (a m i)"), PASSES * M)
         wq_codes = [reorder_wq(0)]
-        quantise_keys(0, 0, 0, HALF)
         wq_codes.append(reorder_wq(1))
 
         kr_bf = in_turn("kr_bf", [P, HALF * PACK], BF16)
@@ -390,6 +392,7 @@ def tile_list_kvt_qf_act_kernel(
             queries(b, wq_codes[b], wq_plane, x_mx)
         for c in second_half[1:]:
             keys(c, 1)
+        quantise_keys(0, 0, 0, HALF)
         qa_mx = [quantise("qa0", qa_bf[0][:], M)]
         ka_bf[1, 0] = in_turn("ka_bf", [P, HALF * PACK], BF16)
         nc.vector.tensor_scalar_max(out=ka_bf[1, 0][:], in0=kr_bf[:], scalar1=0.0)

@@ -44,7 +44,6 @@ SCALAR, VECTOR = "scalar", "vector"
 VECTOR_TILES = 24
 SCALAR_RESULTS = 7
 PSUM_BANKS = 8
-WARM_UPS = 5
 EARLY_COLUMNS = T // 2
 VECTOR_BANK = 1
 NEIGHBOURS = 4
@@ -134,17 +133,6 @@ def tile_list_kvt_qf_act_kernel(
         gather_scales(0)
         move_to_planes(0, slice(first_cols.stop, plane_width[0]))
         load_table(1, slice(EARLY_COLUMNS, T))
-        unread = new_bank([P, HALF])
-        for warm in range(WARM_UPS):
-            nc.tensor.matmul_mx(
-                out=unread[:],
-                lhsT=planes[1][:, 0:P].bitcast(FP8X4),
-                lhsT_scale=v_scale_rows[:, 0:P],
-                rhs=planes[1][:, 0:HALF].bitcast(FP8X4),
-                rhs_scale=v_scale_rows[:],
-                start=True,
-                stop=True,
-            )
         nc.sync.dma_start(out=wk_group0[1][:], in_=wk_dram[0][:, 1, :])
         move_to_planes(1, slice(0, plane_width[1]))
 

@@ -41,8 +41,8 @@ SCALE_ROWS = PASSES * BLOCKS
 FIRST_ROW = P - SCALE_ROWS
 SCORE_SCALE = 0.03125
 SCALAR, VECTOR = "scalar", "vector"
-VECTOR_TILES = 24
-SCALAR_RESULTS = 7
+VECTOR_TILES = 26
+SCALAR_RESULTS = 4
 PSUM_BANKS = 8
 EARLY_COLUMNS = T // 2
 VECTOR_BANK = 1
@@ -287,28 +287,31 @@ def tile_list_kvt_qf_act_kernel(
             nc.scalar.activation(out=result[:], in_=bank[:], func=COPY)
             nc.sync.dma_start(out=out_1[rows, h * HALF : (h + 1) * HALF], in_=result[:])
 
-        def scores(h, tile, first, width, qa_mx, engine):
-            columns = slice(first, first + width)
+        def scores(h, tile, qa_mx, engines):
             rows = slice(tile * P, (tile + 1) * P)
-            bank = new_bank([P, width])
-            for b in range(PASSES):
-                qa_codes, qa_plane = qa_mx[b]
-                ka_codes, ka_plane = ka_mx[h, b]
-                nc.tensor.matmul_mx(
-                    out=bank[:],
-                    lhsT=qa_codes[:, rows].bitcast(FP8X4),
-                    lhsT_scale=qa_plane[:, rows],
-                    rhs=ka_codes[:, columns].bitcast(FP8X4),
-                    rhs_scale=ka_plane[:, columns],
-                    start=(b == 0),
-                    stop=(b == PASSES - 1),
-                )
-            result = result_tile(engine, [P, width])
-            if engine == SCALAR:
-                nc.scalar.activation(out=result[:], in_=bank[:], func=COPY, scale=SCORE_SCALE)
-            else:
-                nc.vector.tensor_scalar(out=result[:], in0=bank[:], scalar1=SCORE_SCALE, scalar2=None, op0=MULT)
-            nc.sync.dma_start(out=out_0[rows, h * HALF + first : h * HALF + first + width], in_=result[:])
+            result = result_tile(engines[0], [P, HALF])
+            for part, engine in enumerate(engines):
+                columns = slice(part * HALF // 2, (part + 1) * HALF // 2)
+                bank = new_bank([P, HALF // 2])
+                for b in range(PASSES):
+                    qa_codes, qa_plane = qa_mx[b]
+                    ka_codes, ka_plane = ka_mx[h, b]
+                    nc.tensor.matmul_mx(
+                        out=bank[:],
+                        lhsT=qa_codes[:, rows].bitcast(FP8X4),
+                        lhsT_scale=qa_plane[:, rows],
+                        rhs=ka_codes[:, columns].bitcast(FP8X4),
+                        rhs_scale=ka_plane[:, columns],
+                        start=(b == 0),
+                        stop=(b == PASSES - 1),
+                    )
+                if engine == SCALAR:
+                    nc.scalar.activation(out=result[:, columns], in_=bank[:], func=COPY, scale=SCORE_SCALE)
+                else:
+                    nc.vector.tensor_scalar(
+                        out=result[:, columns], in0=bank[:], scalar1=SCORE_SCALE, scalar2=None, op0=MULT
+                    )
+            nc.sync.dma_start(out=out_0[rows, h * HALF : (h + 1) * HALF], in_=result[:])
 
         def reorder_wq(b):
             if b == 0:
@@ -385,12 +388,10 @@ def tile_list_kvt_qf_act_kernel(
         ka_bf[1, 0] = in_turn("ka_bf", [P, HALF * PACK], BF16)
         nc.vector.tensor_scalar_max(out=ka_bf[1, 0][:], in0=kr_bf[:], scalar1=0.0)
         qa_mx.append(quantise("qa1", qa_bf[1][:], M))
-        quantise_keys(1, 1, 0, 2 * CHUNK)
         quantise_keys(1, 0, 0, HALF)
-        quantise_keys(1, 1, 2 * CHUNK, CHUNK)
-        quantise_keys(1, 1, 3 * CHUNK, CHUNK)
-        scores(0, 0, 0, HALF, qa_mx, SCALAR)
-        scores(0, 1, 0, HALF, qa_mx, VECTOR)
-        scores(1, 0, 0, HALF, qa_mx, SCALAR)
-        scores(1, 1, 0, HALF // 2, qa_mx, VECTOR)
-        scores(1, 1, HALF // 2, HALF // 2, qa_mx, SCALAR)
+        quantise_keys(1, 1, 0, 2 * CHUNK)
+        scores(0, 0, qa_mx, (VECTOR, SCALAR))
+        quantise_keys(1, 1, 2 * CHUNK, 2 * CHUNK)
+        scores(0, 1, qa_mx, (VECTOR, SCALAR))
+        for tile in range(2):
+            scores(1, tile, qa_mx, (VECTOR, SCALAR))

@@ -46,6 +46,7 @@ SCALAR_RESULTS = 4
 PSUM_BANKS = 8
 EARLY_COLUMNS = T // 2
 VECTOR_BANK = 1
+WARM_UPS = 5
 NEIGHBOURS = 4
 
 
@@ -89,7 +90,6 @@ def tile_list_kvt_qf_act_kernel(
         v_scale_rows = held("v_scale_rows", [P, HALF], U8)
         staged_rows = held("staged_rows", [P, wv4_cols.stop], I32)
         planes = [held("planes%d" % a, [P, plane_width[a]], I32) for a in range(PASSES)]
-        wq_scale_rows = held("wq_scale_rows", [P, R // 4], I32)
         wk_group0 = [held("wk_group0_%d" % a, [P, PASS // 2], I32) for a in range(PASSES)]
         wk_group1 = held("wk_group1", [P, PASSES, PASS // 2], I32)
         wk_dram = wk_words.rearrange("a p (b n) -> b p a n", b=PASSES).bitcast(I32)
@@ -117,7 +117,6 @@ def tile_list_kvt_qf_act_kernel(
         nc.vector.memset(tab_scale_rows[0:FIRST_ROW, :], 0)
         for a in range(PASSES):
             nc.gpsimd.memset(planes[a][:], 0)
-        nc.gpsimd.memset(wq_scale_rows[:], 0)
 
         nc.sync.dma_start(offsets[:], offs)
         nc.sync.dma_start(out=tab_scale_rows[staged, :], in_=tab_scales.rearrange("a q t -> (a q) t").bitcast(I32))
@@ -131,6 +130,20 @@ def tile_list_kvt_qf_act_kernel(
         move_to_planes(0, first_cols)
         load_table(1, slice(0, EARLY_COLUMNS))
         gather_scales(0)
+        wq_scale_rows = keep.tile([P, R // 4], I32, name="wq_scale_rows", tag="v_scale_rows", align_bytes=64)
+        nc.gpsimd.memset(wq_scale_rows[:], 0)
+        unread = new_bank([P, HALF])
+        zeros = wq_scale_rows[:].bitcast(U8)
+        for warm_up in range(WARM_UPS):
+            nc.tensor.matmul_mx(
+                out=unread[:],
+                lhsT=planes[1][:, 0:P].bitcast(FP8X4),
+                lhsT_scale=zeros[:, 0:P],
+                rhs=planes[1][:, 0:HALF].bitcast(FP8X4),
+                rhs_scale=zeros[:, 0:HALF],
+                start=True,
+                stop=True,
+            )
         move_to_planes(0, slice(first_cols.stop, plane_width[0]))
         load_table(1, slice(EARLY_COLUMNS, T))
         nc.sync.dma_start(out=wk_group0[1][:], in_=wk_dram[0][:, 1, :])
@@ -142,7 +155,9 @@ def tile_list_kvt_qf_act_kernel(
         wv4_codes = held("wv4_codes", [P, N // 2], I32)
 
         nc.sync.dma_start(out=wv8_raw[:], in_=wv8.rearrange("(p i) n -> p i n", i=PACK))
-        nc.sync.dma_start(out=x_raw[:], in_=x.rearrange("(a p i) m -> p a i m", a=PASSES, i=PACK))
+        for a in range(PASSES):
+            rows_of_pass = x[a * PASS : (a + 1) * PASS]
+            nc.sync.dma_start(out=x_raw[:, a], in_=rows_of_pass.rearrange("(p i) m -> p i m", i=PACK))
         nc.sync.dma_start(out=wv4_codes[:], in_=wv4_words[0].bitcast(I32))
         for quad in QUADRANTS:
             nc.sync.dma_start(
@@ -205,6 +220,26 @@ def tile_list_kvt_qf_act_kernel(
                     stop=(closes and t == PACK - 1),
                 )
 
+        def wide_pass(a, q, u):
+            bank = new_bank([P, 2, 2 * CHUNK])
+            for place in range(2):
+                t = 2 * u + place
+                nc.tensor.matmul_mx(
+                    out=bank[:, place, :],
+                    lhsT=wk_codes[a, 0].bitcast(U8)[:, 2 * t * P : 2 * (t + 1) * P].bitcast(FP4X4),
+                    lhsT_scale=plane_bytes(a, wk_cols, t * P, P),
+                    rhs=v_codes[a, 1][:, q * 2 * CHUNK : (q + 1) * 2 * CHUNK].bitcast(FP8X4),
+                    rhs_scale=plane_bytes(a, v_cols[1], q * 2 * CHUNK, 2 * CHUNK),
+                    start=(place == 0),
+                    stop=(place == 1),
+                )
+            return bank[:].rearrange("p t n -> p n t")
+
+        def pair_columns(tile, q, u):
+            first = (2 * u + q) * HALF
+            return tile[:, first : first + HALF].rearrange("p (n t) -> p n t", t=2)
+
+        wide_banks = [(q, u) for q in range(2) for u in range(2)]
         ka_bf = {}
 
         def chunk_columns(c):
@@ -326,14 +361,8 @@ def tile_list_kvt_qf_act_kernel(
         reorder_wk_group0(0)
         gather_words(0, 1)
         pass0_sums = held("pass0_sums", [P, HALF * PACK], F32)
-        for c in second_half:
-            bank = new_bank([P, PACK, CHUNK])
-            key_pass(bank, 0, c, 0, True, True)
-            nc.scalar.activation(
-                out=pass0_sums[:, chunk_columns(c)].rearrange("p (n t) -> p n t", t=PACK),
-                in_=bank[:].rearrange("p t n -> p n t"),
-                func=COPY,
-            )
+        for q, u in wide_banks:
+            nc.scalar.activation(out=pair_columns(pass0_sums, q, u), in_=wide_pass(0, q, u), func=COPY)
         gather_words(0, 0)
         reorder_wk_group1()
         open_banks = {}
@@ -355,10 +384,11 @@ def tile_list_kvt_qf_act_kernel(
         wv8_mx = quantise("wv8", wv8_bf[:].rearrange("p n i -> p (n i)"), N)
         quantise_keys(0, 1, 0, HALF)
         x_bf = held("x_bf", [P, PASSES, M, PACK], BF16)
-        nc.vector.tensor_copy(
-            out=x_bf[:].rearrange("p a (c u) i -> p a c i u", u=NEIGHBOURS),
-            in_=x_raw[:].rearrange("p a i (c u) -> p a c i u", u=NEIGHBOURS),
-        )
+        for a in range(PASSES):
+            nc.vector.tensor_copy(
+                out=x_bf[:, a].rearrange("p (c u) i -> p c i u", u=NEIGHBOURS),
+                in_=x_raw[:, a].rearrange("p i (c u) -> p c i u", u=NEIGHBOURS),
+            )
         wq_plane = in_turn("wq_plane", [P, R // 4], I32)
         reorder(wq_plane[:], wq_scale_rows[:], 2)
         x_mx = quantise("x", x_bf[:].rearrange("p a m i -> p (a m i)"), PASSES * M)
@@ -370,14 +400,9 @@ def tile_list_kvt_qf_act_kernel(
         for h in range(J // HALF):
             for tile in range(N // P):
                 values(h, tile, wv8_mx)
-        for c in second_half:
-            bank = new_bank([P, PACK, CHUNK])
-            key_pass(bank, 1, c, 0, True, True)
+        for q, u in wide_banks:
             nc.vector.tensor_tensor(
-                out=kr_bf[:, chunk_columns(c)].rearrange("p (n t) -> p n t", t=PACK),
-                in0=bank[:].rearrange("p t n -> p n t"),
-                in1=pass0_sums[:, chunk_columns(c)].rearrange("p (n t) -> p n t", t=PACK),
-                op=ADD,
+                out=pair_columns(kr_bf, q, u), in0=wide_pass(1, q, u), in1=pair_columns(pass0_sums, q, u), op=ADD
             )
         for b in range(PASSES):
             queries(b, wq_codes[b], wq_plane, x_mx)
@@ -386,7 +411,11 @@ def tile_list_kvt_qf_act_kernel(
         quantise_keys(0, 0, 0, HALF)
         qa_mx = [quantise("qa0", qa_bf[0][:], M)]
         ka_bf[1, 0] = in_turn("ka_bf", [P, HALF * PACK], BF16)
-        nc.vector.tensor_scalar_max(out=ka_bf[1, 0][:], in0=kr_bf[:], scalar1=0.0)
+        nc.vector.tensor_scalar_max(
+            out=ka_bf[1, 0][:].rearrange("p (n u t) -> p n u t", u=2, t=2),
+            in0=kr_bf[:].rearrange("p (u n t) -> p n u t", u=2, t=2),
+            scalar1=0.0,
+        )
         qa_mx.append(quantise("qa1", qa_bf[1][:], M))
         quantise_keys(1, 0, 0, HALF)
         quantise_keys(1, 1, 0, 2 * CHUNK)

@@ -179,8 +179,11 @@ def tile_list_kvt_qf_act_kernel(
         wk_codes = {}
 
         def reorder_wk_group0(a):
-            codes = in_turn("wk_codes", [P, PASS // 2], I32)
-            reorder(codes[:], wk_group0[a][:], 4)
+            if a == 0:
+                codes = in_turn("wk_codes", [P, PASS // 2], I32)
+            else:
+                codes = held("wk_codes_late", [P, PASS // 2], I32)
+            reorder(codes[:], wk_group0[a][:], 4, nc.gpsimd if a else nc.vector)
             wk_codes[a, 0] = codes[:]
 
         def reorder_wk_group1():

@@ -41,11 +41,11 @@ SCALE_ROWS = PASSES * BLOCKS
 FIRST_ROW = P - SCALE_ROWS
 SCORE_SCALE = 0.03125
 SCALAR, VECTOR = "scalar", "vector"
-VECTOR_TILES = 26
+VECTOR_TILES = 28
 SCALAR_RESULTS = 4
 PSUM_BANKS = 8
 EARLY_COLUMNS = T // 2
-VECTOR_BANK = 1
+FIFTH_BEHIND = 3
 WARM_UPS = 5
 NEIGHBOURS = 4
 
@@ -82,7 +82,7 @@ def tile_list_kvt_qf_act_kernel(
         v_cols = [slice(wk_cols.stop, wk_cols.stop + HALF // 4), slice(0, HALF // 4)]
         wv4_cols = slice(v_cols[0].stop, v_cols[0].stop + N // 4)
         plane_width = (v_cols[0].stop, wv4_cols.stop)
-        first_cols = slice(0, wk_cols.start + PASS // 4)
+        first_cols = slice(0, wk_cols.stop)
 
         offsets = keep.tile([P, J // LIST_GROUP], U16, name="offsets")
         tab_scale_rows = held("tab_scale_rows", [P, T // 4], I32)
@@ -366,8 +366,16 @@ def tile_list_kvt_qf_act_kernel(
         pass0_sums = held("pass0_sums", [P, HALF * PACK], F32)
         for q, u in wide_banks:
             nc.scalar.activation(out=pair_columns(pass0_sums, q, u), in_=wide_pass(0, q, u), func=COPY)
-        gather_words(0, 0)
         reorder_wk_group1()
+        gather_words(0, 0)
+
+        def fifth_pass(a):
+            bank = new_bank([P, PACK, CHUNK])
+            key_pass(bank, a, second_half[0], 1, True, True)
+            return bank[:].rearrange("p t n -> p n t")
+
+        fifth_sums = held("fifth_sums", [P, CHUNK, PACK], F32)
+        nc.scalar.activation(out=fifth_sums[:], in_=fifth_pass(0), func=COPY)
         open_banks = {}
         for c, b in open_groups:
             open_banks[c, b] = new_bank([P, PACK, CHUNK])
@@ -377,14 +385,22 @@ def tile_list_kvt_qf_act_kernel(
         gather_words(1, 1)
         for place, (c, b) in enumerate(open_groups):
             key_pass(open_banks[c, b], 1, c, b, False, True)
-            keys_out(open_banks[c, b], c, b, VECTOR if place == VECTOR_BANK else SCALAR)
+            keys_out(open_banks[c, b], c, b, SCALAR)
+            if place == FIFTH_BEHIND:
+                fifth_bank = fifth_pass(1)
 
         wv8_bf = in_turn("wv8_bf", [P, N, PACK], BF16)
         nc.vector.tensor_copy(
             out=wv8_bf[:].rearrange("p (c u) i -> p c i u", u=NEIGHBOURS),
             in_=wv8_raw[:].rearrange("p i (c u) -> p c i u", u=NEIGHBOURS),
         )
+        fifth_bf = in_turn("fifth_bf", [P, CHUNK, PACK], BF16)
+        nc.vector.tensor_tensor(out=fifth_bf[:], in0=fifth_bank, in1=fifth_sums[:], op=ADD)
         wv8_mx = quantise("wv8", wv8_bf[:].rearrange("p n i -> p (n i)"), N)
+        ka_bf[1, 1] = in_turn("ka_bf", [P, HALF * PACK], BF16)
+        nc.vector.tensor_scalar_max(
+            out=ka_bf[1, 1][:, chunk_columns(0)], in0=fifth_bf[:].rearrange("p n t -> p (n t)"), scalar1=0.0
+        )
         quantise_keys(0, 1, 0, HALF)
         x_bf = held("x_bf", [P, PASSES, M, PACK], BF16)
         for a in range(PASSES):
@@ -399,7 +415,7 @@ def tile_list_kvt_qf_act_kernel(
         wq_codes.append(reorder_wq(1))
 
         kr_bf = in_turn("kr_bf", [P, HALF * PACK], BF16)
-        keys(second_half[0], 1)
+        keys(second_half[1], 1)
         for h in range(J // HALF):
             for tile in range(N // P):
                 values(h, tile, wv8_mx)
@@ -409,7 +425,7 @@ def tile_list_kvt_qf_act_kernel(
             )
         for b in range(PASSES):
             queries(b, wq_codes[b], wq_plane, x_mx)
-        for c in second_half[1:]:
+        for c in second_half[2:]:
             keys(c, 1)
         quantise_keys(0, 0, 0, HALF)
         qa_mx = [quantise("qa0", qa_bf[0][:], M)]

from contextlib import ExitStack

import concourse.mybir as mybir

K, R, M, N, T, J = 1024, 1024, 256, 256, 4096, 1024
FLOPS = 2 * (K * R * M + K * R * J + R * M * J + K * N * J)
BYTES = (
    (K * J + K * J // 32)
    + 4 * K * M
    + (K * R + K * R // 32)
    + (K * R // 2 + K * R // 32)
    + 4 * (K // 2) * N
    + ((K // 2) * N // 2 + (K // 2) * N // 32)
    + 2 * J
    + 4 * (M + N) * J
)

F32 = mybir.dt.float32
BF16 = mybir.dt.bfloat16
I32 = mybir.dt.int32
U32 = mybir.dt.uint32
U16 = mybir.dt.uint16
U8 = mybir.dt.uint8
FP8X4 = mybir.dt.float8_e4m3fn_x4
FP4X4 = mybir.dt.float4_e2m1fn_x4
RELU = mybir.ActivationFunctionType.Relu
COPY = mybir.ActivationFunctionType.Copy
MULT = mybir.AluOpType.mult
ADD = mybir.AluOpType.add

P = 128
PACK = 4
PASS = P * PACK
PASSES = K // PASS
BLOCKS = PASS // 32
HALF = J // 2
CHUNK = HALF // PACK
LIST_GROUP = 16
QUADRANTS = (0, 2, 1, 3)
SCALE_ROWS = PASSES * BLOCKS
FIRST_ROW = P - SCALE_ROWS
SCORE_SCALE = 0.03125
SCALAR, VECTOR = "scalar", "vector"
VECTOR_TILES = 28
SCALAR_RESULTS = 4
PSUM_BANKS = 8
EARLY_COLUMNS = T // 2
FIFTH_BEHIND = 3
WARM_UPS = 5
NEIGHBOURS = 4


def tile_list_kvt_qf_act_kernel(
    tc, tab_words, tab_scales, x, wq_words, wq_scales, wk_words, wk_scales, wv8, wv4_words, wv4_scales, offs, out_0, out_1
):
    nc = tc.nc
    with ExitStack() as ctx:
        keep = ctx.enter_context(tc.tile_pool(name="keep", bufs=1))
        stage = ctx.enter_context(tc.tile_pool(name="stage", bufs=SCALAR_RESULTS))
        ring = ctx.enter_context(tc.tile_pool(name="ring", bufs=VECTOR_TILES))
        psum = ctx.enter_context(tc.psum_pool(name="psum", bufs=PSUM_BANKS))

        def held(name, shape, dtype):
            return keep.tile(shape, dtype, name=name, tag=name, align_bytes=64)

        def in_turn(name, shape, dtype):
            return ring.tile(shape, dtype, name=name, tag="in_turn", align_bytes=64)

        def new_bank(shape):
            return psum.tile(shape, F32, name="bank", tag="bank")

        def quadrant_rows(quad, first=0, count=4):
            return slice(32 * quad + first, 32 * quad + first + count)

        def reorder(dst, src, run, engine=nc.vector):
            engine.tensor_copy(
                out=dst.rearrange("p (g t q u) -> p g t q u", t=PACK, q=BLOCKS, u=run),
                in_=src.rearrange("p (g q t u) -> p g t q u", t=PACK, q=BLOCKS, u=run),
            )

        wk_cols = slice(HALF // 4, HALF // 4 + R // 4)
        v_cols = [slice(wk_cols.stop, wk_cols.stop + HALF // 4), slice(0, HALF // 4)]
        wv4_cols = slice(v_cols[0].stop, v_cols[0].stop + N // 4)
        plane_width = (v_cols[0].stop, wv4_cols.stop)
        first_cols = slice(0, wk_cols.stop)

        offsets = keep.tile([P, J // LIST_GROUP], U16, name="offsets")
        tab_scale_rows = held("tab_scale_rows", [P, T // 4], I32)
        wk_scale_rows = held("wk_scale_rows", [P, R // 4], I32)
        v_scale_rows = held("v_scale_rows", [P, HALF], U8)
        staged_rows = held("staged_rows", [P, wv4_cols.stop], I32)
        planes = [held("planes%d" % a, [P, plane_width[a]], I32) for a in range(PASSES)]
        wk_group0 = [held("wk_group0_%d" % a, [P, PASS // 2], I32) for a in range(PASSES)]
        wk_group1 = held("wk_group1", [P, PASSES, PASS // 2], I32)
        wk_dram = wk_words.rearrange("a p (b n) -> b p a n", b=PASSES).bitcast(I32)
        staged = slice(FIRST_ROW, P)
        tab_win = [held("tab_win%d" % a, [P, T], I32) for a in range(PASSES)]

        def load_table(a, cols):
            nc.sync.dma_start(
                out=tab_win[a][:, cols], in_=tab_words[a].rearrange("p t i -> p (t i)").bitcast(I32)[:, cols]
            )

        def half_of_list(h):
            columns = HALF // LIST_GROUP
            return offsets[:, columns * h : columns * (h + 1)]

        def gather_scales(h):
            nc.vector.tensor_copy(out=v_scale_rows[:], in_=tab_scale_rows[:].bitcast(U8).indirect(half_of_list(h)))
            nc.vector.tensor_copy(out=staged_rows[staged, v_cols[h]], in_=v_scale_rows[staged, :].bitcast(I32))

        def move_to_planes(a, cols):
            for quad in QUADRANTS:
                row = FIRST_ROW + BLOCKS * a + 4 * quad
                nc.sync.dma_start(out=planes[a][quadrant_rows(quad), cols], in_=staged_rows[row : row + 4, cols])

        nc.vector.memset(tab_scale_rows[0:FIRST_ROW, :], 0)
        for a in range(PASSES):
            nc.gpsimd.memset(planes[a][:], 0)

        nc.sync.dma_start(offsets[:], offs)
        nc.sync.dma_start(out=tab_scale_rows[staged, :], in_=tab_scales.rearrange("a q t -> (a q) t").bitcast(I32))
        nc.sync.dma_start(out=wk_scale_rows[staged, :], in_=wk_scales.rearrange("a q r -> (a q) r").bitcast(I32))
        nc.sync.dma_start(out=wk_group0[0][:], in_=wk_dram[0][:, 0, :])
        load_table(0, slice(0, T))
        nc.sync.dma_start(out=wk_group1[:], in_=wk_dram[1])
        nc.sync.dma_start(out=staged_rows[FIRST_ROW + BLOCKS : P, wv4_cols], in_=wv4_scales[0].bitcast(I32))
        reorder(staged_rows[staged, wk_cols], wk_scale_rows[staged, :], 2, nc.gpsimd)
        gather_scales(1)
        move_to_planes(0, first_cols)
        load_table(1, slice(0, EARLY_COLUMNS))
        gather_scales(0)
        wq_scale_rows = keep.tile([P, R // 4], I32, name="wq_scale_rows", tag="v_scale_rows", align_bytes=64)
        nc.gpsimd.memset(wq_scale_rows[:], 0)
        unread = new_bank([P, HALF])
        zeros = wq_scale_rows[:].bitcast(U8)
        for warm_up in range(WARM_UPS):
            nc.tensor.matmul_mx(
                out=unread[:],
                lhsT=planes[1][:, 0:P].bitcast(FP8X4),
                lhsT_scale=zeros[:, 0:P],
                rhs=planes[1][:, 0:HALF].bitcast(FP8X4),
                rhs_scale=zeros[:, 0:HALF],
                start=True,
                stop=True,
            )
        move_to_planes(0, slice(first_cols.stop, plane_width[0]))
        load_table(1, slice(EARLY_COLUMNS, T))
        nc.sync.dma_start(out=wk_group0[1][:], in_=wk_dram[0][:, 1, :])
        move_to_planes(1, slice(0, plane_width[1]))

        x_raw = held("x_raw", [P, PASSES, PACK, M], F32)
        wq_raw = [held("wq_raw%d" % b, [P, PASSES, PASS], I32) for b in range(PASSES)]
        wv8_raw = held("wv8_raw", [P, PACK, N], F32)
        wv4_codes = held("wv4_codes", [P, N // 2], I32)

        nc.sync.dma_start(out=wv8_raw[:], in_=wv8.rearrange("(p i) n -> p i n", i=PACK))
        for a in range(PASSES):
            rows_of_pass = x[a * PASS : (a + 1) * PASS]
            nc.sync.dma_start(out=x_raw[:, a], in_=rows_of_pass.rearrange("(p i) m -> p i m", i=PACK))
        nc.sync.dma_start(out=wv4_codes[:], in_=wv4_words[0].bitcast(I32))
        for quad in QUADRANTS:
            nc.sync.dma_start(
                out=wq_scale_rows[quadrant_rows(quad, count=8), :],
                in_=wq_scales[:, 4 * quad : 4 * quad + 4, :].bitcast(I32),
            )
        for b in range(PASSES):
            nc.sync.dma_start(
                out=wq_raw[b][:],
                in_=wq_words[:, :, b * PASS : (b + 1) * PASS, :].rearrange("a p r i -> p a (r i)").bitcast(I32),
            )

        v_codes = {}

        def gather_words(a, h):
            v_codes[a, h] = in_turn("v_codes", [P, HALF], U32)
            nc.vector.tensor_copy(out=v_codes[a, h][:], in_=tab_win[a][:].bitcast(U32).indirect(half_of_list(h)))

        wk_codes = {}

        def reorder_wk_group0(a):
            if a == 0:
                codes = in_turn("wk_codes", [P, PASS // 2], I32)
            else:
                codes = held("wk_codes_late", [P, PASS // 2], I32)
            reorder(codes[:], wk_group0[a][:], 4, nc.gpsimd if a else nc.vector)
            wk_codes[a, 0] = codes[:]

        def reorder_wk_group1():
            codes = in_turn("wk_codes", [P, PASSES, PASS // 2], I32)
            reorder(codes[:].rearrange("p a w -> p (a w)"), wk_group1[:].rearrange("p a w -> p (a w)"), 4)
            for a in range(PASSES):
                wk_codes[a, 1] = codes[:, a, :]

        def plane_bytes(a, cols, first, width):
            return planes[a][:].bitcast(U8)[:, 4 * cols.start + first : 4 * cols.start + first + width]

        def relu_out(engine, out, bank):
            out = out.rearrange("p (n t) -> p n t", t=PACK)
            in_ = bank[:].rearrange("p t n -> p n t")
            if engine == SCALAR:
                nc.scalar.activation(out=out, in_=in_, func=RELU)
            else:
                nc.vector.tensor_scalar_max(out=out, in0=in_, scalar1=0.0)

        def quantise(name, values, width):
            codes = in_turn(name + "_codes", [P, width], U32)
            plane = held(name + "_plane", [P, width], U8)
            nc.vector.quantize_mx(out=codes[:].bitcast(FP8X4), scales=plane[:], in_=values)
            return codes, plane

        def key_pass(bank, a, c, b, opens, closes):
            h, first = divmod(c * CHUNK, HALF)
            for t in range(PACK):
                col = b * PASS + t * P
                nc.tensor.matmul_mx(
                    out=bank[:, t, :],
                    lhsT=wk_codes[a, b].bitcast(U8)[:, 2 * t * P : 2 * (t + 1) * P].bitcast(FP4X4),
                    lhsT_scale=plane_bytes(a, wk_cols, col, P),
                    rhs=v_codes[a, h][:, first : first + CHUNK].bitcast(FP8X4),
                    rhs_scale=plane_bytes(a, v_cols[h], first, CHUNK),
                    start=(opens and t == 0),
                    stop=(closes and t == PACK - 1),
                )

        def wide_pass(a, q, u):
            bank = new_bank([P, 2, 2 * CHUNK])
            for place in range(2):
                t = 2 * u + place
                nc.tensor.matmul_mx(
                    out=bank[:, place, :],
                    lhsT=wk_codes[a, 0].bitcast(U8)[:, 2 * t * P : 2 * (t + 1) * P].bitcast(FP4X4),
                    lhsT_scale=plane_bytes(a, wk_cols, t * P, P),
                    rhs=v_codes[a, 1][:, q * 2 * CHUNK : (q + 1) * 2 * CHUNK].bitcast(FP8X4),
                    rhs_scale=plane_bytes(a, v_cols[1], q * 2 * CHUNK, 2 * CHUNK),
                    start=(place == 0),
                    stop=(place == 1),
                )
            return bank[:].rearrange("p t n -> p n t")

        def pair_columns(tile, q, u):
            first = (2 * u + q) * HALF
            return tile[:, first : first + HALF].rearrange("p (n t) -> p n t", t=2)

        wide_banks = [(q, u) for q in range(2) for u in range(2)]
        ka_bf = {}

        def chunk_columns(c):
            return slice(PACK * CHUNK * (c % PACK), PACK * CHUNK * (c % PACK + 1))

        def keys_out(bank, c, b, engine):
            if (c // PACK, b) not in ka_bf:
                ka_bf[c // PACK, b] = held("ka_bf%d%d" % (c // PACK, b), [P, HALF * PACK], BF16)
            relu_out(engine, ka_bf[c // PACK, b][:, chunk_columns(c)], bank)

        def keys(c, b):
            bank = new_bank([P, PACK, CHUNK])
            key_pass(bank, 0, c, b, True, False)
            key_pass(bank, 1, c, b, False, True)
            keys_out(bank, c, b, SCALAR)

        ka_mx = {}

        def quantise_keys(h, b, first, width):
            if (h, b) not in ka_mx:
                ka_mx[h, b] = (in_turn("ka_codes", [P, HALF], U32), held("ka_plane%d%d" % (h, b), [P, HALF], U8))
            codes, plane = ka_mx[h, b]
            nc.vector.quantize_mx(
                out=codes[:, first : first + width].bitcast(FP8X4),
                scales=plane[:, first : first + width],
                in_=ka_bf[h, b][:, PACK * first : PACK * (first + width)],
            )

        qa_bf = [held("qa_bf%d" % b, [P, M * PACK], BF16) for b in range(PASSES)]

        def queries(b, wq_codes, wq_plane, x_mx):
            x_codes, x_plane = x_mx
            wq_plane_bytes = wq_plane[:].bitcast(U8)
            for c in range(M // CHUNK):
                bank = new_bank([P, PACK, CHUNK])
                for t in range(PACK):
                    for a in range(PASSES):
                        word = a * PASS + t * P
                        col = b * PASS + t * P
                        m0 = a * M + c * CHUNK
                        nc.tensor.matmul_mx(
                            out=bank[:, t, :],
                            lhsT=wq_codes[:, word : word + P].bitcast(FP8X4),
                            lhsT_scale=wq_plane_bytes[4 * a : P, col : col + P],
                            rhs=x_codes[:, m0 : m0 + CHUNK].bitcast(FP8X4),
                            rhs_scale=x_plane[:, m0 : m0 + CHUNK],
                            start=(a == 0),
                            stop=(a == PASSES - 1),
                        )
                relu_out(SCALAR, qa_bf[b][:, PACK * c * CHUNK : PACK * (c + 1) * CHUNK], bank)

        def result_tile(engine, shape):
            if engine == VECTOR:
                return in_turn("result", shape, F32)
            return stage.tile(shape, F32, name="result", tag="result")

        def values(h, tile, wv8_mx):
            wv8_codes, wv8_plane = wv8_mx
            rows = slice(tile * P, (tile + 1) * P)
            bank = new_bank([P, HALF])
            nc.tensor.matmul_mx(
                out=bank[:],
                lhsT=wv8_codes[:, rows].bitcast(FP8X4),
                lhsT_scale=wv8_plane[:, rows],
                rhs=v_codes[0, h][:].bitcast(FP8X4),
                rhs_scale=plane_bytes(0, v_cols[h], 0, HALF),
                start=True,
                stop=False,
            )
            nc.tensor.matmul_mx(
                out=bank[:],
                lhsT=wv4_codes[:].bitcast(U8)[:, 2 * tile * P : 2 * (tile + 1) * P].bitcast(FP4X4),
                lhsT_scale=plane_bytes(1, wv4_cols, tile * P, P),
                rhs=v_codes[1, h][:].bitcast(FP8X4),
                rhs_scale=plane_bytes(1, v_cols[h], 0, HALF),
                start=False,
                stop=True,
            )
            result = result_tile(SCALAR, [P, HALF])
            nc.scalar.activation(out=result[:], in_=bank[:], func=COPY)
            nc.sync.dma_start(out=out_1[rows, h * HALF : (h + 1) * HALF], in_=result[:])

        def scores(h, tile, qa_mx, engines):
            rows = slice(tile * P, (tile + 1) * P)
            result = result_tile(engines[0], [P, HALF])
            for part, engine in enumerate(engines):
                columns = slice(part * HALF // 2, (part + 1) * HALF // 2)
                bank = new_bank([P, HALF // 2])
                for b in range(PASSES):
                    qa_codes, qa_plane = qa_mx[b]
                    ka_codes, ka_plane = ka_mx[h, b]
                    nc.tensor.matmul_mx(
                        out=bank[:],
                        lhsT=qa_codes[:, rows].bitcast(FP8X4),
                        lhsT_scale=qa_plane[:, rows],
                        rhs=ka_codes[:, columns].bitcast(FP8X4),
                        rhs_scale=ka_plane[:, columns],
                        start=(b == 0),
                        stop=(b == PASSES - 1),
                    )
                if engine == SCALAR:
                    nc.scalar.activation(out=result[:, columns], in_=bank[:], func=COPY, scale=SCORE_SCALE)
                else:
                    nc.vector.tensor_scalar(
                        out=result[:, columns], in0=bank[:], scalar1=SCORE_SCALE, scalar2=None, op0=MULT
                    )
            nc.sync.dma_start(out=out_0[rows, h * HALF : (h + 1) * HALF], in_=result[:])

        def reorder_wq(b):
            if b == 0:
                codes = in_turn("wq_codes", [P, R], I32)
            else:
                codes = keep.tile([P, R], I32, name="wq_codes1", tag="x_bf", align_bytes=64)
            reorder(codes[:], wq_raw[b][:].rearrange("p a w -> p (a w)"), 8, nc.gpsimd if b else nc.vector)
            return codes

        first_half, second_half = range(PACK), range(PACK, 2 * PACK)
        open_groups = [(c, b) for b in (1, 0) for c in first_half]
        reorder_wk_group0(0)
        gather_words(0, 1)
        pass0_sums = held("pass0_sums", [P, HALF * PACK], F32)
        for q, u in wide_banks:
            nc.scalar.activation(out=pair_columns(pass0_sums, q, u), in_=wide_pass(0, q, u), func=COPY)
        reorder_wk_group1()
        gather_words(0, 0)

        def fifth_pass(a):
            bank = new_bank([P, PACK, CHUNK])
            key_pass(bank, a, second_half[0], 1, True, True)
            return bank[:].rearrange("p t n -> p n t")

        fifth_sums = held("fifth_sums", [P, CHUNK, PACK], F32)
        nc.scalar.activation(out=fifth_sums[:], in_=fifth_pass(0), func=COPY)
        open_banks = {}
        for c, b in open_groups:
            open_banks[c, b] = new_bank([P, PACK, CHUNK])
            key_pass(open_banks[c, b], 0, c, b, True, False)
        gather_words(1, 0)
        reorder_wk_group0(1)
        gather_words(1, 1)
        for place, (c, b) in enumerate(open_groups):
            key_pass(open_banks[c, b], 1, c, b, False, True)
            keys_out(open_banks[c, b], c, b, SCALAR)
            if place == FIFTH_BEHIND:
                fifth_bank = fifth_pass(1)

        wv8_bf = in_turn("wv8_bf", [P, N, PACK], BF16)
        nc.vector.tensor_copy(
            out=wv8_bf[:].rearrange("p (c u) i -> p c i u", u=NEIGHBOURS),
            in_=wv8_raw[:].rearrange("p i (c u) -> p c i u", u=NEIGHBOURS),
        )
        fifth_bf = in_turn("fifth_bf", [P, CHUNK, PACK], BF16)
        nc.vector.tensor_tensor(out=fifth_bf[:], in0=fifth_bank, in1=fifth_sums[:], op=ADD)
        wv8_mx = quantise("wv8", wv8_bf[:].rearrange("p n i -> p (n i)"), N)
        ka_bf[1, 1] = in_turn("ka_bf", [P, HALF * PACK], BF16)
        nc.vector.tensor_scalar_max(
            out=ka_bf[1, 1][:, chunk_columns(0)], in0=fifth_bf[:].rearrange("p n t -> p (n t)"), scalar1=0.0
        )
        quantise_keys(0, 1, 0, HALF)
        x_bf = held("x_bf", [P, PASSES, M, PACK], BF16)
        for a in range(PASSES):
            nc.vector.tensor_copy(
                out=x_bf[:, a].rearrange("p (c u) i -> p c i u", u=NEIGHBOURS),
                in_=x_raw[:, a].rearrange("p i (c u) -> p c i u", u=NEIGHBOURS),
            )
        wq_plane = in_turn("wq_plane", [P, R // 4], I32)
        reorder(wq_plane[:], wq_scale_rows[:], 2)
        x_mx = quantise("x", x_bf[:].rearrange("p a m i -> p (a m i)"), PASSES * M)
        wq_codes = [reorder_wq(0)]
        wq_codes.append(reorder_wq(1))

        kr_bf = in_turn("kr_bf", [P, HALF * PACK], BF16)
        keys(second_half[1], 1)
        for h in range(J // HALF):
            for tile in range(N // P):
                values(h, tile, wv8_mx)
        for q, u in wide_banks:
            nc.vector.tensor_tensor(
                out=pair_columns(kr_bf, q, u), in0=wide_pass(1, q, u), in1=pair_columns(pass0_sums, q, u), op=ADD
            )
        for b in range(PASSES):
            queries(b, wq_codes[b], wq_plane, x_mx)
        for c in second_half[2:]:
            keys(c, 1)
        quantise_keys(0, 0, 0, HALF)
        qa_mx = [quantise("qa0", qa_bf[0][:], M)]
        ka_bf[1, 0] = in_turn("ka_bf", [P, HALF * PACK], BF16)
        nc.vector.tensor_scalar_max(
            out=ka_bf[1, 0][:].rearrange("p (n u t) -> p n u t", u=2, t=2),
            in0=kr_bf[:].rearrange("p (u n t) -> p n u t", u=2, t=2),
            scalar1=0.0,
        )
        qa_mx.append(quantise("qa1", qa_bf[1][:], M))
        quantise_keys(1, 0, 0, HALF)
        quantise_keys(1, 1, 0, 2 * CHUNK)
        scores(0, 0, qa_mx, (VECTOR, SCALAR))
        quantise_keys(1, 1, 2 * CHUNK, 2 * CHUNK)
        scores(0, 1, qa_mx, (VECTOR, SCALAR))
        for tile in range(2):
            scores(1, tile, qa_mx, (VECTOR, SCALAR))
